import numpy as np
import ml_dtypes


def mxq(x, axis, fmt="e4m3"):
    dtype, down = {"e4m3": (ml_dtypes.float8_e4m3fn, 7), "e5m2": (ml_dtypes.float8_e5m2, 14)}[fmt]
    v = np.moveaxis(np.asarray(x, np.float32).astype(ml_dtypes.bfloat16).astype(np.float64), axis, -1)
    blocks = v.reshape(v.shape[:-1] + (-1, 32))
    amax = np.abs(blocks).max(-1, keepdims=True)
    byte = np.maximum(np.where(amax > 0, np.frexp(amax)[1] - 1 + 127, 0) - down, 1)
    scale = np.exp2(byte - 127.0)
    codes = (blocks / scale).astype(np.float32).astype(dtype).astype(np.float64)
    return np.moveaxis((codes * scale).reshape(v.shape), -1, axis)


WIDE = False


def mx_kscale(k):
    if not WIDE:
        return np.ones(k)
    levels = np.array([10, -10, 5, -5, 0])
    if k % 512:
        return np.exp2(np.random.permutation(np.resize(levels, k // 32))).repeat(32)
    a = np.empty((k // 512, 16))
    for p in range(k // 512):
        a[p, :8] = np.random.permutation(np.resize(levels, 8))
        for g in range(8):
            far = levels[np.abs(levels - a[p, g]) >= 10]
            a[p, g + 8] = far[np.random.randint(len(far))]
    return np.exp2(a.ravel()).repeat(32)


def f64(x):
    return np.asarray(x).astype(np.float64)


def striped(idx):
    return np.tile(idx.reshape(-1, 16).T, (8, 1)).astype(np.uint16)


def unstriped(offs):
    return offs[:16].T.reshape(-1).astype(np.int64)


E2M1 = np.array([0.0, 0.5, 1.0, 1.5, 2.0, 3.0, 4.0, 6.0, -0.0, -0.5, -1.0, -1.5, -2.0, -3.0, -4.0, -6.0])


def pack_weight(w, fmt):
    k, n = w.shape
    w = f64(np.asarray(w, np.float32).astype(ml_dtypes.bfloat16)).reshape(k // 32, 32, n)
    amax = np.abs(w).max(1)
    if fmt == "e4m3":
        byte = np.frexp(amax)[1] - 1 + 127 - 7
    else:
        mant, ex = np.frexp(amax / 6.0)
        byte = np.where(mant > 0.5, ex, ex - 1) + 127
    byte = np.clip(np.where(amax > 0, byte, 1), 1, 254)
    scaled = (w * np.exp2(127.0 - byte)[:, None, :]).reshape(k, n).astype(np.float32)
    by_word = np.ascontiguousarray(scaled.reshape(k // 512, 128, 4, n).transpose(0, 1, 3, 2))
    if fmt == "e4m3":
        words = by_word.astype(ml_dtypes.float8_e4m3fn).view(np.uint8)
    else:
        c = by_word.astype(ml_dtypes.float4_e2m1fn).view(np.uint8) & 0xF
        words = (c[..., 0::2] | (c[..., 1::2] << 4)).reshape(k // 512, 128, 2 * n)
    return np.ascontiguousarray(words), np.ascontiguousarray(byte.astype(np.uint8).reshape(k // 512, 16, n))


def unpack_weight(words, scales, fmt):
    g, _, n = scales.shape
    words = np.ascontiguousarray(words).reshape(g, 128, n, -1)
    if fmt == "e4m3":
        vals = words.view(ml_dtypes.float8_e4m3fn).astype(np.float64)
    else:
        nib = np.empty((g, 128, n, 4), np.uint8)
        nib[..., 0::2] = words & 0xF
        nib[..., 1::2] = words >> 4
        vals = E2M1[nib]
    vals = vals * np.repeat(np.exp2(scales.astype(np.float64) - 127.0), 8, axis=1)[..., None]
    return vals.transpose(0, 1, 3, 2).reshape(g * 512, n)


def gelu(v):
    return 0.5 * v * (1.0 + np.tanh(np.sqrt(2.0 / np.pi) * (v + 0.044715 * v**3)))


def striped8(idx):
    return np.concatenate([v.reshape(-1, 16).T for v in idx]).astype(np.uint16)


def unstriped8(offs):
    return np.stack([offs[16 * g:16 * g + 16].T.reshape(-1) for g in range(8)]).astype(np.int64)


def put_heads(h, wgs, idx8, t2):
    r = np.arange(h.shape[0])
    page = np.zeros((h.shape[0], t2))
    page[r[:, None], idx8[r % 512 // 64]] = wgs[r // 4 % 128] * h
    return page


K, T, S, H, T2, N = 512, 2048, 1024, 1024, 2048, 512


def setup_inputs():
    n = np.random.standard_normal
    s = mx_kscale(K)[:, None]
    u = mx_kscale(H)[:, None]
    tab_words, tab_scales = pack_weight(n((K, T)) * s, "e4m3")
    wp = (n((K, H)) / np.sqrt(K) / s).astype(np.float32)
    wq_words, wq_scales = pack_weight(n((K, H)) / np.sqrt(K) / s, "e2m1")
    wm_words, wm_scales = pack_weight(n((H, N)) / np.sqrt(H) / u, "e4m3")
    offs = striped(np.random.permutation(T)[:S])
    offs2 = striped8(np.stack([np.random.permutation(T2)[:S] for _ in range(8)]))
    wgs = np.repeat(np.random.uniform(0.5, 2.0, (8, S)), 16, axis=0).astype(np.float32)
    rating = (np.exp(0.3 * n((H, T2))) / u).astype(np.float32)
    return {"tab_words": tab_words, "tab_scales": tab_scales, "wp": wp,
            "wq_words": wq_words, "wq_scales": wq_scales,
            "wm_words": wm_words, "wm_scales": wm_scales,
            "offs": offs, "offs2": offs2, "wgs": wgs, "rating": rating}


def reference(tab_words, tab_scales, wp, wq_words, wq_scales, wm_words, wm_scales,
              offs, offs2, wgs, rating):
    v = unpack_weight(tab_words, tab_scales, "e4m3")[:, unstriped(offs)]
    wq = unpack_weight(wq_words, wq_scales, "e2m1")
    wm = unpack_weight(wm_words, wm_scales, "e4m3")
    act = mxq(f64(wp), 0, "e4m3").T @ v
    rea = wq.T @ v
    h = np.sqrt(0.125 + np.square(act) + np.square(rea))
    page = put_heads(h, f64(wgs), unstriped8(offs2), T2)
    z = page / f64(rating)
    return wm.T @ mxq(z, 0, "e4m3")

@@ -1,0 +1,202 @@
+from contextlib import ExitStack
+
+import concourse.mybir as mybir
+from concourse.masks import make_identity
+
+K, T, S, H, T2, N = 512, 2048, 1024, 1024, 2048, 512
+FLOPS = 2 * (2 * K * H * S + H * N * T2)
+
+F32 = mybir.dt.float32
+BF16 = mybir.dt.bfloat16
+I32 = mybir.dt.int32
+U32 = mybir.dt.uint32
+U16 = mybir.dt.uint16
+U8 = mybir.dt.uint8
+FP8X4 = mybir.dt.float8_e4m3fn_x4
+FP4X4 = mybir.dt.float4_e2m1fn_x4
+ACT = mybir.ActivationFunctionType
+MULT = mybir.AluOpType.mult
+
+P = 128
+PACK = 4
+PASS = P * PACK
+BANK = 512
+LIST_COL = 16
+
+
+def tile_list_apparent_power_margins_kernel(
+    tc, tab_words, tab_scales, wp, wq_words, wq_scales, wm_words, wm_scales, offs, offs2, wgs, rating, out
+):
+    nc = tc.nc
+    with ExitStack() as ctx:
+        keep = ctx.enter_context(tc.tile_pool(name="keep", bufs=1))
+        ring = ctx.enter_context(tc.tile_pool(name="ring", bufs=1))
+        psum = ctx.enter_context(tc.psum_pool(name="psum", bufs=8))
+
+        def load_scales(queue, dst, src_rows):
+            for q in range(4):
+                queue.dma_start(out=dst[32 * q : 32 * q + 4, :].bitcast(I32), in_=src_rows[4 * q : 4 * q + 4, :].bitcast(I32))
+
+        def interleave(copy, dst, src):
+            copy(out=dst.rearrange("p (c i) t -> p c t i", i=4), in_=src.rearrange("p t (c i) -> p c t i", i=4))
+
+        def slot(tag, shape, dtype):
+            return ring.tile(shape, dtype, name=tag, tag=tag, bufs=1, align_bytes=64)
+
+        offs_t = keep.tile([P, S // LIST_COL], U16, name="offs_t")
+        offs2_t = keep.tile([P, S // LIST_COL], U16, name="offs2_t")
+        tab_w = slot("inv1", [P, T], I32)
+        tab_s = slot("inv2", [P, T], U8)
+        wq_w = slot("weight_words", [P, 2 * H], U8)
+        wq_s = slot("weight_scales", [P, H], U8)
+        v_w = keep.tile([P, S], U32, name="v_w", align_bytes=64)
+        v_s = keep.tile([P, S], U8, name="v_s", align_bytes=64)
+        wp_w = [slot(tag, [P, PASS], U32) for tag in ("inv3", "wp_w1")]
+        wp_s = [slot(tag, [P, PASS], U8) for tag in ("inv4", "wp_s1")]
+        z_w = [keep.tile([P, T2], U32, name=f"z_w{b}", align_bytes=64) for b in range(2)]
+        z_s = [keep.tile([P, T2], U8, name=f"z_s{b}", align_bytes=64) for b in range(2)]
+        ident = keep.tile([P, P], F32, name="ident")
+        under_root = ring.tile([P, 1], F32, name="under_root", tag="root", bufs=1, align_bytes=64)
+        squared_const = slot("wgs", [P, 1], F32)
+        pages = [slot(f"page{n}", [P, T2], F32) for n in range(3)]
+
+        nc.gpsimd.memset(tab_s[:].bitcast(I32), 0)
+        nc.gpsimd.memset(wq_s[:].bitcast(I32), 0)
+        load_scales(nc.gpsimd, wq_s, wq_scales[0])
+        load_scales(nc.scalar, tab_s, tab_scales[0])
+        nc.vector.memset(squared_const[:], 1.0 / 64.0)
+        nc.scalar.activation(out=under_root[:], in_=squared_const[:], func=ACT.Sqrt)
+        make_identity(nc, ident[:])
+
+        def load_wp(b):
+            raw = slot("inv0", [P, PACK, PASS], F32)
+            nc.sync.dma_start(out=raw[:], in_=wp[:, b * PASS : (b + 1) * PASS].rearrange("(p t) c -> p t c", t=PACK))
+            return raw
+
+        def quantise_wp(b, raw, copy):
+            grouped = slot(f"page{3 + b}", [P, PASS, PACK], BF16)
+            interleave(copy, grouped[:], raw[:])
+            nc.vector.quantize_mx(out=wp_w[b][:].bitcast(FP8X4), scales=wp_s[b][:], in_=grouped[:].rearrange("p c t -> p (c t)"))
+            page = slot(f"page{3 + b}", [P, T2], F32)
+            nc.gpsimd.memset(page[:], 0.0)
+            return page
+
+        nc.sync.dma_start(offs_t[:], offs)
+        nc.sync.dma_start(out=tab_w[:], in_=tab_words[0].rearrange("p n t -> p (n t)").bitcast(I32))
+        raw0 = load_wp(0)
+        nc.sync.dma_start(out=wq_w[:].bitcast(I32), in_=wq_words[0].bitcast(I32))
+        nc.sync.dma_start(offs2_t[:], offs2)
+        wgs_t = slot("wgs", [P, S], F32)
+        nc.sync.dma_start(out=wgs_t[:], in_=wgs)
+
+        def gather(j0, j1):
+            cols = offs_t[:, j0 // LIST_COL : j1 // LIST_COL]
+            nc.vector.tensor_copy(out=v_w[:, j0:j1], in_=tab_w[:].bitcast(U32).indirect(cols))
+            nc.vector.tensor_copy(out=v_s[:, j0:j1], in_=tab_s[:].indirect(cols))
+
+        def apparent_power(b, h, j0):
+            js = slice(j0, j0 + P)
+            rs = slice(b * PASS, (b + 1) * PASS)
+            act = psum.tile([P, BANK], F32, name="bank", tag="bank")
+            nc.tensor.matmul_mx(out=act[:], lhsT=v_w[:, js].bitcast(FP8X4), lhsT_scale=v_s[:, js],
+                                rhs=wp_w[b][:].bitcast(FP8X4), rhs_scale=wp_s[b][:], start=True, stop=True)
+            rea = psum.tile([P, BANK], F32, name="bank", tag="bank")
+            nc.tensor.matmul_mx(out=rea[:], lhsT=v_w[:, js].bitcast(FP8X4), lhsT_scale=v_s[:, js],
+                                rhs=wq_w[:, 2 * b * PASS : 2 * (b + 1) * PASS].bitcast(FP4X4), rhs_scale=wq_s[:, rs],
+                                start=True, stop=True)
+            squares = []
+            for bank in (act, rea):
+                sq = ring.tile([P, PACK, P], F32, name="stage", tag="stage", bufs=6)
+                nc.scalar.activation(out=sq[:], in_=bank[:].rearrange("j (p t) -> j t p", t=PACK), func=ACT.Square)
+                squares.append(sq)
+            total = psum.tile([P, PACK, P], F32, name="bank", tag="bank")
+            for t in range(PACK):
+                for n, sq in enumerate(squares):
+                    nc.tensor.matmul(total[:, t, :], sq[:, t, :], ident[:], start=(n == 0), stop=(n == 1), is_transpose=True)
+            nc.scalar.activation(out=h[:, :, js], in_=total[:], func=ACT.Sqrt, bias=under_root[:])
+
+        def scatter(page, h, t, j0, j1):
+            cols = offs2_t[:, j0 // LIST_COL : j1 // LIST_COL]
+            nc.vector.tensor_tensor(page[:].indirect(cols), h[:, t, j0:j1], wgs_t[:, j0:j1], MULT)
+
+        def inverse_rating(b, t):
+            inv = slot(f"inv{(PACK * b + t) % 5}", [P, T2], F32)
+            nc.sync.dma_start(out=inv[:], in_=rating[b * PASS : (b + 1) * PASS, :].rearrange("(p t) m -> p t m", t=PACK)[:, t, :])
+            inv_root = ring.tile([P, T2], F32, name="inv_root", tag="root", bufs=1, align_bytes=64)
+            nc.scalar.activation(out=inv_root[:], in_=inv[:], func=ACT.Abs_reciprocal_sqrt)
+            nc.scalar.activation(out=inv[:], in_=inv_root[:], func=ACT.Square)
+            return inv
+
+        def divide(z, t, page, inv, ms):
+            nc.vector.tensor_tensor(z[:, t, ms], page[:, ms], inv[:, ms], MULT)
+
+        def quantise_z(b, z, ms, copy, grouped):
+            interleave(copy, grouped, z[:, :, ms])
+            nc.vector.quantize_mx(out=z_w[b][:, ms].bitcast(FP8X4), scales=z_s[b][:, ms], in_=grouped.rearrange("p c t -> p (c t)"))
+
+        h0 = ring.tile([P, PACK, S], F32, name="h0", tag="quad", bufs=3)
+        for page in pages:
+            nc.vector.memset(page[:], 0.0)
+        gather(0, 256)
+        pages.append(quantise_wp(0, raw0, nc.scalar.copy))
+        raw1 = load_wp(1)
+        apparent_power(0, h0, 0)
+        gather(256, 512)
+        apparent_power(0, h0, 128)
+        gather(512, 1024)
+        pages.append(quantise_wp(1, raw1, nc.scalar.copy))
+        for j0 in range(256, S, P):
+            apparent_power(0, h0, j0)
+        for j0, j1 in ((0, 128), (128, 256), (256, 512), (512, 1024)):
+            for t in range(PACK):
+                scatter(pages[t], h0, t, j0, j1)
+
+        h1 = ring.tile([P, PACK, S], F32, name="h1", tag="quad", bufs=3)
+        for j0 in range(0, S, P):
+            apparent_power(1, h1, j0)
+
+        invs = [inverse_rating(0, t) for t in range(PACK)]
+        wm_w = slot("weight_words", [P, 2, N], I32)
+        wm_s = slot("weight_scales", [P, N], U8)
+        nc.sync.dma_start(out=wm_w[:], in_=wm_words.rearrange("a p n t -> p a (n t)").bitcast(I32))
+        nc.gpsimd.memset(wm_s[:].bitcast(I32), 0)
+        for q in range(4):
+            nc.sync.dma_start(out=wm_s[32 * q : 32 * q + 8, :].bitcast(I32), in_=wm_scales[:, 4 * q : 4 * q + 4, :].bitcast(I32))
+
+        everything = slice(0, T2)
+        chunks = [slice(m0, m0 + BANK) for m0 in range(0, T2, BANK)]
+        z0 = ring.tile([P, PACK, T2], BF16, name="z0", tag="quad", bufs=3)
+        z1 = ring.tile([P, PACK, T2], BF16, name="z1", tag="quad", bufs=3)
+        scatter(pages[4], h1, 0, 0, S)
+        inv4 = inverse_rating(1, 0)
+        divide(z0, 0, pages[0], invs[0], everything)
+        inv5 = inverse_rating(1, 1)
+        scatter(pages[0], h1, 1, 0, S)
+        divide(z0, 1, pages[1], invs[1], everything)
+        inv6 = inverse_rating(1, 2)
+        divide(z0, 2, pages[2], invs[2], everything)
+        inv7 = inverse_rating(1, 3)
+        scatter(pages[2], h1, 2, 0, S)
+        divide(z0, 3, pages[3], invs[3], everything)
+        divide(z1, 0, pages[4], inv4, everything)
+        divide(z1, 1, pages[0], inv5, everything)
+        divide(z1, 2, pages[2], inv6, everything)
+        scatter(pages[2], h1, 3, 0, S)
+        grouped0 = ring.tile([P, T2, PACK], BF16, name="grouped0", tag="root", bufs=1, align_bytes=64)
+        for ms in chunks:
+            quantise_z(0, z0, ms, nc.scalar.copy, grouped0[:, ms, :])
+        for c, ms in enumerate(chunks):
+            divide(z1, 3, pages[2], inv7, ms)
+            grouped1 = ring.tile([P, BANK, PACK], BF16, name="grouped1", tag="grouped1", bufs=2, align_bytes=64)
+            quantise_z(1, z1, ms, nc.scalar.copy if c == 1 else nc.vector.tensor_copy, grouped1[:])
+            for n0 in range(0, N, P):
+                ns = slice(n0, n0 + P)
+                acc = psum.tile([P, BANK], F32, name="bank", tag="bank")
+                for b in range(2):
+                    nc.tensor.matmul_mx(out=acc[:], lhsT=wm_w[:, b, ns].bitcast(FP8X4), lhsT_scale=wm_s[4 * b : P, ns],
+                                        rhs=z_w[b][:, ms].bitcast(FP8X4), rhs_scale=z_s[b][:, ms],
+                                        start=(b == 0), stop=(b == 1))
+                res = ring.tile([P, BANK], F32, name="stage", tag="stage", bufs=6)
+                copy = nc.vector.tensor_copy if c == len(chunks) - 1 and n0 % (2 * P) else nc.scalar.copy
+                copy(out=res[:], in_=acc[:])
+                nc.sync.dma_start(out=out[ns, ms], in_=res[:])

@@ -31,7 +31,7 @@ def tile_list_apparent_power_margins_kernel(
     with ExitStack() as ctx:
         keep = ctx.enter_context(tc.tile_pool(name="keep", bufs=1))
         ring = ctx.enter_context(tc.tile_pool(name="ring", bufs=1))
-        psum = ctx.enter_context(tc.psum_pool(name="psum", bufs=8))
+        psum = ctx.enter_context(tc.psum_pool(name="psum", bufs=2))
 
         def load_scales(queue, dst, src_rows):
             for q in range(4):
@@ -45,20 +45,19 @@ def tile_list_apparent_power_margins_kernel(
 
         offs_t = keep.tile([P, S // LIST_COL], U16, name="offs_t")
         offs2_t = keep.tile([P, S // LIST_COL], U16, name="offs2_t")
-        tab_w = slot("inv1", [P, T], I32)
-        tab_s = slot("inv2", [P, T], U8)
+        tab_s = slot("wgs", [P, T], U8)
         wq_w = slot("weight_words", [P, 2 * H], U8)
         wq_s = slot("weight_scales", [P, H], U8)
-        v_w = keep.tile([P, S], U32, name="v_w", align_bytes=64)
-        v_s = keep.tile([P, S], U8, name="v_s", align_bytes=64)
-        wp_w = [slot(tag, [P, PASS], U32) for tag in ("inv3", "wp_w1")]
-        wp_s = [slot(tag, [P, PASS], U8) for tag in ("inv4", "wp_s1")]
+        v_w = slot("inv7", [P, S], U32)
+        v_s = slot("inv2", [P, S], U8)
+        wp_w = [slot(tag, [P, PASS], U32) for tag in ("inv3", "inv5")]
+        wp_s = [slot(tag, [P, PASS], U8) for tag in ("inv4", "inv6")]
         z_w = [keep.tile([P, T2], U32, name=f"z_w{b}", align_bytes=64) for b in range(2)]
         z_s = [keep.tile([P, T2], U8, name=f"z_s{b}", align_bytes=64) for b in range(2)]
         ident = keep.tile([P, P], F32, name="ident")
         under_root = ring.tile([P, 1], F32, name="under_root", tag="root", bufs=1, align_bytes=64)
-        squared_const = slot("wgs", [P, 1], F32)
-        pages = [slot(f"page{n}", [P, T2], F32) for n in range(3)]
+        squared_const = slot("inv1", [P, 1], F32)
+        pages = [slot(f"page{n}", [P, T2], F32) for n in range(2)]
 
         nc.gpsimd.memset(tab_s[:].bitcast(I32), 0)
         nc.gpsimd.memset(wq_s[:].bitcast(I32), 0)
@@ -69,25 +68,28 @@ def tile_list_apparent_power_margins_kernel(
         make_identity(nc, ident[:])
 
         def load_wp(b):
-            raw = slot("inv0", [P, PACK, PASS], F32)
+            raw = slot(f"inv{b}", [P, PACK, PASS], F32)
             nc.sync.dma_start(out=raw[:], in_=wp[:, b * PASS : (b + 1) * PASS].rearrange("(p t) c -> p t c", t=PACK))
             return raw
 
-        def quantise_wp(b, raw, copy):
-            grouped = slot(f"page{3 + b}", [P, PASS, PACK], BF16)
-            interleave(copy, grouped[:], raw[:])
-            nc.vector.quantize_mx(out=wp_w[b][:].bitcast(FP8X4), scales=wp_s[b][:], in_=grouped[:].rearrange("p c t -> p (c t)"))
-            page = slot(f"page{3 + b}", [P, T2], F32)
-            nc.gpsimd.memset(page[:], 0.0)
-            return page
+        def quantise_wp(b, raw, copies):
+            share = PASS // len(copies)
+            for n, copy in enumerate(copies):
+                cs = slice(n * share, (n + 1) * share)
+                tag = f"page{len(pages)}"
+                grouped = slot(tag, [P, share, PACK], BF16)
+                interleave(copy, grouped[:], raw[:, :, cs])
+                nc.vector.quantize_mx(out=wp_w[b][:, cs].bitcast(FP8X4), scales=wp_s[b][:, cs], in_=grouped[:].rearrange("p c t -> p (c t)"))
+                page = slot(tag, [P, T2], F32)
+                nc.gpsimd.memset(page[:], 0.0)
+                pages.append(page)
 
         nc.sync.dma_start(offs_t[:], offs)
-        nc.sync.dma_start(out=tab_w[:], in_=tab_words[0].rearrange("p n t -> p (n t)").bitcast(I32))
         raw0 = load_wp(0)
+        tab_w = slot("inv1", [P, T], I32)
+        nc.sync.dma_start(out=tab_w[:], in_=tab_words[0].rearrange("p n t -> p (n t)").bitcast(I32))
         nc.sync.dma_start(out=wq_w[:].bitcast(I32), in_=wq_words[0].bitcast(I32))
         nc.sync.dma_start(offs2_t[:], offs2)
-        wgs_t = slot("wgs", [P, S], F32)
-        nc.sync.dma_start(out=wgs_t[:], in_=wgs)
 
         def gather(j0, j1):
             cols = offs_t[:, j0 // LIST_COL : j1 // LIST_COL]
@@ -97,10 +99,10 @@ def tile_list_apparent_power_margins_kernel(
         def apparent_power(b, h, j0):
             js = slice(j0, j0 + P)
             rs = slice(b * PASS, (b + 1) * PASS)
-            act = psum.tile([P, BANK], F32, name="bank", tag="bank")
+            act = psum.tile([P, BANK], F32, name="bank0", tag="bank0")
             nc.tensor.matmul_mx(out=act[:], lhsT=v_w[:, js].bitcast(FP8X4), lhsT_scale=v_s[:, js],
                                 rhs=wp_w[b][:].bitcast(FP8X4), rhs_scale=wp_s[b][:], start=True, stop=True)
-            rea = psum.tile([P, BANK], F32, name="bank", tag="bank")
+            rea = psum.tile([P, BANK], F32, name="bank1", tag="bank1")
             nc.tensor.matmul_mx(out=rea[:], lhsT=v_w[:, js].bitcast(FP8X4), lhsT_scale=v_s[:, js],
                                 rhs=wq_w[:, 2 * b * PASS : 2 * (b + 1) * PASS].bitcast(FP4X4), rhs_scale=wq_s[:, rs],
                                 start=True, stop=True)
@@ -109,7 +111,7 @@ def tile_list_apparent_power_margins_kernel(
                 sq = ring.tile([P, PACK, P], F32, name="stage", tag="stage", bufs=6)
                 nc.scalar.activation(out=sq[:], in_=bank[:].rearrange("j (p t) -> j t p", t=PACK), func=ACT.Square)
                 squares.append(sq)
-            total = psum.tile([P, PACK, P], F32, name="bank", tag="bank")
+            total = psum.tile([P, PACK, P], F32, name="bank2", tag="bank2")
             for t in range(PACK):
                 for n, sq in enumerate(squares):
                     nc.tensor.matmul(total[:, t, :], sq[:, t, :], ident[:], start=(n == 0), stop=(n == 1), is_transpose=True)
@@ -119,12 +121,15 @@ def tile_list_apparent_power_margins_kernel(
             cols = offs2_t[:, j0 // LIST_COL : j1 // LIST_COL]
             nc.vector.tensor_tensor(page[:].indirect(cols), h[:, t, j0:j1], wgs_t[:, j0:j1], MULT)
 
-        def inverse_rating(b, t):
-            inv = slot(f"inv{(PACK * b + t) % 5}", [P, T2], F32)
+        def inverse_rating(b, t, inv_root=None):
+            inv = slot(f"inv{PACK * b + t}", [P, T2], F32)
             nc.sync.dma_start(out=inv[:], in_=rating[b * PASS : (b + 1) * PASS, :].rearrange("(p t) m -> p t m", t=PACK)[:, t, :])
-            inv_root = ring.tile([P, T2], F32, name="inv_root", tag="root", bufs=1, align_bytes=64)
-            nc.scalar.activation(out=inv_root[:], in_=inv[:], func=ACT.Abs_reciprocal_sqrt)
-            nc.scalar.activation(out=inv[:], in_=inv_root[:], func=ACT.Square)
+            between = inv if inv_root is None else inv_root
+            halves = (slice(0, T2 // 2), slice(T2 // 2, T2))
+            for ms in halves:
+                nc.scalar.activation(out=between[:, ms], in_=inv[:, ms], func=ACT.Abs_reciprocal_sqrt)
+            for ms in halves:
+                nc.scalar.activation(out=inv[:, ms], in_=between[:, ms], func=ACT.Square)
             return inv
 
         def divide(z, t, page, inv, ms):
@@ -137,17 +142,21 @@ def tile_list_apparent_power_margins_kernel(
         h0 = ring.tile([P, PACK, S], F32, name="h0", tag="quad", bufs=3)
         for page in pages:
             nc.vector.memset(page[:], 0.0)
+        quantise_wp(0, raw0, (nc.scalar.copy, nc.scalar.copy))
         gather(0, 256)
-        pages.append(quantise_wp(0, raw0, nc.scalar.copy))
-        raw1 = load_wp(1)
         apparent_power(0, h0, 0)
         gather(256, 512)
         apparent_power(0, h0, 128)
         gather(512, 1024)
-        pages.append(quantise_wp(1, raw1, nc.scalar.copy))
-        for j0 in range(256, S, P):
+        wgs_t = slot("wgs", [P, S], F32)
+        nc.sync.dma_start(out=wgs_t[:], in_=wgs)
+        raw1 = load_wp(1)
+        for j0 in range(256, 640, P):
             apparent_power(0, h0, j0)
-        for j0, j1 in ((0, 128), (128, 256), (256, 512), (512, 1024)):
+        quantise_wp(1, raw1, (nc.scalar.copy,))
+        for j0 in range(640, S, P):
+            apparent_power(0, h0, j0)
+        for j0, j1 in ((0, 128), (128, 256), (256, 384), (384, 640), (640, 1024)):
             for t in range(PACK):
                 scatter(pages[t], h0, t, j0, j1)
 
@@ -155,7 +164,8 @@ def tile_list_apparent_power_margins_kernel(
         for j0 in range(0, S, P):
             apparent_power(1, h1, j0)
 
-        invs = [inverse_rating(0, t) for t in range(PACK)]
+        inv_root = slot("root", [P, T2], F32)
+        invs = [inverse_rating(n // PACK, n % PACK, inv_root) for n in range(7)]
         wm_w = slot("weight_words", [P, 2, N], I32)
         wm_s = slot("weight_scales", [P, N], U8)
         nc.sync.dma_start(out=wm_w[:], in_=wm_words.rearrange("a p n t -> p a (n t)").bitcast(I32))
@@ -167,36 +177,35 @@ def tile_list_apparent_power_margins_kernel(
         chunks = [slice(m0, m0 + BANK) for m0 in range(0, T2, BANK)]
         z0 = ring.tile([P, PACK, T2], BF16, name="z0", tag="quad", bufs=3)
         z1 = ring.tile([P, PACK, T2], BF16, name="z1", tag="quad", bufs=3)
-        scatter(pages[4], h1, 0, 0, S)
-        inv4 = inverse_rating(1, 0)
+        scatter(pages[4], h1, 0, 0, S // 2)
+        scatter(pages[4], h1, 0, S // 2, S)
         divide(z0, 0, pages[0], invs[0], everything)
-        inv5 = inverse_rating(1, 1)
         scatter(pages[0], h1, 1, 0, S)
         divide(z0, 1, pages[1], invs[1], everything)
-        inv6 = inverse_rating(1, 2)
         divide(z0, 2, pages[2], invs[2], everything)
-        inv7 = inverse_rating(1, 3)
         scatter(pages[2], h1, 2, 0, S)
         divide(z0, 3, pages[3], invs[3], everything)
-        divide(z1, 0, pages[4], inv4, everything)
-        divide(z1, 1, pages[0], inv5, everything)
-        divide(z1, 2, pages[2], inv6, everything)
+        divide(z1, 0, pages[4], invs[4], everything)
+        divide(z1, 1, pages[0], invs[5], everything)
+        divide(z1, 2, pages[2], invs[6], everything)
         scatter(pages[2], h1, 3, 0, S)
-        grouped0 = ring.tile([P, T2, PACK], BF16, name="grouped0", tag="root", bufs=1, align_bytes=64)
+        grouped0 = slot("root", [P, T2, PACK], BF16)
         for ms in chunks:
             quantise_z(0, z0, ms, nc.scalar.copy, grouped0[:, ms, :])
+        inv7 = inverse_rating(1, 3)
         for c, ms in enumerate(chunks):
             divide(z1, 3, pages[2], inv7, ms)
-            grouped1 = ring.tile([P, BANK, PACK], BF16, name="grouped1", tag="grouped1", bufs=2, align_bytes=64)
-            quantise_z(1, z1, ms, nc.scalar.copy if c == 1 else nc.vector.tensor_copy, grouped1[:])
+            grouped1 = ring.tile([P, BANK, PACK], BF16, name="grouped1", tag="grouped1", bufs=3, align_bytes=64)
+            quantise_z(1, z1, ms, nc.scalar.copy if c == 0 else nc.vector.tensor_copy, grouped1[:])
+        for c, ms in enumerate(chunks):
+            res = slot(f"inv{c}", [P, N // P, BANK], F32)
             for n0 in range(0, N, P):
                 ns = slice(n0, n0 + P)
-                acc = psum.tile([P, BANK], F32, name="bank", tag="bank")
+                acc = psum.tile([P, BANK], F32, name=f"bank{n0 // P}", tag=f"bank{n0 // P}")
                 for b in range(2):
                     nc.tensor.matmul_mx(out=acc[:], lhsT=wm_w[:, b, ns].bitcast(FP8X4), lhsT_scale=wm_s[4 * b : P, ns],
                                         rhs=z_w[b][:, ms].bitcast(FP8X4), rhs_scale=z_s[b][:, ms],
                                         start=(b == 0), stop=(b == 1))
-                res = ring.tile([P, BANK], F32, name="stage", tag="stage", bufs=6)
-                copy = nc.vector.tensor_copy if c == len(chunks) - 1 and n0 % (2 * P) else nc.scalar.copy
-                copy(out=res[:], in_=acc[:])
-                nc.sync.dma_start(out=out[ns, ms], in_=res[:])
+                copy = nc.vector.tensor_copy if c == len(chunks) - 1 else nc.scalar.copy
+                copy(out=res[:, n0 // P, :], in_=acc[:])
+                nc.sync.dma_start(out=out[ns, ms], in_=res[:, n0 // P, :])

@@ -45,7 +45,7 @@ def tile_list_apparent_power_margins_kernel(
 
         offs_t = keep.tile([P, S // LIST_COL], U16, name="offs_t")
         offs2_t = keep.tile([P, S // LIST_COL], U16, name="offs2_t")
-        tab_s = slot("wgs", [P, T], U8)
+        tab_s = slot("inv0", [P, T], U8)
         wq_w = slot("weight_words", [P, 2 * H], U8)
         wq_s = slot("weight_scales", [P, H], U8)
         v_w = slot("inv7", [P, S], U32)
@@ -57,7 +57,7 @@ def tile_list_apparent_power_margins_kernel(
         ident = keep.tile([P, P], F32, name="ident")
         under_root = ring.tile([P, 1], F32, name="under_root", tag="root", bufs=1, align_bytes=64)
         squared_const = slot("inv1", [P, 1], F32)
-        pages = [slot(f"page{n}", [P, T2], F32) for n in range(2)]
+        pages = [slot(f"page{n}", [P, T2], F32) for n in range(3)]
 
         nc.gpsimd.memset(tab_s[:].bitcast(I32), 0)
         nc.gpsimd.memset(wq_s[:].bitcast(I32), 0)
@@ -68,21 +68,18 @@ def tile_list_apparent_power_margins_kernel(
         make_identity(nc, ident[:])
 
         def load_wp(b):
-            raw = slot(f"inv{b}", [P, PACK, PASS], F32)
+            raw = slot(("wgs", "inv1")[b], [P, PACK, PASS], F32)
             nc.sync.dma_start(out=raw[:], in_=wp[:, b * PASS : (b + 1) * PASS].rearrange("(p t) c -> p t c", t=PACK))
             return raw
 
-        def quantise_wp(b, raw, copies):
-            share = PASS // len(copies)
-            for n, copy in enumerate(copies):
-                cs = slice(n * share, (n + 1) * share)
-                tag = f"page{len(pages)}"
-                grouped = slot(tag, [P, share, PACK], BF16)
-                interleave(copy, grouped[:], raw[:, :, cs])
-                nc.vector.quantize_mx(out=wp_w[b][:, cs].bitcast(FP8X4), scales=wp_s[b][:, cs], in_=grouped[:].rearrange("p c t -> p (c t)"))
-                page = slot(tag, [P, T2], F32)
-                nc.gpsimd.memset(page[:], 0.0)
-                pages.append(page)
+        def quantise_wp(b, raw):
+            tag = f"page{len(pages)}"
+            grouped = slot(tag, [P, PASS, PACK], BF16)
+            interleave(nc.scalar.copy, grouped[:], raw[:])
+            nc.vector.quantize_mx(out=wp_w[b][:].bitcast(FP8X4), scales=wp_s[b][:], in_=grouped[:].rearrange("p c t -> p (c t)"))
+            page = slot(tag, [P, T2], F32)
+            nc.gpsimd.memset(page[:].bitcast(I32), 0)
+            pages.append(page)
 
         nc.sync.dma_start(offs_t[:], offs)
         raw0 = load_wp(0)
@@ -96,7 +93,7 @@ def tile_list_apparent_power_margins_kernel(
             nc.vector.tensor_copy(out=v_w[:, j0:j1], in_=tab_w[:].bitcast(U32).indirect(cols))
             nc.vector.tensor_copy(out=v_s[:, j0:j1], in_=tab_s[:].indirect(cols))
 
-        def apparent_power(b, h, j0):
+        def apparent_power(b, h, j0, parts=1):
             js = slice(j0, j0 + P)
             rs = slice(b * PASS, (b + 1) * PASS)
             act = psum.tile([P, BANK], F32, name="bank0", tag="bank0")
@@ -109,13 +106,15 @@ def tile_list_apparent_power_margins_kernel(
             squares = []
             for bank in (act, rea):
                 sq = ring.tile([P, PACK, P], F32, name="stage", tag="stage", bufs=6)
-                nc.scalar.activation(out=sq[:], in_=bank[:].rearrange("j (p t) -> j t p", t=PACK), func=ACT.Square)
+                nc.scalar.activation(out=sq[:].rearrange("j t p -> j p t"), in_=bank[:].rearrange("j (p t) -> j p t", t=PACK), func=ACT.Square)
                 squares.append(sq)
-            total = psum.tile([P, PACK, P], F32, name="bank2", tag="bank2")
-            for t in range(PACK):
-                for n, sq in enumerate(squares):
-                    nc.tensor.matmul(total[:, t, :], sq[:, t, :], ident[:], start=(n == 0), stop=(n == 1), is_transpose=True)
-            nc.scalar.activation(out=h[:, :, js], in_=total[:], func=ACT.Sqrt, bias=under_root[:])
+            planes = PACK // parts
+            for part in range(parts):
+                total = psum.tile([P, planes, P], F32, name=f"bank{2 + part}", tag=f"bank{2 + part}")
+                for t in range(planes):
+                    for n, sq in enumerate(squares):
+                        nc.tensor.matmul(total[:, t, :], sq[:, part * planes + t, :], ident[:], start=(n == 0), stop=(n == 1), is_transpose=True)
+                nc.scalar.activation(out=h[:, part * planes : (part + 1) * planes, js], in_=total[:], func=ACT.Sqrt, bias=under_root[:])
 
         def scatter(page, h, t, j0, j1):
             cols = offs2_t[:, j0 // LIST_COL : j1 // LIST_COL]
@@ -141,20 +140,18 @@ def tile_list_apparent_power_margins_kernel(
 
         h0 = ring.tile([P, PACK, S], F32, name="h0", tag="quad", bufs=3)
         for page in pages:
-            nc.vector.memset(page[:], 0.0)
-        quantise_wp(0, raw0, (nc.scalar.copy, nc.scalar.copy))
+            nc.vector.memset(page[:].bitcast(I32), 0)
+        quantise_wp(0, raw0)
+        wgs_t = slot("wgs", [P, S], F32)
+        nc.sync.dma_start(out=wgs_t[:], in_=wgs)
         gather(0, 256)
-        apparent_power(0, h0, 0)
+        apparent_power(0, h0, 0, parts=2)
         gather(256, 512)
         apparent_power(0, h0, 128)
         gather(512, 1024)
-        wgs_t = slot("wgs", [P, S], F32)
-        nc.sync.dma_start(out=wgs_t[:], in_=wgs)
         raw1 = load_wp(1)
-        for j0 in range(256, 640, P):
-            apparent_power(0, h0, j0)
-        quantise_wp(1, raw1, (nc.scalar.copy,))
-        for j0 in range(640, S, P):
+        quantise_wp(1, raw1)
+        for j0 in range(256, S, P):
             apparent_power(0, h0, j0)
         for j0, j1 in ((0, 128), (128, 256), (256, 384), (384, 640), (640, 1024)):
             for t in range(PACK):

@@ -22,6 +22,7 @@ PACK = 4
 PASS = P * PACK
 BANK = 512
 LIST_COL = 16
+BANKS = {"act": 3, "rea": 3, "sum": 2}
 
 
 def tile_list_apparent_power_margins_kernel(
@@ -31,7 +32,7 @@ def tile_list_apparent_power_margins_kernel(
     with ExitStack() as ctx:
         keep = ctx.enter_context(tc.tile_pool(name="keep", bufs=1))
         ring = ctx.enter_context(tc.tile_pool(name="ring", bufs=1))
-        psum = ctx.enter_context(tc.psum_pool(name="psum", bufs=2))
+        psum = ctx.enter_context(tc.psum_pool(name="psum", bufs=1))
 
         def load_scales(queue, dst, src_rows):
             for q in range(4):
@@ -42,6 +43,9 @@ def tile_list_apparent_power_margins_kernel(
 
         def slot(tag, shape, dtype):
             return ring.tile(shape, dtype, name=tag, tag=tag, bufs=1, align_bytes=64)
+
+        def bank(tag, shape):
+            return psum.tile(shape, F32, name=tag, tag=tag, bufs=BANKS[tag])
 
         offs_t = keep.tile([P, S // LIST_COL], U16, name="offs_t")
         offs2_t = keep.tile([P, S // LIST_COL], U16, name="offs2_t")
@@ -57,7 +61,8 @@ def tile_list_apparent_power_margins_kernel(
         ident = keep.tile([P, P], F32, name="ident")
         under_root = ring.tile([P, 1], F32, name="under_root", tag="root", bufs=1, align_bytes=64)
         squared_const = slot("inv1", [P, 1], F32)
-        pages = [slot(f"page{n}", [P, T2], F32) for n in range(3)]
+        pages = [keep.tile([P, T2], F32, name=f"page{n}") for n in range(2 * PACK)]
+        chunks = [slice(m0, m0 + BANK) for m0 in range(0, T2, BANK)]
 
         nc.gpsimd.memset(tab_s[:].bitcast(I32), 0)
         nc.gpsimd.memset(wq_s[:].bitcast(I32), 0)
@@ -73,13 +78,9 @@ def tile_list_apparent_power_margins_kernel(
             return raw
 
         def quantise_wp(b, raw):
-            tag = f"page{len(pages)}"
-            grouped = slot(tag, [P, PASS, PACK], BF16)
+            grouped = ring.tile([P, PASS, PACK], BF16, name="grouped", tag="grouped", bufs=3, align_bytes=64)
             interleave(nc.scalar.copy, grouped[:], raw[:])
             nc.vector.quantize_mx(out=wp_w[b][:].bitcast(FP8X4), scales=wp_s[b][:], in_=grouped[:].rearrange("p c t -> p (c t)"))
-            page = slot(tag, [P, T2], F32)
-            nc.gpsimd.memset(page[:].bitcast(I32), 0)
-            pages.append(page)
 
         nc.sync.dma_start(offs_t[:], offs)
         raw0 = load_wp(0)
@@ -93,76 +94,92 @@ def tile_list_apparent_power_margins_kernel(
             nc.vector.tensor_copy(out=v_w[:, j0:j1], in_=tab_w[:].bitcast(U32).indirect(cols))
             nc.vector.tensor_copy(out=v_s[:, j0:j1], in_=tab_s[:].indirect(cols))
 
-        def apparent_power(b, h, j0, parts=1):
+        def squared_powers(u):
+            b, j0 = divmod(u * P, S)
             js = slice(j0, j0 + P)
             rs = slice(b * PASS, (b + 1) * PASS)
-            act = psum.tile([P, BANK], F32, name="bank0", tag="bank0")
+            act = bank("act", [P, BANK])
             nc.tensor.matmul_mx(out=act[:], lhsT=v_w[:, js].bitcast(FP8X4), lhsT_scale=v_s[:, js],
                                 rhs=wp_w[b][:].bitcast(FP8X4), rhs_scale=wp_s[b][:], start=True, stop=True)
-            rea = psum.tile([P, BANK], F32, name="bank1", tag="bank1")
+            rea = bank("rea", [P, BANK])
             nc.tensor.matmul_mx(out=rea[:], lhsT=v_w[:, js].bitcast(FP8X4), lhsT_scale=v_s[:, js],
                                 rhs=wq_w[:, 2 * b * PASS : 2 * (b + 1) * PASS].bitcast(FP4X4), rhs_scale=wq_s[:, rs],
                                 start=True, stop=True)
             squares = []
-            for bank in (act, rea):
-                sq = ring.tile([P, PACK, P], F32, name="stage", tag="stage", bufs=6)
-                nc.scalar.activation(out=sq[:].rearrange("j t p -> j p t"), in_=bank[:].rearrange("j (p t) -> j p t", t=PACK), func=ACT.Square)
+            for power in (act, rea):
+                sq = ring.tile([P, PACK, P], F32, name="square", tag="square", bufs=8)
+                nc.scalar.activation(out=sq[:], in_=power[:].rearrange("j (p t) -> j t p", t=PACK), func=ACT.Square)
                 squares.append(sq)
+            return squares
+
+        def apparent_power(u, squares, parts=1):
+            b, j0 = divmod(u * P, S)
             planes = PACK // parts
             for part in range(parts):
-                total = psum.tile([P, planes, P], F32, name=f"bank{2 + part}", tag=f"bank{2 + part}")
+                total = bank("sum", [P, planes, P])
                 for t in range(planes):
                     for n, sq in enumerate(squares):
                         nc.tensor.matmul(total[:, t, :], sq[:, part * planes + t, :], ident[:], start=(n == 0), stop=(n == 1), is_transpose=True)
-                nc.scalar.activation(out=h[:, part * planes : (part + 1) * planes, js], in_=total[:], func=ACT.Sqrt, bias=under_root[:])
+                nc.scalar.activation(out=h[b][:, part * planes : (part + 1) * planes, j0 : j0 + P], in_=total[:], func=ACT.Sqrt, bias=under_root[:])
 
-        def scatter(page, h, t, j0, j1):
+        def scatter(b, t, j0, j1):
             cols = offs2_t[:, j0 // LIST_COL : j1 // LIST_COL]
-            nc.vector.tensor_tensor(page[:].indirect(cols), h[:, t, j0:j1], wgs_t[:, j0:j1], MULT)
+            nc.gpsimd.tensor_tensor(h[b][:, t, j0:j1], h[b][:, t, j0:j1], wgs_t[:, j0:j1], MULT)
+            nc.vector.tensor_copy(out=pages[PACK * b + t][:].indirect(cols), in_=h[b][:, t, j0:j1])
 
-        def inverse_rating(b, t, inv_root=None):
+        def inverse_rating(b, t):
             inv = slot(f"inv{PACK * b + t}", [P, T2], F32)
             nc.sync.dma_start(out=inv[:], in_=rating[b * PASS : (b + 1) * PASS, :].rearrange("(p t) m -> p t m", t=PACK)[:, t, :])
-            between = inv if inv_root is None else inv_root
             halves = (slice(0, T2 // 2), slice(T2 // 2, T2))
             for ms in halves:
-                nc.scalar.activation(out=between[:, ms], in_=inv[:, ms], func=ACT.Abs_reciprocal_sqrt)
+                nc.scalar.activation(out=inv_root[:, ms], in_=inv[:, ms], func=ACT.Abs_reciprocal_sqrt)
             for ms in halves:
-                nc.scalar.activation(out=inv[:, ms], in_=between[:, ms], func=ACT.Square)
+                nc.scalar.activation(out=inv[:, ms], in_=inv_root[:, ms], func=ACT.Square)
             return inv
 
-        def divide(z, t, page, inv, ms):
-            nc.vector.tensor_tensor(z[:, t, ms], page[:, ms], inv[:, ms], MULT)
+        def divide(b, t, ms):
+            n = PACK * b + t
+            (nc.gpsimd if b == 0 else nc.vector).tensor_tensor(z[b][:, t, ms], pages[n][:, ms], invs[n][:, ms], MULT)
 
-        def quantise_z(b, z, ms, copy, grouped):
-            interleave(copy, grouped, z[:, :, ms])
+        def quantise_z(b, ms, copy, grouped=None):
+            if grouped is None:
+                grouped = ring.tile([P, BANK, PACK], BF16, name="grouped", tag="grouped", bufs=3, align_bytes=64)[:]
+            interleave(copy, grouped, z[b][:, :, ms])
             nc.vector.quantize_mx(out=z_w[b][:, ms].bitcast(FP8X4), scales=z_s[b][:, ms], in_=grouped.rearrange("p c t -> p (c t)"))
 
-        h0 = ring.tile([P, PACK, S], F32, name="h0", tag="quad", bufs=3)
-        for page in pages:
+        h = [ring.tile([P, PACK, S], F32, name=f"h{b}", tag="quad", bufs=2) for b in range(2)]
+        for page in pages[:3]:
             nc.vector.memset(page[:].bitcast(I32), 0)
+        for ms in chunks:
+            nc.gpsimd.memset(pages[3][:, ms].bitcast(I32), 0)
         quantise_wp(0, raw0)
         wgs_t = slot("wgs", [P, S], F32)
         nc.sync.dma_start(out=wgs_t[:], in_=wgs)
         gather(0, 256)
-        apparent_power(0, h0, 0, parts=2)
+        apparent_power(0, squared_powers(0), parts=2)
         gather(256, 512)
-        apparent_power(0, h0, 128)
         gather(512, 1024)
         raw1 = load_wp(1)
+        units = 2 * S // P
+        squares = {u: squared_powers(u) for u in (1, 2)}
+        apparent_power(1, squares[1])
         quantise_wp(1, raw1)
-        for j0 in range(256, S, P):
-            apparent_power(0, h0, j0)
-        for j0, j1 in ((0, 128), (128, 256), (256, 384), (384, 640), (640, 1024)):
-            for t in range(PACK):
-                scatter(pages[t], h0, t, j0, j1)
-
-        h1 = ring.tile([P, PACK, S], F32, name="h1", tag="quad", bufs=3)
-        for j0 in range(0, S, P):
-            apparent_power(1, h1, j0)
+        squares[3] = squared_powers(3)
+        for u in range(2, units):
+            if u + 2 < units:
+                squares[u + 2] = squared_powers(u + 2)
+            apparent_power(u, squares[u])
+        for b, cuts in enumerate(((0, 128, 256, 384, 512, 768, 1024), (0, 512, 1024))):
+            if b == 1:
+                for page in pages[PACK:]:
+                    for ms in chunks:
+                        nc.gpsimd.memset(page[:, ms].bitcast(I32), 0)
+            for j0, j1 in zip(cuts, cuts[1:]):
+                for t in range(PACK):
+                    scatter(b, t, j0, j1)
 
         inv_root = slot("root", [P, T2], F32)
-        invs = [inverse_rating(n // PACK, n % PACK, inv_root) for n in range(7)]
+        invs = [inverse_rating(n // PACK, n % PACK) for n in range(2 * PACK)]
         wm_w = slot("weight_words", [P, 2, N], I32)
         wm_s = slot("weight_scales", [P, N], U8)
         nc.sync.dma_start(out=wm_w[:], in_=wm_words.rearrange("a p n t -> p a (n t)").bitcast(I32))
@@ -171,38 +188,32 @@ def tile_list_apparent_power_margins_kernel(
             nc.sync.dma_start(out=wm_s[32 * q : 32 * q + 8, :].bitcast(I32), in_=wm_scales[:, 4 * q : 4 * q + 4, :].bitcast(I32))
 
         everything = slice(0, T2)
-        chunks = [slice(m0, m0 + BANK) for m0 in range(0, T2, BANK)]
-        z0 = ring.tile([P, PACK, T2], BF16, name="z0", tag="quad", bufs=3)
-        z1 = ring.tile([P, PACK, T2], BF16, name="z1", tag="quad", bufs=3)
-        scatter(pages[4], h1, 0, 0, S // 2)
-        scatter(pages[4], h1, 0, S // 2, S)
-        divide(z0, 0, pages[0], invs[0], everything)
-        scatter(pages[0], h1, 1, 0, S)
-        divide(z0, 1, pages[1], invs[1], everything)
-        divide(z0, 2, pages[2], invs[2], everything)
-        scatter(pages[2], h1, 2, 0, S)
-        divide(z0, 3, pages[3], invs[3], everything)
-        divide(z1, 0, pages[4], invs[4], everything)
-        divide(z1, 1, pages[0], invs[5], everything)
-        divide(z1, 2, pages[2], invs[6], everything)
-        scatter(pages[2], h1, 3, 0, S)
-        grouped0 = slot("root", [P, T2, PACK], BF16)
-        for ms in chunks:
-            quantise_z(0, z0, ms, nc.scalar.copy, grouped0[:, ms, :])
-        inv7 = inverse_rating(1, 3)
+        z = [ring.tile([P, PACK, T2], BF16, name=f"z{b}", tag="quad", bufs=2) for b in range(2)]
+        for t in range(PACK):
+            divide(0, t, everything)
+        for ms in chunks[:3]:
+            quantise_z(0, ms, nc.vector.tensor_copy)
+        for t in range(PACK - 1):
+            divide(1, t, everything)
+        late = slot("root", [P, 1, BANK, PACK], BF16)
+        for n, ms in enumerate(chunks[3:]):
+            quantise_z(0, ms, nc.scalar.copy, late[:, n])
+        divide(1, PACK - 1, chunks[0])
+        divide(1, PACK - 1, chunks[-1])
         for c, ms in enumerate(chunks):
-            divide(z1, 3, pages[2], inv7, ms)
-            grouped1 = ring.tile([P, BANK, PACK], BF16, name="grouped1", tag="grouped1", bufs=3, align_bytes=64)
-            quantise_z(1, z1, ms, nc.scalar.copy if c == 0 else nc.vector.tensor_copy, grouped1[:])
+            if 0 < c < len(chunks) - 1:
+                divide(1, PACK - 1, ms)
+            quantise_z(1, ms, nc.scalar.copy if c == len(chunks) - 1 else nc.vector.tensor_copy)
+        rotation = ("act", "rea", "sum", "act", "rea", "sum", "act", "rea")
         for c, ms in enumerate(chunks):
             res = slot(f"inv{c}", [P, N // P, BANK], F32)
             for n0 in range(0, N, P):
                 ns = slice(n0, n0 + P)
-                acc = psum.tile([P, BANK], F32, name=f"bank{n0 // P}", tag=f"bank{n0 // P}")
+                acc = bank(rotation[(c * N + n0) // P % len(rotation)], [P, BANK])
                 for b in range(2):
                     nc.tensor.matmul_mx(out=acc[:], lhsT=wm_w[:, b, ns].bitcast(FP8X4), lhsT_scale=wm_s[4 * b : P, ns],
                                         rhs=z_w[b][:, ms].bitcast(FP8X4), rhs_scale=z_s[b][:, ms],
                                         start=(b == 0), stop=(b == 1))
-                copy = nc.vector.tensor_copy if c == len(chunks) - 1 else nc.scalar.copy
+                copy = nc.vector.tensor_copy if c == len(chunks) - 1 and n0 % (2 * P) == 0 else nc.scalar.copy
                 copy(out=res[:, n0 // P, :], in_=acc[:])
                 nc.sync.dma_start(out=out[ns, ms], in_=res[:, n0 // P, :])

@@ -16,13 +16,17 @@ FP8X4 = mybir.dt.float8_e4m3fn_x4
 FP4X4 = mybir.dt.float4_e2m1fn_x4
 ACT = mybir.ActivationFunctionType
 MULT = mybir.AluOpType.mult
+ADD = mybir.AluOpType.add
 
 P = 128
 PACK = 4
 PASS = P * PACK
 BANK = 512
 LIST_COL = 16
+PLANES = H // P
+PAGES = 6
 BANKS = {"act": 3, "rea": 3, "sum": 2}
+PAGE_BYTES = 4 * T2
 
 
 def tile_list_apparent_power_margins_kernel(
@@ -32,6 +36,7 @@ def tile_list_apparent_power_margins_kernel(
     with ExitStack() as ctx:
         keep = ctx.enter_context(tc.tile_pool(name="keep", bufs=1))
         ring = ctx.enter_context(tc.tile_pool(name="ring", bufs=1))
+        placed = ctx.enter_context(tc.tile_pool(name="placed", bufs=1))
         psum = ctx.enter_context(tc.psum_pool(name="psum", bufs=1))
 
         def load_scales(queue, dst, src_rows):
@@ -41,179 +46,209 @@ def tile_list_apparent_power_margins_kernel(
         def interleave(copy, dst, src):
             copy(out=dst.rearrange("p (c i) t -> p c t i", i=4), in_=src.rearrange("p t (c i) -> p c t i", i=4))
 
-        def slot(tag, shape, dtype):
-            return ring.tile(shape, dtype, name=tag, tag=tag, bufs=1, align_bytes=64)
+        def slot(tag, shape, dtype, bufs=1):
+            return ring.tile(shape, dtype, name=tag, tag=tag, bufs=bufs, align_bytes=64)
+
+        def at(name, offset, shape, dtype):
+            return placed.tile(shape, dtype, name=name, tag=name, bufs=1, align_bytes=64, offset=offset)
 
         def bank(tag, shape):
             return psum.tile(shape, F32, name=tag, tag=tag, bufs=BANKS[tag])
 
+        def quantise(words, scales, grouped):
+            nc.vector.quantize_mx(out=words.bitcast(FP8X4), scales=scales, in_=grouped.rearrange("p c t -> p (c t)"))
+
+        chunks = [slice(m0, m0 + BANK) for m0 in range(0, T2, BANK)]
+        halves = (slice(0, T2 // 2), slice(T2 // 2, T2))
+
         offs_t = keep.tile([P, S // LIST_COL], U16, name="offs_t")
         offs2_t = keep.tile([P, S // LIST_COL], U16, name="offs2_t")
-        tab_s = slot("inv0", [P, T], U8)
-        wq_w = slot("weight_words", [P, 2 * H], U8)
-        wq_s = slot("weight_scales", [P, H], U8)
-        v_w = slot("inv7", [P, S], U32)
-        v_s = slot("inv2", [P, S], U8)
-        wp_w = [slot(tag, [P, PASS], U32) for tag in ("inv3", "inv5")]
-        wp_s = [slot(tag, [P, PASS], U8) for tag in ("inv4", "inv6")]
+        ident = keep.tile([P, P], F32, name="ident")
+        wq_s = keep.tile([P, H], U8, name="wq_s", align_bytes=64)
+        v_s = keep.tile([P, S], U8, name="v_s", align_bytes=64)
         z_w = [keep.tile([P, T2], U32, name=f"z_w{b}", align_bytes=64) for b in range(2)]
         z_s = [keep.tile([P, T2], U8, name=f"z_s{b}", align_bytes=64) for b in range(2)]
-        ident = keep.tile([P, P], F32, name="ident")
-        under_root = ring.tile([P, 1], F32, name="under_root", tag="root", bufs=1, align_bytes=64)
-        squared_const = slot("inv1", [P, 1], F32)
-        pages = [keep.tile([P, T2], F32, name=f"page{n}") for n in range(2 * PACK)]
-        chunks = [slice(m0, m0 + BANK) for m0 in range(0, T2, BANK)]
+        v_w = slot("rating2", [P, S], U32)
+        wp_w = [slot(f"words{b}", [P, PASS], U32) for b in range(2)]
+        wp_s = [slot(f"scales{b}", [P, PASS], U8) for b in range(2)]
+        tab_w = slot("pairs1", [P, T], I32)
+        under_root = slot("root", [P, 1], F32)
+        squared_const = at("squared_const", PAGE_BYTES - 64, [P, 32], F32)
+        tab_s = at("tab_s", 2 * PAGE_BYTES + 2 * H - T // 2, [P, T], U8)
+        pages = [keep.tile([P, T2], F32, name=f"page{n}") for n in range(2)]
 
-        nc.gpsimd.memset(tab_s[:].bitcast(I32), 0)
-        nc.gpsimd.memset(wq_s[:].bitcast(I32), 0)
-        load_scales(nc.gpsimd, wq_s, wq_scales[0])
-        load_scales(nc.scalar, tab_s, tab_scales[0])
-        nc.vector.memset(squared_const[:], 1.0 / 64.0)
-        nc.scalar.activation(out=under_root[:], in_=squared_const[:], func=ACT.Sqrt)
-        make_identity(nc, ident[:])
-
-        def load_wp(b):
-            raw = slot(("wgs", "inv1")[b], [P, PACK, PASS], F32)
-            nc.sync.dma_start(out=raw[:], in_=wp[:, b * PASS : (b + 1) * PASS].rearrange("(p t) c -> p t c", t=PACK))
-            return raw
-
-        def quantise_wp(b, raw):
-            grouped = ring.tile([P, PASS, PACK], BF16, name="grouped", tag="grouped", bufs=3, align_bytes=64)
-            interleave(nc.scalar.copy, grouped[:], raw[:])
-            nc.vector.quantize_mx(out=wp_w[b][:].bitcast(FP8X4), scales=wp_s[b][:], in_=grouped[:].rearrange("p c t -> p (c t)"))
-
+        nc.vector.memset(tab_s[:].bitcast(I32), 0)
+        nc.vector.memset(wq_s[:].bitcast(I32), 0)
         nc.sync.dma_start(offs_t[:], offs)
-        raw0 = load_wp(0)
-        tab_w = slot("inv1", [P, T], I32)
         nc.sync.dma_start(out=tab_w[:], in_=tab_words[0].rearrange("p n t -> p (n t)").bitcast(I32))
-        nc.sync.dma_start(out=wq_w[:].bitcast(I32), in_=wq_words[0].bitcast(I32))
+        raw0 = slot("page4", [P, PACK, PASS], F32)
+        nc.sync.dma_start(out=raw0[:], in_=wp[:, 0:PASS].rearrange("(p t) c -> p t c", t=PACK))
+        load_scales(nc.scalar, tab_s, tab_scales[0])
         nc.sync.dma_start(offs2_t[:], offs2)
+        load_scales(nc.scalar, wq_s, wq_scales[0])
+        make_identity(nc, ident[:])
+        for page in pages:
+            nc.vector.memset(page[:].bitcast(I32), 0)
+        nc.vector.memset(squared_const[:, 0:1], 1.0 / 64.0)
+        nc.scalar.activation(out=under_root[:], in_=squared_const[:, 0:1], func=ACT.Sqrt)
+        wq_w = at("wq_w", PAGE_BYTES, [P, 2 * H], U8)
+        nc.sync.dma_start(out=wq_w[:].bitcast(I32), in_=wq_words[0].bitcast(I32))
 
-        def gather(j0, j1):
-            cols = offs_t[:, j0 // LIST_COL : j1 // LIST_COL]
-            nc.vector.tensor_copy(out=v_w[:, j0:j1], in_=tab_w[:].bitcast(U32).indirect(cols))
-            nc.vector.tensor_copy(out=v_s[:, j0:j1], in_=tab_s[:].indirect(cols))
+        def clear(page):
+            for ms in chunks:
+                nc.gpsimd.memset(page[:, ms].bitcast(I32), 0)
 
-        def squared_powers(u):
+        pages.append(at("page2", 0, [P, T2], F32))
+        clear(pages[2])
+        nc.vector.tensor_copy(out=v_s[:], in_=tab_s[:].indirect(offs_t[:]))
+        wgs_t = at("wgs_t", 2 * PAGE_BYTES + 2 * H, [P, S], F32)
+        nc.sync.dma_start(out=wgs_t[:], in_=wgs)
+        pages.append(at("page3", PAGE_BYTES + 2 * H, [P, T2], F32))
+        clear(pages[3])
+        nc.vector.tensor_copy(out=v_w[:], in_=tab_w[:].bitcast(U32).indirect(offs_t[:]))
+        half = PASS // 2
+        grouped0 = [slot(tag, [P, half, PACK], BF16) for tag in ("page5", "rating0")]
+        interleave(nc.scalar.copy, grouped0[0][:], raw0[:, :, 0:half])
+        interleave(nc.vector.tensor_copy, grouped0[1][:], raw0[:, :, half:PASS])
+        for n in range(2):
+            cs = slice(n * half, (n + 1) * half)
+            quantise(wp_w[0][:, cs], wp_s[0][:, cs], grouped0[n][:])
+        raw1 = slot("rating0", [P, PACK, PASS], F32)
+        nc.sync.dma_start(out=raw1[:], in_=wp[:, PASS:H].rearrange("(p t) c -> p t c", t=PACK))
+
+        h = [slot(f"h{b}", [P, PACK, S], F32) for b in range(2)]
+
+        def squared_powers(u, parts=1):
             b, j0 = divmod(u * P, S)
             js = slice(j0, j0 + P)
-            rs = slice(b * PASS, (b + 1) * PASS)
+            rea = bank("rea", [P, BANK])
+            nc.tensor.matmul_mx(out=rea[:], lhsT=v_w[:, js].bitcast(FP8X4), lhsT_scale=v_s[:, js],
+                                rhs=wq_w[:, 2 * b * PASS : 2 * (b + 1) * PASS].bitcast(FP4X4),
+                                rhs_scale=wq_s[:, b * PASS : (b + 1) * PASS], start=True, stop=True)
             act = bank("act", [P, BANK])
             nc.tensor.matmul_mx(out=act[:], lhsT=v_w[:, js].bitcast(FP8X4), lhsT_scale=v_s[:, js],
                                 rhs=wp_w[b][:].bitcast(FP8X4), rhs_scale=wp_s[b][:], start=True, stop=True)
-            rea = bank("rea", [P, BANK])
-            nc.tensor.matmul_mx(out=rea[:], lhsT=v_w[:, js].bitcast(FP8X4), lhsT_scale=v_s[:, js],
-                                rhs=wq_w[:, 2 * b * PASS : 2 * (b + 1) * PASS].bitcast(FP4X4), rhs_scale=wq_s[:, rs],
-                                start=True, stop=True)
             squares = []
-            for power in (act, rea):
-                sq = ring.tile([P, PACK, P], F32, name="square", tag="square", bufs=8)
-                nc.scalar.activation(out=sq[:], in_=power[:].rearrange("j (p t) -> j t p", t=PACK), func=ACT.Square)
+            for power, pieces in ((rea, 1), (act, parts)):
+                sq = slot("square", [P, PACK, P], F32, bufs=8)
+                planes = PACK // pieces
+                for t0 in range(0, PACK, planes):
+                    ts = slice(t0, t0 + planes)
+                    nc.scalar.activation(out=sq[:, ts, :], in_=power[:].rearrange("j (p t) -> j t p", t=PACK)[:, ts, :], func=ACT.Square)
                 squares.append(sq)
             return squares
 
         def apparent_power(u, squares, parts=1):
             b, j0 = divmod(u * P, S)
+            js = slice(j0, j0 + P)
             planes = PACK // parts
-            for part in range(parts):
+            for t0 in range(0, PACK, planes):
+                ts = slice(t0, t0 + planes)
                 total = bank("sum", [P, planes, P])
                 for t in range(planes):
                     for n, sq in enumerate(squares):
-                        nc.tensor.matmul(total[:, t, :], sq[:, part * planes + t, :], ident[:], start=(n == 0), stop=(n == 1), is_transpose=True)
-                nc.scalar.activation(out=h[b][:, part * planes : (part + 1) * planes, j0 : j0 + P], in_=total[:], func=ACT.Sqrt, bias=under_root[:])
+                        nc.tensor.matmul(total[:, t, :], sq[:, t0 + t, :], ident[:], start=(n == 0), stop=(n == 1), is_transpose=True)
+                nc.scalar.activation(out=h[b][:, ts, js], in_=total[:], func=ACT.Sqrt, bias=under_root[:])
+                nc.gpsimd.tensor_tensor(h[b][:, ts, js], h[b][:, ts, js], wgs_t[:, js].unsqueeze(1).to_broadcast([P, planes, P]), MULT)
 
-        def scatter(b, t, j0, j1):
+        def scatter(n, j0, j1):
+            b, t = divmod(n, PACK)
             cols = offs2_t[:, j0 // LIST_COL : j1 // LIST_COL]
-            nc.gpsimd.tensor_tensor(h[b][:, t, j0:j1], h[b][:, t, j0:j1], wgs_t[:, j0:j1], MULT)
-            nc.vector.tensor_copy(out=pages[PACK * b + t][:].indirect(cols), in_=h[b][:, t, j0:j1])
+            nc.vector.tensor_copy(out=pages[n % PAGES][:].indirect(cols), in_=h[b][:, t, j0:j1])
 
-        def inverse_rating(b, t):
-            inv = slot(f"inv{PACK * b + t}", [P, T2], F32)
-            nc.sync.dma_start(out=inv[:], in_=rating[b * PASS : (b + 1) * PASS, :].rearrange("(p t) m -> p t m", t=PACK)[:, t, :])
-            halves = (slice(0, T2 // 2), slice(T2 // 2, T2))
-            for ms in halves:
-                nc.scalar.activation(out=inv_root[:, ms], in_=inv[:, ms], func=ACT.Abs_reciprocal_sqrt)
-            for ms in halves:
-                nc.scalar.activation(out=inv[:, ms], in_=inv_root[:, ms], func=ACT.Square)
-            return inv
-
-        def divide(b, t, ms):
-            n = PACK * b + t
-            (nc.gpsimd if b == 0 else nc.vector).tensor_tensor(z[b][:, t, ms], pages[n][:, ms], invs[n][:, ms], MULT)
-
-        def quantise_z(b, ms, copy, grouped=None):
-            if grouped is None:
-                grouped = ring.tile([P, BANK, PACK], BF16, name="grouped", tag="grouped", bufs=3, align_bytes=64)[:]
-            interleave(copy, grouped, z[b][:, :, ms])
-            nc.vector.quantize_mx(out=z_w[b][:, ms].bitcast(FP8X4), scales=z_s[b][:, ms], in_=grouped.rearrange("p c t -> p (c t)"))
-
-        h = [ring.tile([P, PACK, S], F32, name=f"h{b}", tag="quad", bufs=2) for b in range(2)]
-        for page in pages[:3]:
-            nc.vector.memset(page[:].bitcast(I32), 0)
-        for ms in chunks:
-            nc.gpsimd.memset(pages[3][:, ms].bitcast(I32), 0)
-        quantise_wp(0, raw0)
-        wgs_t = slot("wgs", [P, S], F32)
-        nc.sync.dma_start(out=wgs_t[:], in_=wgs)
-        gather(0, 256)
-        apparent_power(0, squared_powers(0), parts=2)
-        gather(256, 512)
-        gather(512, 1024)
-        raw1 = load_wp(1)
         units = 2 * S // P
-        squares = {u: squared_powers(u) for u in (1, 2)}
+        squares = {0: squared_powers(0, parts=PACK)}
+        squares[1] = squared_powers(1)
+        apparent_power(0, squares[0], parts=PACK)
+        squares[2] = squared_powers(2)
         apparent_power(1, squares[1])
-        quantise_wp(1, raw1)
-        squares[3] = squared_powers(3)
+        grouped1 = slot("rating1", [P, PASS, PACK], BF16)
         for u in range(2, units):
-            if u + 2 < units:
-                squares[u + 2] = squared_powers(u + 2)
+            if u < 4:
+                cs = slice((u - 2) * half, (u - 1) * half)
+                nc.gpsimd.tensor_scalar(grouped1[:, cs, :], raw1[:, :, cs].rearrange("p t c -> p c t"), 1.0, 0.0, MULT, ADD)
+            if u == 4:
+                quantise(wp_w[1][:], wp_s[1][:], grouped1[:])
+            if u + 1 < units:
+                squares[u + 1] = squared_powers(u + 1)
             apparent_power(u, squares[u])
-        for b, cuts in enumerate(((0, 128, 256, 384, 512, 768, 1024), (0, 512, 1024))):
-            if b == 1:
-                for page in pages[PACK:]:
-                    for ms in chunks:
-                        nc.gpsimd.memset(page[:, ms].bitcast(I32), 0)
-            for j0, j1 in zip(cuts, cuts[1:]):
-                for t in range(PACK):
-                    scatter(b, t, j0, j1)
+        cuts = (0, 128, 256, 384, 640, 1024)
+        for j0, j1 in zip(cuts, cuts[1:]):
+            for t in range(PACK):
+                scatter(t, j0, j1)
+        for n in (4, 5):
+            pages.append(slot(f"page{n}", [P, T2], F32))
+            clear(pages[n])
+        for j0 in (0, S // 2):
+            for n in (4, 5):
+                scatter(n, j0, j0 + S // 2)
 
         inv_root = slot("root", [P, T2], F32)
-        invs = [inverse_rating(n // PACK, n % PACK) for n in range(2 * PACK)]
-        wm_w = slot("weight_words", [P, 2, N], I32)
-        wm_s = slot("weight_scales", [P, N], U8)
+
+        def inverse_ratings(pair):
+            inv = slot(f"rating{pair % 3}", [P, 2, T2], F32)
+            b, t0 = divmod(2 * pair, PACK)
+            nc.sync.dma_start(out=inv[:], in_=rating[b * PASS : (b + 1) * PASS, :].rearrange("(p t) m -> p t m", t=PACK)[:, t0 : t0 + 2, :])
+            for e in range(2):
+                for ms in halves:
+                    nc.scalar.activation(out=inv_root[:, ms], in_=inv[:, e, ms], func=ACT.Abs_reciprocal_sqrt)
+                for ms in halves:
+                    nc.scalar.activation(out=inv[:, e, ms], in_=inv_root[:, ms], func=ACT.Square)
+            return inv
+
+        invs = [inverse_ratings(pair) for pair in range(3)]
+        wm_w = slot("words0", [P, 2, N], I32)
+        wm_s = slot("scales0", [P, N], U8)
         nc.sync.dma_start(out=wm_w[:], in_=wm_words.rearrange("a p n t -> p a (n t)").bitcast(I32))
         nc.gpsimd.memset(wm_s[:].bitcast(I32), 0)
         for q in range(4):
             nc.sync.dma_start(out=wm_s[32 * q : 32 * q + 8, :].bitcast(I32), in_=wm_scales[:, 4 * q : 4 * q + 4, :].bitcast(I32))
 
+        zp = [slot(tag, [P, 2, T2, 2], BF16) for tag in ("h0", "pairs1")]
+
+        def divide(engine, n, ms):
+            pair, e = divmod(n, 2)
+            engine.tensor_tensor(zp[n // PACK][:, pair % 2, ms, e], pages[n % PAGES][:, ms], invs[pair][:, e, ms], MULT)
+
+        def weave(b, ms):
+            grouped = slot("grouped", [P, BANK, PACK], BF16, bufs=3)
+            src = zp[b][:].rearrange("p u m e -> p u (m e)").bitcast(I32)[:, :, ms]
+            nc.vector.tensor_copy(out=grouped[:].rearrange("p m t -> p (m t)").bitcast(I32).rearrange("p (m u) -> p m u", u=2),
+                                  in_=src.rearrange("p u m -> p m u"))
+            return grouped
+
         everything = slice(0, T2)
-        z = [ring.tile([P, PACK, T2], BF16, name=f"z{b}", tag="quad", bufs=2) for b in range(2)]
-        for t in range(PACK):
-            divide(0, t, everything)
-        for ms in chunks[:3]:
-            quantise_z(0, ms, nc.vector.tensor_copy)
-        for t in range(PACK - 1):
-            divide(1, t, everything)
-        late = slot("root", [P, 1, BANK, PACK], BF16)
-        for n, ms in enumerate(chunks[3:]):
-            quantise_z(0, ms, nc.scalar.copy, late[:, n])
-        divide(1, PACK - 1, chunks[0])
-        divide(1, PACK - 1, chunks[-1])
+        for n in range(PAGES):
+            divide(nc.gpsimd, n, everything)
+            if n + PAGES < PLANES:
+                scatter(n + PAGES, 0, S)
+            if n == 1:
+                invs.append(inverse_ratings(3))
+        woven = [weave(0, chunks[0])]
         for c, ms in enumerate(chunks):
-            if 0 < c < len(chunks) - 1:
-                divide(1, PACK - 1, ms)
-            quantise_z(1, ms, nc.scalar.copy if c == len(chunks) - 1 else nc.vector.tensor_copy)
+            if c + 1 < len(chunks):
+                woven.append(weave(0, chunks[c + 1]))
+            quantise(z_w[0][:, ms], z_s[0][:, ms], woven[c][:])
+        woven = []
+        for c, ms in enumerate(chunks):
+            divide(nc.vector, 6, ms)
+            divide(nc.vector, 7, ms)
+            if c > 0:
+                quantise(z_w[1][:, chunks[c - 1]], z_s[1][:, chunks[c - 1]], woven[c - 1][:])
+            woven.append(weave(1, ms))
+        quantise(z_w[1][:, chunks[-1]], z_s[1][:, chunks[-1]], woven[-1][:])
+
         rotation = ("act", "rea", "sum", "act", "rea", "sum", "act", "rea")
         for c, ms in enumerate(chunks):
-            res = slot(f"inv{c}", [P, N // P, BANK], F32)
-            for n0 in range(0, N, P):
-                ns = slice(n0, n0 + P)
-                acc = bank(rotation[(c * N + n0) // P % len(rotation)], [P, BANK])
-                for b in range(2):
+            accs = [bank(rotation[(c * PACK + k) % len(rotation)], [P, BANK]) for k in range(N // P)]
+            for b in range(2):
+                for k, acc in enumerate(accs):
+                    ns = slice(k * P, (k + 1) * P)
                     nc.tensor.matmul_mx(out=acc[:], lhsT=wm_w[:, b, ns].bitcast(FP8X4), lhsT_scale=wm_s[4 * b : P, ns],
                                         rhs=z_w[b][:, ms].bitcast(FP8X4), rhs_scale=z_s[b][:, ms],
                                         start=(b == 0), stop=(b == 1))
-                copy = nc.vector.tensor_copy if c == len(chunks) - 1 and n0 % (2 * P) == 0 else nc.scalar.copy
-                copy(out=res[:, n0 // P, :], in_=acc[:])
-                nc.sync.dma_start(out=out[ns, ms], in_=res[:, n0 // P, :])
+            for k, acc in enumerate(accs):
+                res = slot("square", [P, BANK], F32, bufs=8)
+                copy = nc.vector.tensor_copy if c == len(chunks) - 1 and k % 2 == 0 else nc.scalar.copy
+                copy(out=res[:], in_=acc[:])
+                nc.sync.dma_start(out=out[k * P : (k + 1) * P, ms], in_=res[:])

@@ -16,7 +16,6 @@ FP8X4 = mybir.dt.float8_e4m3fn_x4
 FP4X4 = mybir.dt.float4_e2m1fn_x4
 ACT = mybir.ActivationFunctionType
 MULT = mybir.AluOpType.mult
-ADD = mybir.AluOpType.add
 
 P = 128
 PACK = 4
@@ -26,7 +25,6 @@ LIST_COL = 16
 PLANES = H // P
 PAGES = 6
 BANKS = {"act": 3, "rea": 3, "sum": 2}
-PAGE_BYTES = 4 * T2
 
 
 def tile_list_apparent_power_margins_kernel(
@@ -68,65 +66,70 @@ def tile_list_apparent_power_margins_kernel(
         v_s = keep.tile([P, S], U8, name="v_s", align_bytes=64)
         z_w = [keep.tile([P, T2], U32, name=f"z_w{b}", align_bytes=64) for b in range(2)]
         z_s = [keep.tile([P, T2], U8, name=f"z_s{b}", align_bytes=64) for b in range(2)]
-        v_w = slot("rating2", [P, S], U32)
-        wp_w = [slot(f"words{b}", [P, PASS], U32) for b in range(2)]
+        half = PASS // 2
+        v_first = keep.tile([P, S // 2], U32, name="v_first", align_bytes=64)
+        wp_w = [slot(tag, [P, PASS], U32) for tag in ("rating1", "words")]
         wp_s = [slot(f"scales{b}", [P, PASS], U8) for b in range(2)]
-        tab_w = slot("pairs1", [P, T], I32)
+        tab_w = slot("z1", [P, T], I32)
         under_root = slot("root", [P, 1], F32)
-        squared_const = at("squared_const", PAGE_BYTES - 64, [P, 32], F32)
-        tab_s = at("tab_s", 2 * PAGE_BYTES + 2 * H - T // 2, [P, T], U8)
-        pages = [keep.tile([P, T2], F32, name=f"page{n}") for n in range(2)]
-
-        nc.vector.memset(tab_s[:].bitcast(I32), 0)
-        nc.vector.memset(wq_s[:].bitcast(I32), 0)
-        nc.sync.dma_start(offs_t[:], offs)
-        nc.sync.dma_start(out=tab_w[:], in_=tab_words[0].rearrange("p n t -> p (n t)").bitcast(I32))
-        raw0 = slot("page4", [P, PACK, PASS], F32)
-        nc.sync.dma_start(out=raw0[:], in_=wp[:, 0:PASS].rearrange("(p t) c -> p t c", t=PACK))
-        load_scales(nc.scalar, tab_s, tab_scales[0])
-        nc.sync.dma_start(offs2_t[:], offs2)
-        load_scales(nc.scalar, wq_s, wq_scales[0])
-        make_identity(nc, ident[:])
-        for page in pages:
-            nc.vector.memset(page[:].bitcast(I32), 0)
-        nc.vector.memset(squared_const[:, 0:1], 1.0 / 64.0)
-        nc.scalar.activation(out=under_root[:], in_=squared_const[:, 0:1], func=ACT.Sqrt)
-        wq_w = at("wq_w", PAGE_BYTES, [P, 2 * H], U8)
-        nc.sync.dma_start(out=wq_w[:].bitcast(I32), in_=wq_words[0].bitcast(I32))
+        squared_const = slot("wq_w", [P, 1], F32)
+        tab_s = at("tab_s", 4 * S - T // 2, [P, T], U8)
+        pages = [keep.tile([P, T2], F32, name=f"page{n}") for n in range(3)]
 
         def clear(page):
             for ms in chunks:
                 nc.gpsimd.memset(page[:, ms].bitcast(I32), 0)
 
-        pages.append(at("page2", 0, [P, T2], F32))
+        nc.gpsimd.memset(tab_s[:].bitcast(I32), 0)
+        nc.gpsimd.memset(wq_s[:].bitcast(I32), 0)
+        nc.vector.memset(squared_const[:], 1.0 / 64.0)
+        nc.sync.dma_start(offs_t[:], offs)
+        nc.sync.dma_start(out=tab_w[:], in_=tab_words[0].rearrange("p n t -> p (n t)").bitcast(I32))
+        raw0 = slot("page4", [P, PACK, PASS], F32)
+        nc.sync.dma_start(out=raw0[:], in_=wp[:, 0:PASS].rearrange("(p t) c -> p t c", t=PACK))
+        load_scales(nc.scalar, tab_s, tab_scales[0])
+        nc.scalar.activation(out=under_root[:], in_=squared_const[:], func=ACT.Sqrt)
+        nc.sync.dma_start(offs2_t[:], offs2)
+        load_scales(nc.scalar, wq_s, wq_scales[0])
+        make_identity(nc, ident[:])
+        nc.vector.memset(pages[0][:].bitcast(I32), 0)
+        clear(pages[1])
         clear(pages[2])
+        wq_w = slot("wq_w", [P, 2 * H], U8)
+        nc.sync.dma_start(out=wq_w[:].bitcast(I32), in_=wq_words[0].bitcast(I32))
         nc.vector.tensor_copy(out=v_s[:], in_=tab_s[:].indirect(offs_t[:]))
-        wgs_t = at("wgs_t", 2 * PAGE_BYTES + 2 * H, [P, S], F32)
+        raw1 = at("raw1", 4 * S, [P, PACK, PASS], F32)
+        nc.sync.dma_start(out=raw1[:], in_=wp[:, PASS:H].rearrange("(p t) c -> p t c", t=PACK))
+        wgs_t = at("wgs_t", 0, [P, S], F32)
         nc.sync.dma_start(out=wgs_t[:], in_=wgs)
-        pages.append(at("page3", PAGE_BYTES + 2 * H, [P, T2], F32))
-        clear(pages[3])
-        nc.vector.tensor_copy(out=v_w[:], in_=tab_w[:].bitcast(U32).indirect(offs_t[:]))
-        half = PASS // 2
-        grouped0 = [slot(tag, [P, half, PACK], BF16) for tag in ("page5", "rating0")]
+        nc.vector.tensor_copy(out=v_first[:], in_=tab_w[:].bitcast(U32).indirect(offs_t[:, 0 : S // 2 // LIST_COL]))
+        grouped0 = [slot(tag, [P, half, PACK], BF16) for tag in ("page3", "rating2")]
         interleave(nc.scalar.copy, grouped0[0][:], raw0[:, :, 0:half])
         interleave(nc.vector.tensor_copy, grouped0[1][:], raw0[:, :, half:PASS])
-        for n in range(2):
+        for n in (1, 0):
             cs = slice(n * half, (n + 1) * half)
             quantise(wp_w[0][:, cs], wp_s[0][:, cs], grouped0[n][:])
-        raw1 = slot("rating0", [P, PACK, PASS], F32)
-        nc.sync.dma_start(out=raw1[:], in_=wp[:, PASS:H].rearrange("(p t) c -> p t c", t=PACK))
+        v_second = slot("rating2", [P, S // 2], U32)
+        nc.vector.tensor_copy(out=v_second[:], in_=tab_w[:].bitcast(U32).indirect(offs_t[:, S // 2 // LIST_COL : S // LIST_COL]))
+        v_w = (v_first, v_second)
+        pages.append(slot("page3", [P, T2], F32))
+        clear(pages[3])
+        grouped1 = slot("page5", [P, PASS, PACK], BF16)
+        interleave(nc.vector.tensor_copy, grouped1[:], raw1[:])
+        quantise(wp_w[1][:], wp_s[1][:], grouped1[:])
 
         h = [slot(f"h{b}", [P, PACK, S], F32) for b in range(2)]
 
         def squared_powers(u, parts=1):
             b, j0 = divmod(u * P, S)
             js = slice(j0, j0 + P)
+            words = v_w[2 * j0 // S][:, j0 % (S // 2) : j0 % (S // 2) + P].bitcast(FP8X4)
             rea = bank("rea", [P, BANK])
-            nc.tensor.matmul_mx(out=rea[:], lhsT=v_w[:, js].bitcast(FP8X4), lhsT_scale=v_s[:, js],
+            nc.tensor.matmul_mx(out=rea[:], lhsT=words, lhsT_scale=v_s[:, js],
                                 rhs=wq_w[:, 2 * b * PASS : 2 * (b + 1) * PASS].bitcast(FP4X4),
                                 rhs_scale=wq_s[:, b * PASS : (b + 1) * PASS], start=True, stop=True)
             act = bank("act", [P, BANK])
-            nc.tensor.matmul_mx(out=act[:], lhsT=v_w[:, js].bitcast(FP8X4), lhsT_scale=v_s[:, js],
+            nc.tensor.matmul_mx(out=act[:], lhsT=words, lhsT_scale=v_s[:, js],
                                 rhs=wp_w[b][:].bitcast(FP8X4), rhs_scale=wp_s[b][:], start=True, stop=True)
             squares = []
             for power, pieces in ((rea, 1), (act, parts)):
@@ -162,13 +165,7 @@ def tile_list_apparent_power_margins_kernel(
         apparent_power(0, squares[0], parts=PACK)
         squares[2] = squared_powers(2)
         apparent_power(1, squares[1])
-        grouped1 = slot("rating1", [P, PASS, PACK], BF16)
         for u in range(2, units):
-            if u < 4:
-                cs = slice((u - 2) * half, (u - 1) * half)
-                nc.gpsimd.tensor_scalar(grouped1[:, cs, :], raw1[:, :, cs].rearrange("p t c -> p c t"), 1.0, 0.0, MULT, ADD)
-            if u == 4:
-                quantise(wp_w[1][:], wp_s[1][:], grouped1[:])
             if u + 1 < units:
                 squares[u + 1] = squared_powers(u + 1)
             apparent_power(u, squares[u])
@@ -186,35 +183,37 @@ def tile_list_apparent_power_margins_kernel(
         inv_root = slot("root", [P, T2], F32)
 
         def inverse_ratings(pair):
-            inv = slot(f"rating{pair % 3}", [P, 2, T2], F32)
+            inv = at(f"rating{pair}", 4 * S, [P, 2, T2], F32) if pair % 3 == 0 else slot(f"rating{pair}", [P, 2, T2], F32)
             b, t0 = divmod(2 * pair, PACK)
             nc.sync.dma_start(out=inv[:], in_=rating[b * PASS : (b + 1) * PASS, :].rearrange("(p t) m -> p t m", t=PACK)[:, t0 : t0 + 2, :])
-            for e in range(2):
-                for ms in halves:
-                    nc.scalar.activation(out=inv_root[:, ms], in_=inv[:, e, ms], func=ACT.Abs_reciprocal_sqrt)
-                for ms in halves:
-                    nc.scalar.activation(out=inv[:, e, ms], in_=inv_root[:, ms], func=ACT.Square)
+            if pair < 3:
+                steps = [[(e, ms, ms) for ms in halves] for e in range(2)]
+            else:
+                steps = [[(e, ms, chunks[(2 * c + e) % len(chunks)]) for e in range(2)] for c, ms in enumerate(chunks)]
+            for step in steps:
+                for e, ms, tmp in step:
+                    nc.scalar.activation(out=inv_root[:, tmp], in_=inv[:, e, ms], func=ACT.Abs_reciprocal_sqrt)
+                for e, ms, tmp in step:
+                    nc.scalar.activation(out=inv[:, e, ms], in_=inv_root[:, tmp], func=ACT.Square)
             return inv
 
         invs = [inverse_ratings(pair) for pair in range(3)]
-        wm_w = slot("words0", [P, 2, N], I32)
+        wm_w = slot("words", [P, 2, N], I32)
         wm_s = slot("scales0", [P, N], U8)
         nc.sync.dma_start(out=wm_w[:], in_=wm_words.rearrange("a p n t -> p a (n t)").bitcast(I32))
         nc.gpsimd.memset(wm_s[:].bitcast(I32), 0)
         for q in range(4):
             nc.sync.dma_start(out=wm_s[32 * q : 32 * q + 8, :].bitcast(I32), in_=wm_scales[:, 4 * q : 4 * q + 4, :].bitcast(I32))
 
-        zp = [slot(tag, [P, 2, T2, 2], BF16) for tag in ("h0", "pairs1")]
+        z = [slot(tag, [P, PACK, T2], BF16) for tag in ("h0", "z1")]
 
         def divide(engine, n, ms):
             pair, e = divmod(n, 2)
-            engine.tensor_tensor(zp[n // PACK][:, pair % 2, ms, e], pages[n % PAGES][:, ms], invs[pair][:, e, ms], MULT)
+            engine.tensor_tensor(z[n // PACK][:, n % PACK, ms], pages[n % PAGES][:, ms], invs[pair][:, e, ms], MULT)
 
         def weave(b, ms):
             grouped = slot("grouped", [P, BANK, PACK], BF16, bufs=3)
-            src = zp[b][:].rearrange("p u m e -> p u (m e)").bitcast(I32)[:, :, ms]
-            nc.vector.tensor_copy(out=grouped[:].rearrange("p m t -> p (m t)").bitcast(I32).rearrange("p (m u) -> p m u", u=2),
-                                  in_=src.rearrange("p u m -> p m u"))
+            interleave(nc.vector.tensor_copy, grouped[:], z[b][:, :, ms])
             return grouped
 
         everything = slice(0, T2)

@@ -24,7 +24,8 @@ BANK = 512
 LIST_COL = 16
 PLANES = H // P
 PAGES = 6
-BANKS = {"act": 3, "rea": 3, "sum": 2}
+BANKS = {"act": 2, "rea": 2, "sum": 4}
+SQUARES = 16
 
 
 def tile_list_apparent_power_margins_kernel(
@@ -133,7 +134,7 @@ def tile_list_apparent_power_margins_kernel(
                                 rhs=wp_w[b][:].bitcast(FP8X4), rhs_scale=wp_s[b][:], start=True, stop=True)
             squares = []
             for power, pieces in ((rea, 1), (act, parts)):
-                sq = slot("square", [P, PACK, P], F32, bufs=8)
+                sq = slot("square", [P, PACK, P], F32, bufs=SQUARES)
                 planes = PACK // pieces
                 for t0 in range(0, PACK, planes):
                     ts = slice(t0, t0 + planes)
@@ -163,13 +164,12 @@ def tile_list_apparent_power_margins_kernel(
         squares = {0: squared_powers(0, parts=PACK)}
         squares[1] = squared_powers(1)
         apparent_power(0, squares[0], parts=PACK)
-        squares[2] = squared_powers(2)
-        apparent_power(1, squares[1])
-        for u in range(2, units):
-            if u + 1 < units:
-                squares[u + 1] = squared_powers(u + 1)
+        for u in range(1, units):
+            for ahead in (2 * u - 1, 2 * u):
+                if 1 < ahead < units:
+                    squares[ahead] = squared_powers(ahead)
             apparent_power(u, squares[u])
-        cuts = (0, 128, 256, 384, 640, 1024)
+        cuts = (0, 128, 256, 384, 512, 640, 768, 1024)
         for j0, j1 in zip(cuts, cuts[1:]):
             for t in range(PACK):
                 scatter(t, j0, j1)
@@ -237,7 +237,7 @@ def tile_list_apparent_power_margins_kernel(
             woven.append(weave(1, ms))
         quantise(z_w[1][:, chunks[-1]], z_s[1][:, chunks[-1]], woven[-1][:])
 
-        rotation = ("act", "rea", "sum", "act", "rea", "sum", "act", "rea")
+        rotation = ("act", "rea", "sum", "sum")
         for c, ms in enumerate(chunks):
             accs = [bank(rotation[(c * PACK + k) % len(rotation)], [P, BANK]) for k in range(N // P)]
             for b in range(2):
@@ -247,7 +247,7 @@ def tile_list_apparent_power_margins_kernel(
                                         rhs=z_w[b][:, ms].bitcast(FP8X4), rhs_scale=z_s[b][:, ms],
                                         start=(b == 0), stop=(b == 1))
             for k, acc in enumerate(accs):
-                res = slot("square", [P, BANK], F32, bufs=8)
+                res = slot("square", [P, BANK], F32, bufs=SQUARES)
                 copy = nc.vector.tensor_copy if c == len(chunks) - 1 and k % 2 == 0 else nc.scalar.copy
                 copy(out=res[:], in_=acc[:])
                 nc.sync.dma_start(out=out[k * P : (k + 1) * P, ms], in_=res[:])

@@ -23,9 +23,10 @@ PASS = P * PACK
 BANK = 512
 LIST_COL = 16
 PLANES = H // P
-PAGES = 6
+PAGES = 7
+ON_GPSIMD = 4
 BANKS = {"act": 2, "rea": 2, "sum": 4}
-SQUARES = 16
+SQUARES = 12
 
 
 def tile_list_apparent_power_margins_kernel(
@@ -71,7 +72,7 @@ def tile_list_apparent_power_margins_kernel(
         v_first = keep.tile([P, S // 2], U32, name="v_first", align_bytes=64)
         wp_w = [slot(tag, [P, PASS], U32) for tag in ("rating1", "words")]
         wp_s = [slot(f"scales{b}", [P, PASS], U8) for b in range(2)]
-        tab_w = slot("z1", [P, T], I32)
+        tab_w = slot("page5", [P, T], I32)
         under_root = slot("root", [P, 1], F32)
         squared_const = slot("wq_w", [P, 1], F32)
         tab_s = at("tab_s", 4 * S - T // 2, [P, T], U8)
@@ -91,10 +92,10 @@ def tile_list_apparent_power_margins_kernel(
         load_scales(nc.scalar, tab_s, tab_scales[0])
         nc.scalar.activation(out=under_root[:], in_=squared_const[:], func=ACT.Sqrt)
         nc.sync.dma_start(offs2_t[:], offs2)
-        load_scales(nc.scalar, wq_s, wq_scales[0])
+        load_scales(nc.gpsimd, wq_s, wq_scales[0])
         make_identity(nc, ident[:])
-        nc.vector.memset(pages[0][:].bitcast(I32), 0)
-        clear(pages[1])
+        for page in pages[:2]:
+            nc.vector.memset(page[:].bitcast(I32), 0)
         clear(pages[2])
         wq_w = slot("wq_w", [P, 2 * H], U8)
         nc.sync.dma_start(out=wq_w[:].bitcast(I32), in_=wq_words[0].bitcast(I32))
@@ -115,7 +116,7 @@ def tile_list_apparent_power_margins_kernel(
         v_w = (v_first, v_second)
         pages.append(slot("page3", [P, T2], F32))
         clear(pages[3])
-        grouped1 = slot("page5", [P, PASS, PACK], BF16)
+        grouped1 = slot("page6", [P, PASS, PACK], BF16)
         interleave(nc.vector.tensor_copy, grouped1[:], raw1[:])
         quantise(wp_w[1][:], wp_s[1][:], grouped1[:])
 
@@ -160,25 +161,39 @@ def tile_list_apparent_power_margins_kernel(
             cols = offs2_t[:, j0 // LIST_COL : j1 // LIST_COL]
             nc.vector.tensor_copy(out=pages[n % PAGES][:].indirect(cols), in_=h[b][:, t, j0:j1])
 
+        def apparent_power_by_planes(u0, squares):
+            b, j0 = divmod(u0 * P, S)
+            js = slice(j0, j0 + BANK)
+            for t in range(PACK):
+                total = bank("sum", [P, PACK, P])
+                for k in range(PACK):
+                    for n, sq in enumerate(squares[u0 + k]):
+                        nc.tensor.matmul(total[:, k, :], sq[:, t, :], ident[:], start=(n == 0), stop=(n == 1), is_transpose=True)
+                nc.scalar.activation(out=h[b][:, t, js], in_=total[:].rearrange("p k j -> p (k j)"), func=ACT.Sqrt, bias=under_root[:])
+                nc.gpsimd.tensor_tensor(h[b][:, t, js], h[b][:, t, js], wgs_t[:, js], MULT)
+
         units = 2 * S // P
         squares = {0: squared_powers(0, parts=PACK)}
         squares[1] = squared_powers(1)
         apparent_power(0, squares[0], parts=PACK)
-        for u in range(1, units):
-            for ahead in (2 * u - 1, 2 * u):
-                if 1 < ahead < units:
-                    squares[ahead] = squared_powers(ahead)
+        for u in range(1, PACK):
+            squares[u + 1] = squared_powers(u + 1)
             apparent_power(u, squares[u])
-        cuts = (0, 128, 256, 384, 512, 640, 768, 1024)
+        for u0 in range(PACK, units, PACK):
+            for u in range(u0 + 1, min(u0 + PACK + 1, units)):
+                squares[u] = squared_powers(u)
+            apparent_power_by_planes(u0, squares)
+        cuts = (0, 128, 256, 384, 512, 1024)
         for j0, j1 in zip(cuts, cuts[1:]):
             for t in range(PACK):
                 scatter(t, j0, j1)
-        for n in (4, 5):
+        for n in (4, 5, 6):
             pages.append(slot(f"page{n}", [P, T2], F32))
             clear(pages[n])
         for j0 in (0, S // 2):
             for n in (4, 5):
                 scatter(n, j0, j0 + S // 2)
+        scatter(6, 0, S)
 
         inv_root = slot("root", [P, T2], F32)
 
@@ -212,34 +227,42 @@ def tile_list_apparent_power_margins_kernel(
             engine.tensor_tensor(z[n // PACK][:, n % PACK, ms], pages[n % PAGES][:, ms], invs[pair][:, e, ms], MULT)
 
         def weave(b, ms):
-            grouped = slot("grouped", [P, BANK, PACK], BF16, bufs=3)
+            grouped = slot("grouped", [P, ms.stop - ms.start, PACK], BF16, bufs=3)
             interleave(nc.vector.tensor_copy, grouped[:], z[b][:, :, ms])
-            return grouped
+            return grouped[:]
 
         everything = slice(0, T2)
-        for n in range(PAGES):
-            divide(nc.gpsimd, n, everything)
-            if n + PAGES < PLANES:
-                scatter(n + PAGES, 0, S)
+        for n in range(ON_GPSIMD):
+            for ms in halves:
+                divide(nc.gpsimd, n, ms)
+            if n == 0:
+                scatter(PLANES - 1, 0, S)
             if n == 1:
                 invs.append(inverse_ratings(3))
-        woven = [weave(0, chunks[0])]
-        for c, ms in enumerate(chunks):
-            if c + 1 < len(chunks):
-                woven.append(weave(0, chunks[c + 1]))
-            quantise(z_w[0][:, ms], z_s[0][:, ms], woven[c][:])
-        woven = []
-        for c, ms in enumerate(chunks):
-            divide(nc.vector, 6, ms)
-            divide(nc.vector, 7, ms)
-            if c > 0:
-                quantise(z_w[1][:, chunks[c - 1]], z_s[1][:, chunks[c - 1]], woven[c - 1][:])
-            woven.append(weave(1, ms))
-        quantise(z_w[1][:, chunks[-1]], z_s[1][:, chunks[-1]], woven[-1][:])
+        late = slot("root", [P, 2, BANK, PACK], BF16)
+        divide(nc.vector, 4, everything)
+        woven0 = [weave(0, ms) for ms in chunks[:2]]
+        for n, ms in enumerate(chunks[2:]):
+            interleave(nc.scalar.copy, late[:, n], z[0][:, :, ms])
+            woven0.append(late[:, n])
+        for c in range(2):
+            quantise(z_w[0][:, chunks[c]], z_s[0][:, chunks[c]], woven0[c])
+        for n in (5, 6):
+            divide(nc.vector, n, everything)
+        pieces = chunks
+        divide(nc.vector, PLANES - 1, pieces[0])
+        for c, ms in enumerate(pieces):
+            woven = weave(1, ms)
+            if c + 1 < len(pieces):
+                divide(nc.vector, PLANES - 1, pieces[c + 1])
+            if c >= 2:
+                quantise(z_w[0][:, ms], z_s[0][:, ms], woven0[c])
+            quantise(z_w[1][:, ms], z_s[1][:, ms], woven)
 
         rotation = ("act", "rea", "sum", "sum")
-        for c, ms in enumerate(chunks):
-            accs = [bank(rotation[(c * PACK + k) % len(rotation)], [P, BANK]) for k in range(N // P)]
+        for c, ms in enumerate(pieces):
+            width = ms.stop - ms.start
+            accs = [bank(rotation[k], [P, width]) for k in range(N // P)]
             for b in range(2):
                 for k, acc in enumerate(accs):
                     ns = slice(k * P, (k + 1) * P)
@@ -247,7 +270,7 @@ def tile_list_apparent_power_margins_kernel(
                                         rhs=z_w[b][:, ms].bitcast(FP8X4), rhs_scale=z_s[b][:, ms],
                                         start=(b == 0), stop=(b == 1))
             for k, acc in enumerate(accs):
-                res = slot("square", [P, BANK], F32, bufs=SQUARES)
-                copy = nc.vector.tensor_copy if c == len(chunks) - 1 and k % 2 == 0 else nc.scalar.copy
+                res = slot("square", [P, width], F32, bufs=SQUARES)
+                copy = nc.vector.tensor_copy if c == len(pieces) - 1 and k % 2 == 0 else nc.scalar.copy
                 copy(out=res[:], in_=acc[:])
                 nc.sync.dma_start(out=out[k * P : (k + 1) * P, ms], in_=res[:])

@@ -22,11 +22,21 @@ PACK = 4
 PASS = P * PACK
 BANK = 512
 LIST_COL = 16
-PLANES = H // P
-PAGES = 7
-ON_GPSIMD = 4
+CHUNKS = T2 // BANK
+FIRST = 512
+SQUARES = 16
 BANKS = {"act": 2, "rea": 2, "sum": 4}
-SQUARES = 12
+SQUARED_ON_GPSIMD = ((0, 0),)
+
+KIB = 1024
+JOINED = (0, 32 * KIB)
+RATING = 64 * KIB
+POWER = (128 * KIB, 144 * KIB)
+PAGES = 160 * KIB
+ROOTS = 192 * KIB
+Z_FIRST = 208 * KIB
+V_REST = 222 * KIB
+WEIGHTS = 226 * KIB
 
 
 def tile_list_apparent_power_margins_kernel(
@@ -35,113 +45,138 @@ def tile_list_apparent_power_margins_kernel(
     nc = tc.nc
     with ExitStack() as ctx:
         keep = ctx.enter_context(tc.tile_pool(name="keep", bufs=1))
-        ring = ctx.enter_context(tc.tile_pool(name="ring", bufs=1))
         placed = ctx.enter_context(tc.tile_pool(name="placed", bufs=1))
         psum = ctx.enter_context(tc.psum_pool(name="psum", bufs=1))
+
+        def at(name, offset, shape, dtype, bufs=1):
+            return placed.tile(shape, dtype, name=name, tag=name, bufs=bufs, align_bytes=64, offset=offset)
+
+        def bank(tag, shape):
+            return psum.tile(shape, F32, name=tag, tag=tag, bufs=BANKS[tag])
 
         def load_scales(queue, dst, src_rows):
             for q in range(4):
                 queue.dma_start(out=dst[32 * q : 32 * q + 4, :].bitcast(I32), in_=src_rows[4 * q : 4 * q + 4, :].bitcast(I32))
 
-        def interleave(copy, dst, src):
-            copy(out=dst.rearrange("p (c i) t -> p c t i", i=4), in_=src.rearrange("p t (c i) -> p c t i", i=4))
+        def woven(grouped):
+            return grouped.rearrange("p (c i) t -> p c t i", i=4)
 
-        def slot(tag, shape, dtype, bufs=1):
-            return ring.tile(shape, dtype, name=tag, tag=tag, bufs=bufs, align_bytes=64)
-
-        def at(name, offset, shape, dtype):
-            return placed.tile(shape, dtype, name=name, tag=name, bufs=1, align_bytes=64, offset=offset)
-
-        def bank(tag, shape):
-            return psum.tile(shape, F32, name=tag, tag=tag, bufs=BANKS[tag])
+        def by_fours(planes):
+            return planes.rearrange("p t (c i) -> p c t i", i=4)
 
         def quantise(words, scales, grouped):
             nc.vector.quantize_mx(out=words.bitcast(FP8X4), scales=scales, in_=grouped.rearrange("p c t -> p (c t)"))
 
+        def rating_at(b, c):
+            return RATING + (b * CHUNKS + c) * 8 * KIB
+
         chunks = [slice(m0, m0 + BANK) for m0 in range(0, T2, BANK)]
-        halves = (slice(0, T2 // 2), slice(T2 // 2, T2))
 
         offs_t = keep.tile([P, S // LIST_COL], U16, name="offs_t")
         offs2_t = keep.tile([P, S // LIST_COL], U16, name="offs2_t")
         ident = keep.tile([P, P], F32, name="ident")
         wq_s = keep.tile([P, H], U8, name="wq_s", align_bytes=64)
-        v_s = keep.tile([P, S], U8, name="v_s", align_bytes=64)
-        z_w = [keep.tile([P, T2], U32, name=f"z_w{b}", align_bytes=64) for b in range(2)]
-        z_s = [keep.tile([P, T2], U8, name=f"z_s{b}", align_bytes=64) for b in range(2)]
+        v_w = keep.tile([P, S], U32, name="v_w", align_bytes=64)
+        wp_w = [at(f"wp_w{b}", WEIGHTS + b * 2 * KIB, [P, PASS], U32) for b in range(2)]
+        wp_s = [at(f"wp_s{b}", WEIGHTS + 4 * KIB + b * PASS, [P, PASS], U8) for b in range(2)]
+        pages = [at(f"page{t}", PAGES + t * 8 * KIB, [P, T2], F32) for t in range(PACK)]
+        tab_w = at("tab_w", ROOTS + KIB, [P, T], I32)
+        tab_s = at("tab_s", rating_at(0, 2), [P, T], U8)
+        squared_const = at("squared_const", JOINED[1] + 2 * KIB - 64, [P, 32], F32)
+        under_root = at("under_root", ROOTS, [P, 1], F32)
+
+        def wp_columns(cs):
+            return wp[:, cs].rearrange("(p t) c -> p t c", t=PACK)
+
+        def gather_scales(name, offset, j0, j1):
+            picked = at(name, offset, [P, j1 - j0], U8)
+            nc.vector.tensor_copy(out=picked[:], in_=tab_s[:].indirect(offs_t[:, j0 // LIST_COL : j1 // LIST_COL]))
+            return picked
+
         half = PASS // 2
-        v_first = keep.tile([P, S // 2], U32, name="v_first", align_bytes=64)
-        wp_w = [slot(tag, [P, PASS], U32) for tag in ("rating1", "words")]
-        wp_s = [slot(f"scales{b}", [P, PASS], U8) for b in range(2)]
-        tab_w = slot("page5", [P, T], I32)
-        under_root = slot("root", [P, 1], F32)
-        squared_const = slot("wq_w", [P, 1], F32)
-        tab_s = at("tab_s", 4 * S - T // 2, [P, T], U8)
-        pages = [keep.tile([P, T2], F32, name=f"page{n}") for n in range(3)]
-
-        def clear(page):
-            for ms in chunks:
-                nc.gpsimd.memset(page[:, ms].bitcast(I32), 0)
-
         nc.gpsimd.memset(tab_s[:].bitcast(I32), 0)
         nc.gpsimd.memset(wq_s[:].bitcast(I32), 0)
-        nc.vector.memset(squared_const[:], 1.0 / 64.0)
+        nc.vector.memset(squared_const[:, 0:1], 1.0 / 64.0)
         nc.sync.dma_start(offs_t[:], offs)
         nc.sync.dma_start(out=tab_w[:], in_=tab_words[0].rearrange("p n t -> p (n t)").bitcast(I32))
-        raw0 = slot("page4", [P, PACK, PASS], F32)
-        nc.sync.dma_start(out=raw0[:], in_=wp[:, 0:PASS].rearrange("(p t) c -> p t c", t=PACK))
+        raw0 = [at(f"raw0{n}", rating_at(0, n), [P, PACK, half], F32) for n in range(2)]
+        for n in range(2):
+            nc.sync.dma_start(out=raw0[n][:], in_=wp_columns(slice(n * half, (n + 1) * half)))
         load_scales(nc.scalar, tab_s, tab_scales[0])
-        nc.scalar.activation(out=under_root[:], in_=squared_const[:], func=ACT.Sqrt)
         nc.sync.dma_start(offs2_t[:], offs2)
+        nc.scalar.activation(out=under_root[:], in_=squared_const[:, 0:1], func=ACT.Sqrt)
         load_scales(nc.gpsimd, wq_s, wq_scales[0])
         make_identity(nc, ident[:])
+        wq_w = at("wq_w", JOINED[1], [P, 2 * H], U8)
+        later = at("later", JOINED[1] + 2 * KIB, [P, PACK * PASS + S], F32)
+        raw1 = later[:, 0 : PACK * PASS].rearrange("p (t c) -> p t c", t=PACK)
+        wgs_t = later[:, PACK * PASS :]
+        nc.sync.dma_start(out=wq_w[:].bitcast(I32), in_=wq_words[0].bitcast(I32))
+        nc.sync.dma_start(out=raw1, in_=wp_columns(slice(PASS, H)))
+        nc.sync.dma_start(out=wgs_t, in_=wgs)
         for page in pages[:2]:
             nc.vector.memset(page[:].bitcast(I32), 0)
-        clear(pages[2])
-        wq_w = slot("wq_w", [P, 2 * H], U8)
-        nc.sync.dma_start(out=wq_w[:].bitcast(I32), in_=wq_words[0].bitcast(I32))
-        nc.vector.tensor_copy(out=v_s[:], in_=tab_s[:].indirect(offs_t[:]))
-        raw1 = at("raw1", 4 * S, [P, PACK, PASS], F32)
-        nc.sync.dma_start(out=raw1[:], in_=wp[:, PASS:H].rearrange("(p t) c -> p t c", t=PACK))
-        wgs_t = at("wgs_t", 0, [P, S], F32)
-        nc.sync.dma_start(out=wgs_t[:], in_=wgs)
-        nc.vector.tensor_copy(out=v_first[:], in_=tab_w[:].bitcast(U32).indirect(offs_t[:, 0 : S // 2 // LIST_COL]))
-        grouped0 = [slot(tag, [P, half, PACK], BF16) for tag in ("page3", "rating2")]
-        interleave(nc.scalar.copy, grouped0[0][:], raw0[:, :, 0:half])
-        interleave(nc.vector.tensor_copy, grouped0[1][:], raw0[:, :, half:PASS])
-        for n in (1, 0):
+        for page in pages[2:]:
+            for ms in chunks:
+                nc.gpsimd.memset(page[:, ms].bitcast(I32), 0)
+        nc.vector.tensor_copy(out=v_w[:], in_=tab_w[:].bitcast(U32).indirect(offs_t[:]))
+        v_s = [gather_scales("v_s_first", ROOTS + KIB, 0, FIRST)]
+        for n in range(2):
+            grouped = at(f"grouped_wp0{n}", V_REST + n * 2 * KIB, [P, half, PACK], BF16)
+            nc.scalar.copy(out=woven(grouped[:]), in_=by_fours(raw0[n][:]))
             cs = slice(n * half, (n + 1) * half)
-            quantise(wp_w[0][:, cs], wp_s[0][:, cs], grouped0[n][:])
-        v_second = slot("rating2", [P, S // 2], U32)
-        nc.vector.tensor_copy(out=v_second[:], in_=tab_w[:].bitcast(U32).indirect(offs_t[:, S // 2 // LIST_COL : S // LIST_COL]))
-        v_w = (v_first, v_second)
-        pages.append(slot("page3", [P, T2], F32))
-        clear(pages[3])
-        grouped1 = slot("page6", [P, PASS, PACK], BF16)
-        interleave(nc.vector.tensor_copy, grouped1[:], raw1[:])
-        quantise(wp_w[1][:], wp_s[1][:], grouped1[:])
+            quantise(wp_w[0][:, cs], wp_s[0][:, cs], grouped[:])
+        v_s.append(gather_scales("v_s_rest", V_REST + 2 * KIB, FIRST, S))
+        grouped_wp1 = at("grouped_wp1", rating_at(0, 3), [P, PASS, PACK], BF16)
+        nc.vector.tensor_copy(out=woven(grouped_wp1[:]), in_=by_fours(raw1))
+        quantise(wp_w[1][:], wp_s[1][:], grouped_wp1[:])
 
-        h = [slot(f"h{b}", [P, PACK, S], F32) for b in range(2)]
+        inverse = {}
+
+        def load_ratings(b):
+            tile = at(f"rating{b}", rating_at(b, 0), [P, CHUNKS, PACK, BANK], F32)
+            for c, ms in enumerate(chunks):
+                inverse[b, c] = tile[:, c]
+                rows = rating[b * PASS : (b + 1) * PASS, ms]
+                nc.sync.dma_start(out=inverse[b, c], in_=rows.rearrange("(p t) m -> p t m", t=PACK))
+
+        h = [at(f"h{b}", POWER[b], [P, PACK, S], F32) for b in range(2)]
+        joined = [at(f"joined{b}", JOINED[b], [P, PACK, T2], F32) for b in range(2)]
 
         def squared_powers(u, parts=1):
             b, j0 = divmod(u * P, S)
-            js = slice(j0, j0 + P)
-            words = v_w[2 * j0 // S][:, j0 % (S // 2) : j0 % (S // 2) + P].bitcast(FP8X4)
+            piece = min(j0 // FIRST, 1)
+            js = slice(j0 - piece * FIRST, j0 - piece * FIRST + P)
+            words, scales = v_w[:, j0 : j0 + P].bitcast(FP8X4), v_s[piece][:, js]
+            act = bank("act", [P, BANK])
+            nc.tensor.matmul_mx(out=act[:], lhsT=words, lhsT_scale=scales,
+                                rhs=wp_w[b][:].bitcast(FP8X4), rhs_scale=wp_s[b][:], start=True, stop=True)
             rea = bank("rea", [P, BANK])
-            nc.tensor.matmul_mx(out=rea[:], lhsT=words, lhsT_scale=v_s[:, js],
+            nc.tensor.matmul_mx(out=rea[:], lhsT=words, lhsT_scale=scales,
                                 rhs=wq_w[:, 2 * b * PASS : 2 * (b + 1) * PASS].bitcast(FP4X4),
                                 rhs_scale=wq_s[:, b * PASS : (b + 1) * PASS], start=True, stop=True)
-            act = bank("act", [P, BANK])
-            nc.tensor.matmul_mx(out=act[:], lhsT=words, lhsT_scale=v_s[:, js],
-                                rhs=wp_w[b][:].bitcast(FP8X4), rhs_scale=wp_s[b][:], start=True, stop=True)
             squares = []
-            for power, pieces in ((rea, 1), (act, parts)):
-                sq = slot("square", [P, PACK, P], F32, bufs=SQUARES)
+            for power, pieces in ((act, 1), (rea, parts)):
+                sq = at("square", rating_at(1, 0), [P, PACK, P], F32, bufs=SQUARES)
                 planes = PACK // pieces
                 for t0 in range(0, PACK, planes):
                     ts = slice(t0, t0 + planes)
                     nc.scalar.activation(out=sq[:, ts, :], in_=power[:].rearrange("j (p t) -> j t p", t=PACK)[:, ts, :], func=ACT.Square)
                 squares.append(sq)
             return squares
+
+        def weigh(b, ts, js):
+            planes = ts.stop - ts.start
+            weights = wgs_t[:, js].unsqueeze(1).to_broadcast([P, planes, js.stop - js.start])
+            nc.gpsimd.tensor_tensor(h[b][:, ts, js], h[b][:, ts, js], weights, MULT)
+
+        def scatter(b, t, j0, j1):
+            cols = offs2_t[:, j0 // LIST_COL : j1 // LIST_COL]
+            nc.vector.tensor_copy(out=pages[t][:].indirect(cols), in_=h[b][:, t, j0:j1])
+
+        def join(b, t, pieces):
+            for ms in pieces:
+                nc.sync.dma_start(out=joined[b][:, t, ms], in_=pages[t][:, ms])
 
         def apparent_power(u, squares, parts=1):
             b, j0 = divmod(u * P, S)
@@ -154,123 +189,103 @@ def tile_list_apparent_power_margins_kernel(
                     for n, sq in enumerate(squares):
                         nc.tensor.matmul(total[:, t, :], sq[:, t0 + t, :], ident[:], start=(n == 0), stop=(n == 1), is_transpose=True)
                 nc.scalar.activation(out=h[b][:, ts, js], in_=total[:], func=ACT.Sqrt, bias=under_root[:])
-                nc.gpsimd.tensor_tensor(h[b][:, ts, js], h[b][:, ts, js], wgs_t[:, js].unsqueeze(1).to_broadcast([P, planes, P]), MULT)
+                if u < PACK:
+                    weigh(b, ts, js)
+            if u < PACK:
+                for t in range(PACK):
+                    scatter(b, t, j0, j0 + P)
+            elif u % PACK == PACK - 1:
+                for t in range(PACK):
+                    weigh(b, slice(t, t + 1), slice(j0 + P - BANK, j0 + P))
 
-        def scatter(n, j0, j1):
-            b, t = divmod(n, PACK)
-            cols = offs2_t[:, j0 // LIST_COL : j1 // LIST_COL]
-            nc.vector.tensor_copy(out=pages[n % PAGES][:].indirect(cols), in_=h[b][:, t, j0:j1])
-
-        def apparent_power_by_planes(u0, squares):
-            b, j0 = divmod(u0 * P, S)
-            js = slice(j0, j0 + BANK)
-            for t in range(PACK):
-                total = bank("sum", [P, PACK, P])
-                for k in range(PACK):
-                    for n, sq in enumerate(squares[u0 + k]):
-                        nc.tensor.matmul(total[:, k, :], sq[:, t, :], ident[:], start=(n == 0), stop=(n == 1), is_transpose=True)
-                nc.scalar.activation(out=h[b][:, t, js], in_=total[:].rearrange("p k j -> p (k j)"), func=ACT.Sqrt, bias=under_root[:])
-                nc.gpsimd.tensor_tensor(h[b][:, t, js], h[b][:, t, js], wgs_t[:, js], MULT)
-
+        everything = [slice(0, T2)]
         units = 2 * S // P
-        squares = {0: squared_powers(0, parts=PACK)}
-        squares[1] = squared_powers(1)
-        apparent_power(0, squares[0], parts=PACK)
-        for u in range(1, PACK):
-            squares[u + 1] = squared_powers(u + 1)
-            apparent_power(u, squares[u])
-        for u0 in range(PACK, units, PACK):
-            for u in range(u0 + 1, min(u0 + PACK + 1, units)):
-                squares[u] = squared_powers(u)
-            apparent_power_by_planes(u0, squares)
-        cuts = (0, 128, 256, 384, 512, 1024)
-        for j0, j1 in zip(cuts, cuts[1:]):
-            for t in range(PACK):
-                scatter(t, j0, j1)
-        for n in (4, 5, 6):
-            pages.append(slot(f"page{n}", [P, T2], F32))
-            clear(pages[n])
-        for j0 in (0, S // 2):
-            for n in (4, 5):
-                scatter(n, j0, j0 + S // 2)
-        scatter(6, 0, S)
-
-        inv_root = slot("root", [P, T2], F32)
-
-        def inverse_ratings(pair):
-            inv = at(f"rating{pair}", 4 * S, [P, 2, T2], F32) if pair % 3 == 0 else slot(f"rating{pair}", [P, 2, T2], F32)
-            b, t0 = divmod(2 * pair, PACK)
-            nc.sync.dma_start(out=inv[:], in_=rating[b * PASS : (b + 1) * PASS, :].rearrange("(p t) m -> p t m", t=PACK)[:, t0 : t0 + 2, :])
-            if pair < 3:
-                steps = [[(e, ms, ms) for ms in halves] for e in range(2)]
-            else:
-                steps = [[(e, ms, chunks[(2 * c + e) % len(chunks)]) for e in range(2)] for c, ms in enumerate(chunks)]
-            for step in steps:
-                for e, ms, tmp in step:
-                    nc.scalar.activation(out=inv_root[:, tmp], in_=inv[:, e, ms], func=ACT.Abs_reciprocal_sqrt)
-                for e, ms, tmp in step:
-                    nc.scalar.activation(out=inv[:, e, ms], in_=inv_root[:, tmp], func=ACT.Square)
-            return inv
-
-        invs = [inverse_ratings(pair) for pair in range(3)]
-        wm_w = slot("words", [P, 2, N], I32)
-        wm_s = slot("scales0", [P, N], U8)
+        squares = squared_powers(0, parts=PACK)
+        for u in range(units):
+            ahead = squared_powers(u + 1) if u + 1 < units else None
+            apparent_power(u, squares, parts=PACK if u == 0 else 1)
+            squares = ahead
+            if u == 1:
+                load_ratings(0)
+            if u == 7:
+                for t in range(PACK):
+                    scatter(0, t, S // 2, S)
+                    join(0, t, everything)
+            if u == 11:
+                for t in range(2):
+                    scatter(1, t, 0, S // 2)
+        load_ratings(1)
+        wm_w = at("wm_w", WEIGHTS, [P, 2, N], I32)
+        wm_s = at("wm_s", WEIGHTS + 4 * KIB, [P, N], U8)
         nc.sync.dma_start(out=wm_w[:], in_=wm_words.rearrange("a p n t -> p a (n t)").bitcast(I32))
         nc.gpsimd.memset(wm_s[:].bitcast(I32), 0)
         for q in range(4):
             nc.sync.dma_start(out=wm_s[32 * q : 32 * q + 8, :].bitcast(I32), in_=wm_scales[:, 4 * q : 4 * q + 4, :].bitcast(I32))
+        for t in range(PACK):
+            scatter(1, t, S // 2 if t < 2 else 0, S)
+            join(1, t, everything if t < PACK - 1 else chunks)
 
-        z = [slot(tag, [P, PACK, T2], BF16) for tag in ("h0", "z1")]
+        roots = at("roots", ROOTS, [P, 2, T2], F32)
 
-        def divide(engine, n, ms):
-            pair, e = divmod(n, 2)
-            engine.tensor_tensor(z[n // PACK][:, n % PACK, ms], pages[n % PAGES][:, ms], invs[pair][:, e, ms], MULT)
+        def invert(b, c):
+            flat = inverse[b, c].rearrange("p t m -> p (t m)")
+            if (b, c) in SQUARED_ON_GPSIMD:
+                nc.scalar.activation(out=roots[:, 1, :], in_=flat, func=ACT.Abs_reciprocal_sqrt)
+                nc.gpsimd.tensor_tensor(flat, roots[:, 1, :], roots[:, 1, :], MULT)
+            else:
+                halves = (slice(0, T2 // 2), slice(T2 // 2, T2))
+                for ms in halves:
+                    nc.scalar.activation(out=roots[:, 0, ms], in_=flat[:, ms], func=ACT.Abs_reciprocal_sqrt)
+                for ms in halves:
+                    nc.scalar.activation(out=flat[:, ms], in_=roots[:, 0, ms], func=ACT.Square)
 
-        def weave(b, ms):
-            grouped = slot("grouped", [P, ms.stop - ms.start, PACK], BF16, bufs=3)
-            interleave(nc.vector.tensor_copy, grouped[:], z[b][:, :, ms])
-            return grouped[:]
+        def divide(engine, b, c):
+            grouped = at(f"grouped{b}", POWER[b], [P, BANK, PACK], BF16, bufs=CHUNKS)
+            engine.tensor_tensor(woven(grouped[:]), by_fours(joined[b][:, :, chunks[c]]), by_fours(inverse[b, c]), MULT)
+            return grouped
 
-        everything = slice(0, T2)
-        for n in range(ON_GPSIMD):
-            for ms in halves:
-                divide(nc.gpsimd, n, ms)
-            if n == 0:
-                scatter(PLANES - 1, 0, S)
-            if n == 1:
-                invs.append(inverse_ratings(3))
-        late = slot("root", [P, 2, BANK, PACK], BF16)
-        divide(nc.vector, 4, everything)
-        woven0 = [weave(0, ms) for ms in chunks[:2]]
-        for n, ms in enumerate(chunks[2:]):
-            interleave(nc.scalar.copy, late[:, n], z[0][:, :, ms])
-            woven0.append(late[:, n])
-        for c in range(2):
-            quantise(z_w[0][:, chunks[c]], z_s[0][:, chunks[c]], woven0[c])
-        for n in (5, 6):
-            divide(nc.vector, n, everything)
-        pieces = chunks
-        divide(nc.vector, PLANES - 1, pieces[0])
-        for c, ms in enumerate(pieces):
-            woven = weave(1, ms)
-            if c + 1 < len(pieces):
-                divide(nc.vector, PLANES - 1, pieces[c + 1])
-            if c >= 2:
-                quantise(z_w[0][:, ms], z_s[0][:, ms], woven0[c])
-            quantise(z_w[1][:, ms], z_s[1][:, ms], woven)
+        z_at = (Z_FIRST, JOINED[0])
+        z_w, z_s = {}, {}
+
+        def quantise_z(b, c, grouped):
+            z_w[b, c] = at(f"z_w{b}{c}", z_at[b] + c * 2 * KIB, [P, BANK], U32)
+            z_s[b, c] = at(f"z_s{b}{c}", z_at[b] + 8 * KIB + c * BANK, [P, BANK], U8)
+            quantise(z_w[b, c][:], z_s[b, c][:], grouped[:])
+
+        for c in range(CHUNKS):
+            invert(0, c)
+            quantise_z(0, c, divide(nc.gpsimd, 0, c))
+        for c in range(CHUNKS):
+            invert(1, c)
+        ahead = divide(nc.vector, 1, 0)
+        for c in range(CHUNKS):
+            grouped = ahead
+            if c + 1 < CHUNKS and c > 0:
+                ahead = divide(nc.vector, 1, c + 1)
+            quantise_z(1, c, grouped)
+            if c == 0:
+                ahead = divide(nc.vector, 1, 1)
 
         rotation = ("act", "rea", "sum", "sum")
-        for c, ms in enumerate(pieces):
-            width = ms.stop - ms.start
-            accs = [bank(rotation[k], [P, width]) for k in range(N // P)]
-            for b in range(2):
-                for k, acc in enumerate(accs):
-                    ns = slice(k * P, (k + 1) * P)
-                    nc.tensor.matmul_mx(out=acc[:], lhsT=wm_w[:, b, ns].bitcast(FP8X4), lhsT_scale=wm_s[4 * b : P, ns],
-                                        rhs=z_w[b][:, ms].bitcast(FP8X4), rhs_scale=z_s[b][:, ms],
-                                        start=(b == 0), stop=(b == 1))
-            for k, acc in enumerate(accs):
-                res = slot("square", [P, width], F32, bufs=SQUARES)
-                copy = nc.vector.tensor_copy if c == len(pieces) - 1 and k % 2 == 0 else nc.scalar.copy
+        accs = {}
+
+        def margins(b, c):
+            if b == 0:
+                accs[c] = [bank(rotation[k], [P, BANK]) for k in range(N // P)]
+            for k, acc in enumerate(accs[c]):
+                ns = slice(k * P, (k + 1) * P)
+                nc.tensor.matmul_mx(out=acc[:], lhsT=wm_w[:, b, ns].bitcast(FP8X4), lhsT_scale=wm_s[4 * b : P, ns],
+                                    rhs=z_w[b, c][:].bitcast(FP8X4), rhs_scale=z_s[b, c][:],
+                                    start=(b == 0), stop=(b == 1))
+
+        margins(0, 0)
+        margins(0, 1)
+        for c in range(CHUNKS):
+            if c >= 2:
+                margins(0, c)
+            margins(1, c)
+            for k, acc in enumerate(accs[c]):
+                res = at(f"result{c // 2}", (ROOTS, rating_at(0, 0))[c // 2], [P, BANK], F32, bufs=8)
+                copy = nc.vector.tensor_copy if c == CHUNKS - 1 and k % 2 == 0 else nc.scalar.copy
                 copy(out=res[:], in_=acc[:])
-                nc.sync.dma_start(out=out[k * P : (k + 1) * P, ms], in_=res[:])
+                nc.sync.dma_start(out=out[k * P : (k + 1) * P, chunks[c]], in_=res[:])

@@ -26,7 +26,8 @@ CHUNKS = T2 // BANK
 FIRST = 512
 SQUARES = 16
 BANKS = {"act": 2, "rea": 2, "sum": 4}
-SQUARED_ON_GPSIMD = ((0, 0),)
+
+RUNS = (4, 4)
 
 KIB = 1024
 JOINED = (0, 32 * KIB)
@@ -58,11 +59,11 @@ def tile_list_apparent_power_margins_kernel(
             for q in range(4):
                 queue.dma_start(out=dst[32 * q : 32 * q + 4, :].bitcast(I32), in_=src_rows[4 * q : 4 * q + 4, :].bitcast(I32))
 
-        def woven(grouped):
-            return grouped.rearrange("p (c i) t -> p c t i", i=4)
+        def woven(grouped, run=4):
+            return grouped.rearrange("p (c i) t -> p c t i", i=run)
 
-        def by_fours(planes):
-            return planes.rearrange("p t (c i) -> p c t i", i=4)
+        def by_fours(planes, run=4):
+            return planes.rearrange("p t (c i) -> p c t i", i=run)
 
         def quantise(words, scales, grouped):
             nc.vector.quantize_mx(out=words.bitcast(FP8X4), scales=scales, in_=grouped.rearrange("p c t -> p (c t)"))
@@ -225,25 +226,24 @@ def tile_list_apparent_power_margins_kernel(
             scatter(1, t, S // 2 if t < 2 else 0, S)
             join(1, t, everything if t < PACK - 1 else chunks)
 
-        roots = at("roots", ROOTS, [P, 2, T2], F32)
+        roots = at("roots", ROOTS, [P, 2, PACK, BANK // 2], F32)
+        halves = (slice(0, BANK // 2), slice(BANK // 2, BANK))
 
         def invert(b, c):
-            flat = inverse[b, c].rearrange("p t m -> p (t m)")
-            if (b, c) in SQUARED_ON_GPSIMD:
-                nc.scalar.activation(out=roots[:, 1, :], in_=flat, func=ACT.Abs_reciprocal_sqrt)
-                nc.gpsimd.tensor_tensor(flat, roots[:, 1, :], roots[:, 1, :], MULT)
-            else:
-                halves = (slice(0, T2 // 2), slice(T2 // 2, T2))
-                for ms in halves:
-                    nc.scalar.activation(out=roots[:, 0, ms], in_=flat[:, ms], func=ACT.Abs_reciprocal_sqrt)
-                for ms in halves:
-                    nc.scalar.activation(out=flat[:, ms], in_=roots[:, 0, ms], func=ACT.Square)
+            for n, ms in enumerate(halves):
+                nc.scalar.activation(out=roots[:, n], in_=inverse[b, c][:, :, ms], func=ACT.Abs_reciprocal_sqrt)
+            for n, ms in enumerate(halves):
+                nc.scalar.activation(out=inverse[b, c][:, :, ms], in_=roots[:, n], func=ACT.Square)
 
-        def divide(engine, b, c):
+        def divide(engine, b, c, pieces):
             grouped = at(f"grouped{b}", POWER[b], [P, BANK, PACK], BF16, bufs=CHUNKS)
-            engine.tensor_tensor(woven(grouped[:]), by_fours(joined[b][:, :, chunks[c]]), by_fours(inverse[b, c]), MULT)
+            for ms in pieces:
+                placed_powers = joined[b][:, :, chunks[c]][:, :, ms]
+                run = RUNS[b]
+                engine.tensor_tensor(woven(grouped[:, ms, :], run), by_fours(placed_powers, run), by_fours(inverse[b, c][:, :, ms], run), MULT)
             return grouped
 
+        whole = (slice(0, BANK),)
         z_at = (Z_FIRST, JOINED[0])
         z_w, z_s = {}, {}
 
@@ -254,17 +254,17 @@ def tile_list_apparent_power_margins_kernel(
 
         for c in range(CHUNKS):
             invert(0, c)
-            quantise_z(0, c, divide(nc.gpsimd, 0, c))
+            quantise_z(0, c, divide(nc.gpsimd, 0, c, halves))
         for c in range(CHUNKS):
             invert(1, c)
-        ahead = divide(nc.vector, 1, 0)
+        ahead = divide(nc.vector, 1, 0, whole)
         for c in range(CHUNKS):
             grouped = ahead
             if c + 1 < CHUNKS and c > 0:
-                ahead = divide(nc.vector, 1, c + 1)
+                ahead = divide(nc.vector, 1, c + 1, whole)
             quantise_z(1, c, grouped)
             if c == 0:
-                ahead = divide(nc.vector, 1, 1)
+                ahead = divide(nc.vector, 1, 1, whole)
 
         rotation = ("act", "rea", "sum", "sum")
         accs = {}

@@ -157,13 +157,13 @@ def tile_list_apparent_power_margins_kernel(
                                 rhs=wq_w[:, 2 * b * PASS : 2 * (b + 1) * PASS].bitcast(FP4X4),
                                 rhs_scale=wq_s[:, b * PASS : (b + 1) * PASS], start=True, stop=True)
             squares = []
-            for power, pieces in ((act, 1), (rea, parts)):
-                sq = at("square", rating_at(1, 0), [P, PACK, P], F32, bufs=SQUARES)
-                planes = PACK // pieces
-                for t0 in range(0, PACK, planes):
-                    ts = slice(t0, t0 + planes)
+            for power in (rea, act):
+                squares.append(at("square", rating_at(1, 0), [P, PACK, P], F32, bufs=SQUARES))
+            planes = PACK // parts
+            for t0 in range(0, PACK, planes):
+                ts = slice(t0, t0 + planes)
+                for power, sq in zip((rea, act), squares):
                     nc.scalar.activation(out=sq[:, ts, :], in_=power[:].rearrange("j (p t) -> j t p", t=PACK)[:, ts, :], func=ACT.Square)
-                squares.append(sq)
             return squares
 
         def weigh(b, ts, js):
@@ -190,31 +190,44 @@ def tile_list_apparent_power_margins_kernel(
                     for n, sq in enumerate(squares):
                         nc.tensor.matmul(total[:, t, :], sq[:, t0 + t, :], ident[:], start=(n == 0), stop=(n == 1), is_transpose=True)
                 nc.scalar.activation(out=h[b][:, ts, js], in_=total[:], func=ACT.Sqrt, bias=under_root[:])
-                if u < PACK:
+                if u < 2:
                     weigh(b, ts, js)
-            if u < PACK:
-                for t in range(PACK):
-                    scatter(b, t, j0, j0 + P)
-            elif u % PACK == PACK - 1:
-                for t in range(PACK):
-                    weigh(b, slice(t, t + 1), slice(j0 + P - BANK, j0 + P))
+
+        def place(b, planes, j0, j1):
+            for t in planes:
+                scatter(b, t, j0, j1)
 
         everything = [slice(0, T2)]
         units = 2 * S // P
-        squares = squared_powers(0, parts=PACK)
-        for u in range(units):
-            ahead = squared_powers(u + 1) if u + 1 < units else None
-            apparent_power(u, squares, parts=PACK if u == 0 else 1)
-            squares = ahead
-            if u == 1:
-                load_ratings(0)
-            if u == 7:
-                for t in range(PACK):
-                    scatter(0, t, S // 2, S)
-                    join(0, t, everything)
-            if u == 11:
-                for t in range(2):
-                    scatter(1, t, 0, S // 2)
+        all_planes = range(PACK)
+        squares = {0: squared_powers(0, parts=2), 1: squared_powers(1)}
+        apparent_power(0, squares[0], parts=PACK)
+        place(0, all_planes, 0, P)
+        squares[2], squares[3] = squared_powers(2), squared_powers(3)
+        apparent_power(1, squares[1])
+        place(0, all_planes, P, 2 * P)
+        load_ratings(0)
+        for u in range(2, units, 2):
+            for ahead in range(u + 2, min(u + 4, units)):
+                squares[ahead] = squared_powers(ahead)
+            for done in (u, u + 1):
+                apparent_power(done, squares[done])
+            b, j0 = divmod(u * P, S)
+            for t0 in (0, 2):
+                weigh(b, slice(t0, t0 + 2), slice(j0, j0 + 2 * P))
+            if b == 0:
+                last = PACK - 1
+                for t in all_planes:
+                    if t < last or j0 < S // 2:
+                        scatter(0, t, j0, j0 + 2 * P)
+                    elif j0 > S // 2:
+                        scatter(0, t, S // 2, S)
+                    if j0 + 2 * P == S:
+                        join(0, t, everything if t < last else chunks)
+            elif j0 < S // 2:
+                place(1, (0, 1), j0, j0 + 2 * P)
+                if j0 > 0:
+                    scatter(1, 2, 0, S // 2)
         load_ratings(1)
         wm_w = at("wm_w", WEIGHTS, [P, 2, N], I32)
         wm_s = at("wm_s", WEIGHTS + 4 * KIB, [P, N], U8)
@@ -223,7 +236,7 @@ def tile_list_apparent_power_margins_kernel(
         for q in range(4):
             nc.sync.dma_start(out=wm_s[32 * q : 32 * q + 8, :].bitcast(I32), in_=wm_scales[:, 4 * q : 4 * q + 4, :].bitcast(I32))
         for t in range(PACK):
-            scatter(1, t, S // 2 if t < 2 else 0, S)
+            scatter(1, t, S // 2 if t < PACK - 1 else 0, S)
             join(1, t, everything if t < PACK - 1 else chunks)
 
         roots = at("roots", ROOTS, [P, 2, PACK, BANK // 2], F32)

@@ -23,11 +23,13 @@ PASS = P * PACK
 BANK = 512
 LIST_COL = 16
 CHUNKS = T2 // BANK
-FIRST = 512
+FIRST = 256
 SQUARES = 16
 BANKS = {"act": 2, "rea": 2, "sum": 4}
 
 RUNS = (4, 4)
+
+PAIRED = 2
 
 KIB = 1024
 JOINED = (0, 32 * KIB)
@@ -55,8 +57,8 @@ def tile_list_apparent_power_margins_kernel(
         def bank(tag, shape):
             return psum.tile(shape, F32, name=tag, tag=tag, bufs=BANKS[tag])
 
-        def load_scales(queue, dst, src_rows):
-            for q in range(4):
+        def load_scales(queues, dst, src_rows):
+            for q, queue in enumerate(queues):
                 queue.dma_start(out=dst[32 * q : 32 * q + 4, :].bitcast(I32), in_=src_rows[4 * q : 4 * q + 4, :].bitcast(I32))
 
         def woven(grouped, run=4):
@@ -99,25 +101,26 @@ def tile_list_apparent_power_margins_kernel(
         nc.gpsimd.memset(wq_s[:].bitcast(I32), 0)
         nc.vector.memset(squared_const[:, 0:1], 1.0 / 64.0)
         nc.sync.dma_start(offs_t[:], offs)
+        nc.sync.dma_start(offs2_t[:], offs2)
         nc.sync.dma_start(out=tab_w[:], in_=tab_words[0].rearrange("p n t -> p (n t)").bitcast(I32))
         raw0 = [at(f"raw0{n}", rating_at(0, n), [P, PACK, half], F32) for n in range(2)]
         for n in range(2):
             nc.sync.dma_start(out=raw0[n][:], in_=wp_columns(slice(n * half, (n + 1) * half)))
-        load_scales(nc.scalar, tab_s, tab_scales[0])
-        nc.sync.dma_start(offs2_t[:], offs2)
+        load_scales([nc.scalar] * 4, tab_s, tab_scales[0])
         nc.scalar.activation(out=under_root[:], in_=squared_const[:, 0:1], func=ACT.Sqrt)
-        load_scales(nc.gpsimd, wq_s, wq_scales[0])
+        load_scales([nc.gpsimd, nc.gpsimd, nc.sync, nc.sync], wq_s, wq_scales[0])
         make_identity(nc, ident[:])
         wq_w = at("wq_w", JOINED[1], [P, 2 * H], U8)
         later = at("later", JOINED[1] + 2 * KIB, [P, PACK * PASS + S], F32)
         raw1 = later[:, 0 : PACK * PASS].rearrange("p (t c) -> p t c", t=PACK)
         wgs_t = later[:, PACK * PASS :]
         nc.sync.dma_start(out=wq_w[:].bitcast(I32), in_=wq_words[0].bitcast(I32))
+        nc.sync.dma_start(out=wgs_t[:, 0:FIRST], in_=wgs[:, 0:FIRST])
         nc.sync.dma_start(out=raw1, in_=wp_columns(slice(PASS, H)))
-        nc.sync.dma_start(out=wgs_t, in_=wgs)
-        for page in pages[:2]:
+        nc.sync.dma_start(out=wgs_t[:, FIRST:S], in_=wgs[:, FIRST:S])
+        for page in pages[:1]:
             nc.vector.memset(page[:].bitcast(I32), 0)
-        for page in pages[2:]:
+        for page in pages[1:]:
             for ms in chunks:
                 nc.gpsimd.memset(page[:, ms].bitcast(I32), 0)
         nc.vector.tensor_copy(out=v_w[:], in_=tab_w[:].bitcast(U32).indirect(offs_t[:]))
@@ -200,7 +203,7 @@ def tile_list_apparent_power_margins_kernel(
         everything = [slice(0, T2)]
         units = 2 * S // P
         all_planes = range(PACK)
-        squares = {0: squared_powers(0, parts=2), 1: squared_powers(1)}
+        squares = {0: squared_powers(0, parts=PACK), 1: squared_powers(1)}
         apparent_power(0, squares[0], parts=PACK)
         place(0, all_planes, 0, P)
         squares[2], squares[3] = squared_powers(2), squared_powers(3)
@@ -239,14 +242,28 @@ def tile_list_apparent_power_margins_kernel(
             scatter(1, t, S // 2 if t < PACK - 1 else 0, S)
             join(1, t, everything if t < PACK - 1 else chunks)
 
-        roots = at("roots", ROOTS, [P, 2, PACK, BANK // 2], F32)
+        roots = at("roots", ROOTS, [P, 2, T2 // 2], F32)
         halves = (slice(0, BANK // 2), slice(BANK // 2, BANK))
 
-        def invert(b, c):
-            for n, ms in enumerate(halves):
-                nc.scalar.activation(out=roots[:, n], in_=inverse[b, c][:, :, ms], func=ACT.Abs_reciprocal_sqrt)
-            for n, ms in enumerate(halves):
-                nc.scalar.activation(out=inverse[b, c][:, :, ms], in_=roots[:, n], func=ACT.Square)
+        def invert(*parts):
+            views = [roots[:, n].rearrange("p (t m) -> p t m", t=part.shape[1]) for n, part in enumerate(parts)]
+            for part, root in zip(parts, views):
+                nc.scalar.activation(out=root, in_=part, func=ACT.Abs_reciprocal_sqrt)
+            for part, root in zip(parts, views):
+                nc.scalar.activation(out=part, in_=root, func=ACT.Square)
+
+        def invert_chunk(b, c):
+            invert(*(inverse[b, c][:, :, ms] for ms in halves))
+
+        def divide_pair(engine, pairs, c, u):
+            ts = slice(2 * u, 2 * u + 2)
+            engine.tensor_tensor(woven(pairs[:, u]), by_fours(joined[1][:, ts, chunks[c]]), by_fours(inverse[1, c][:, ts, :]), MULT)
+
+        def weave_pairs(pairs):
+            grouped = at("grouped1", POWER[1], [P, BANK, PACK], BF16, bufs=CHUNKS)
+            words = pairs.rearrange("p u m e -> p u (m e)").bitcast(I32)
+            nc.vector.tensor_copy(out=woven(grouped[:].bitcast(I32)), in_=by_fours(words))
+            return grouped
 
         def divide(engine, b, c, pieces):
             grouped = at(f"grouped{b}", POWER[b], [P, BANK, PACK], BF16, bufs=CHUNKS)
@@ -265,19 +282,30 @@ def tile_list_apparent_power_margins_kernel(
             z_s[b, c] = at(f"z_s{b}{c}", z_at[b] + 8 * KIB + c * BANK, [P, BANK], U8)
             quantise(z_w[b, c][:], z_s[b, c][:], grouped[:])
 
+        first_half = []
         for c in range(CHUNKS):
-            invert(0, c)
-            quantise_z(0, c, divide(nc.gpsimd, 0, c, halves))
-        for c in range(CHUNKS):
-            invert(1, c)
-        ahead = divide(nc.vector, 1, 0, whole)
-        for c in range(CHUNKS):
+            invert_chunk(0, c)
+            first_half.append(divide(nc.gpsimd, 0, c, halves))
+        for u in range(2):
+            invert(*(inverse[1, c][:, 2 * u : 2 * u + 2, :] for c in range(PAIRED)))
+        for c in range(PAIRED, CHUNKS):
+            invert_chunk(1, c)
+        pairs = [at(f"pairs{c}", ROOTS + (8 + 4 * c) * KIB, [P, 2, BANK, 2], BF16) for c in range(PAIRED)]
+        for c in range(PAIRED):
+            divide_pair(nc.gpsimd, pairs[c], c, 0)
+        for c in range(CHUNKS - 1):
+            quantise_z(0, c, first_half[c])
+        divide_pair(nc.vector, pairs[0], 0, 1)
+        quantise_z(0, CHUNKS - 1, first_half[-1])
+        grouped = weave_pairs(pairs[0][:])
+        divide_pair(nc.vector, pairs[1], 1, 1)
+        quantise_z(1, 0, grouped)
+        grouped = weave_pairs(pairs[1][:])
+        for c in range(PAIRED, CHUNKS):
+            ahead = divide(nc.vector, 1, c, whole)
+            quantise_z(1, c - 1, grouped)
             grouped = ahead
-            if c + 1 < CHUNKS and c > 0:
-                ahead = divide(nc.vector, 1, c + 1, whole)
-            quantise_z(1, c, grouped)
-            if c == 0:
-                ahead = divide(nc.vector, 1, 1, whole)
+        quantise_z(1, CHUNKS - 1, grouped)
 
         rotation = ("act", "rea", "sum", "sum")
         accs = {}

@@ -27,8 +27,6 @@ FIRST = 256
 SQUARES = 16
 BANKS = {"act": 2, "rea": 2, "sum": 4}
 
-RUNS = (4, 4)
-
 PAIRED = 2
 
 KIB = 1024
@@ -193,7 +191,7 @@ def tile_list_apparent_power_margins_kernel(
                     for n, sq in enumerate(squares):
                         nc.tensor.matmul(total[:, t, :], sq[:, t0 + t, :], ident[:], start=(n == 0), stop=(n == 1), is_transpose=True)
                 nc.scalar.activation(out=h[b][:, ts, js], in_=total[:], func=ACT.Sqrt, bias=under_root[:])
-                if u < 2:
+                if u < PACK:
                     weigh(b, ts, js)
 
         def place(b, planes, j0, j1):
@@ -203,34 +201,33 @@ def tile_list_apparent_power_margins_kernel(
         everything = [slice(0, T2)]
         units = 2 * S // P
         all_planes = range(PACK)
-        squares = {0: squared_powers(0, parts=PACK), 1: squared_powers(1)}
-        apparent_power(0, squares[0], parts=PACK)
-        place(0, all_planes, 0, P)
-        squares[2], squares[3] = squared_powers(2), squared_powers(3)
-        apparent_power(1, squares[1])
-        place(0, all_planes, P, 2 * P)
-        load_ratings(0)
-        for u in range(2, units, 2):
-            for ahead in range(u + 2, min(u + 4, units)):
-                squares[ahead] = squared_powers(ahead)
-            for done in (u, u + 1):
-                apparent_power(done, squares[done])
+        last = PACK - 1
+        squares = squared_powers(0, parts=PACK)
+        for u in range(units):
+            ahead = squared_powers(u + 1) if u + 1 < units else None
+            apparent_power(u, squares, parts=PACK if u == 0 else 1)
+            squares = ahead
             b, j0 = divmod(u * P, S)
-            for t0 in (0, 2):
-                weigh(b, slice(t0, t0 + 2), slice(j0, j0 + 2 * P))
-            if b == 0:
-                last = PACK - 1
-                for t in all_planes:
-                    if t < last or j0 < S // 2:
-                        scatter(0, t, j0, j0 + 2 * P)
-                    elif j0 > S // 2:
-                        scatter(0, t, S // 2, S)
-                    if j0 + 2 * P == S:
-                        join(0, t, everything if t < last else chunks)
-            elif j0 < S // 2:
-                place(1, (0, 1), j0, j0 + 2 * P)
-                if j0 > 0:
-                    scatter(1, 2, 0, S // 2)
+            if u < PACK:
+                place(0, all_planes, j0, j0 + P)
+                if u == 1:
+                    load_ratings(0)
+            elif u % 2 == 1:
+                j0, j1 = j0 - P, j0 + P
+                for t0 in (0, 2):
+                    weigh(b, slice(t0, t0 + 2), slice(j0, j1))
+                if b == 0:
+                    for t in all_planes:
+                        if t < last:
+                            scatter(0, t, j0, j1)
+                        elif j1 == S:
+                            scatter(0, t, S // 2, S)
+                        if j1 == S:
+                            join(0, t, everything if t < last else chunks)
+                elif j1 <= S // 2:
+                    place(1, (0, 1), j0, j1)
+                    if j1 == S // 2:
+                        scatter(1, 2, 0, S // 2)
         load_ratings(1)
         wm_w = at("wm_w", WEIGHTS, [P, 2, N], I32)
         wm_s = at("wm_s", WEIGHTS + 4 * KIB, [P, N], U8)
@@ -244,89 +241,96 @@ def tile_list_apparent_power_margins_kernel(
 
         roots = at("roots", ROOTS, [P, 2, T2 // 2], F32)
         halves = (slice(0, BANK // 2), slice(BANK // 2, BANK))
+        whole = slice(0, BANK)
 
-        def invert(*parts):
-            views = [roots[:, n].rearrange("p (t m) -> p t m", t=part.shape[1]) for n, part in enumerate(parts)]
-            for part, root in zip(parts, views):
-                nc.scalar.activation(out=root, in_=part, func=ACT.Abs_reciprocal_sqrt)
-            for part, root in zip(parts, views):
-                nc.scalar.activation(out=part, in_=root, func=ACT.Square)
+        def invert(b, *places):
+            parts = [inverse[b, c][:, 2 * u : 2 * u + 2, :].rearrange("p t m -> p (t m)") for c, u in places]
+            for n, part in enumerate(parts):
+                nc.scalar.activation(out=roots[:, n], in_=part, func=ACT.Abs_reciprocal_sqrt)
+            for n, part in enumerate(parts):
+                nc.scalar.activation(out=part, in_=roots[:, n], func=ACT.Square)
 
-        def invert_chunk(b, c):
-            invert(*(inverse[b, c][:, :, ms] for ms in halves))
-
-        def divide_pair(engine, pairs, c, u):
-            ts = slice(2 * u, 2 * u + 2)
-            engine.tensor_tensor(woven(pairs[:, u]), by_fours(joined[1][:, ts, chunks[c]]), by_fours(inverse[1, c][:, ts, :]), MULT)
-
-        def weave_pairs(pairs):
-            grouped = at("grouped1", POWER[1], [P, BANK, PACK], BF16, bufs=CHUNKS)
-            words = pairs.rearrange("p u m e -> p u (m e)").bitcast(I32)
-            nc.vector.tensor_copy(out=woven(grouped[:].bitcast(I32)), in_=by_fours(words))
-            return grouped
-
-        def divide(engine, b, c, pieces):
-            grouped = at(f"grouped{b}", POWER[b], [P, BANK, PACK], BF16, bufs=CHUNKS)
-            for ms in pieces:
-                placed_powers = joined[b][:, :, chunks[c]][:, :, ms]
-                run = RUNS[b]
-                engine.tensor_tensor(woven(grouped[:, ms, :], run), by_fours(placed_powers, run), by_fours(inverse[b, c][:, :, ms], run), MULT)
-            return grouped
-
-        whole = (slice(0, BANK),)
+        pairs, grouped, z_w, z_s = {}, {}, {}, {}
         z_at = (Z_FIRST, JOINED[0])
-        z_w, z_s = {}, {}
 
-        def quantise_z(b, c, grouped):
-            z_w[b, c] = at(f"z_w{b}{c}", z_at[b] + c * 2 * KIB, [P, BANK], U32)
-            z_s[b, c] = at(f"z_s{b}{c}", z_at[b] + 8 * KIB + c * BANK, [P, BANK], U8)
-            quantise(z_w[b, c][:], z_s[b, c][:], grouped[:])
+        def divide(engine, b, c, u, ms=whole):
+            if (b, c) not in pairs:
+                early = b == 1 and c < PAIRED
+                pairs[b, c] = (at(f"pairs_early{c}", ROOTS + (8 + 4 * c) * KIB, [P, 2, BANK, 2], BF16) if early
+                               else at("pairs", POWER[0], [P, 2, BANK, 2], BF16, bufs=CHUNKS))
+            ts = slice(2 * u, 2 * u + 2)
+            placed_powers = joined[b][:, ts, chunks[c]][:, :, ms]
+            engine.tensor_tensor(woven(pairs[b, c][:, u, ms]), by_fours(placed_powers), by_fours(inverse[b, c][:, ts, ms]), MULT)
 
-        first_half = []
+        def weave(b, c, ms=whole):
+            if (b, c) not in grouped:
+                grouped[b, c] = at("grouped", POWER[1], [P, BANK, PACK], BF16, bufs=CHUNKS)
+            words = pairs[b, c][:].rearrange("p u m e -> p u (m e)").bitcast(I32)
+            nc.vector.tensor_copy(out=woven(grouped[b, c][:].bitcast(I32)[:, ms]), in_=by_fours(words[:, :, ms]))
+
+        def quantise_z(b, c, ms=whole):
+            if (b, c) not in z_w:
+                z_w[b, c] = at(f"z_w{b}{c}", z_at[b] + c * 2 * KIB, [P, BANK], U32)
+                z_s[b, c] = at(f"z_s{b}{c}", z_at[b] + 8 * KIB + c * BANK, [P, BANK], U8)
+            quantise(z_w[b, c][:, ms], z_s[b, c][:, ms], grouped[b, c][:, ms, :])
+
         for c in range(CHUNKS):
-            invert_chunk(0, c)
-            first_half.append(divide(nc.gpsimd, 0, c, halves))
-        for u in range(2):
-            invert(*(inverse[1, c][:, 2 * u : 2 * u + 2, :] for c in range(PAIRED)))
-        for c in range(PAIRED, CHUNKS):
-            invert_chunk(1, c)
-        pairs = [at(f"pairs{c}", ROOTS + (8 + 4 * c) * KIB, [P, 2, BANK, 2], BF16) for c in range(PAIRED)]
+            invert(0, (c, 0), (c, 1))
+            for u in range(2):
+                divide(nc.gpsimd, 0, c, u)
+        invert(1, (0, 0), (1, 0))
         for c in range(PAIRED):
-            divide_pair(nc.gpsimd, pairs[c], c, 0)
-        for c in range(CHUNKS - 1):
-            quantise_z(0, c, first_half[c])
-        divide_pair(nc.vector, pairs[0], 0, 1)
-        quantise_z(0, CHUNKS - 1, first_half[-1])
-        grouped = weave_pairs(pairs[0][:])
-        divide_pair(nc.vector, pairs[1], 1, 1)
-        quantise_z(1, 0, grouped)
-        grouped = weave_pairs(pairs[1][:])
+            divide(nc.gpsimd, 1, c, 0)
+        invert(1, (0, 1), (1, 1))
         for c in range(PAIRED, CHUNKS):
-            ahead = divide(nc.vector, 1, c, whole)
-            quantise_z(1, c - 1, grouped)
-            grouped = ahead
-        quantise_z(1, CHUNKS - 1, grouped)
+            invert(1, (c, 0), (c, 1))
+
+        def both_pairs(c, ms=whole):
+            for u in range(0 if c >= PAIRED else 1, 2):
+                divide(nc.vector, 1, c, u, ms)
+
+        for step in (weave, quantise_z):
+            for c in range(2):
+                step(0, c)
+        for c in range(2):
+            both_pairs(c)
+            weave(0, c + 2)
+            weave(1, c)
+            quantise_z(0, c + 2)
+            quantise_z(1, c)
+        both_pairs(2)
+        both_pairs(3, halves[0])
+        weave(1, 2)
+        weave(1, 3, halves[0])
+        quantise_z(1, 2)
+        both_pairs(3, halves[1])
+        quantise_z(1, 3, halves[0])
+        weave(1, 3, halves[1])
+        quantise_z(1, 3, halves[1])
 
         rotation = ("act", "rea", "sum", "sum")
+        pieces = [(c, whole) for c in range(CHUNKS - 1)] + [(CHUNKS - 1, ms) for ms in halves]
         accs = {}
 
-        def margins(b, c):
+        def margins(b, n):
+            c, ms = pieces[n]
             if b == 0:
-                accs[c] = [bank(rotation[k], [P, BANK]) for k in range(N // P)]
-            for k, acc in enumerate(accs[c]):
+                accs[n] = [bank(rotation[k], [P, ms.stop - ms.start]) for k in range(N // P)]
+            for k, acc in enumerate(accs[n]):
                 ns = slice(k * P, (k + 1) * P)
                 nc.tensor.matmul_mx(out=acc[:], lhsT=wm_w[:, b, ns].bitcast(FP8X4), lhsT_scale=wm_s[4 * b : P, ns],
-                                    rhs=z_w[b, c][:].bitcast(FP8X4), rhs_scale=z_s[b, c][:],
+                                    rhs=z_w[b, c][:, ms].bitcast(FP8X4), rhs_scale=z_s[b, c][:, ms],
                                     start=(b == 0), stop=(b == 1))
 
         margins(0, 0)
         margins(0, 1)
-        for c in range(CHUNKS):
-            if c >= 2:
-                margins(0, c)
-            margins(1, c)
-            for k, acc in enumerate(accs[c]):
-                res = at(f"result{c // 2}", (ROOTS, rating_at(0, 0))[c // 2], [P, BANK], F32, bufs=8)
-                copy = nc.vector.tensor_copy if c == CHUNKS - 1 and k % 2 == 0 else nc.scalar.copy
+        for n, (c, ms) in enumerate(pieces):
+            if n >= 2:
+                margins(0, n)
+            margins(1, n)
+            for k, acc in enumerate(accs[n]):
+                width = ms.stop - ms.start
+                res = at("result", rating_at(0, 0), [P, width], F32, bufs=16) if c >= 2 else at("result0", ROOTS, [P, width], F32, bufs=8)
+                copy = nc.vector.tensor_copy if n == len(pieces) - 1 and k % 2 == 0 else nc.scalar.copy
                 copy(out=res[:], in_=acc[:])
-                nc.sync.dma_start(out=out[k * P : (k + 1) * P, chunks[c]], in_=res[:])
+                nc.sync.dma_start(out=out[k * P : (k + 1) * P, chunks[c]][:, ms], in_=res[:])

@@ -27,8 +27,6 @@ FIRST = 256
 SQUARES = 16
 BANKS = {"act": 2, "rea": 2, "sum": 4}
 
-PAIRED = 2
-
 KIB = 1024
 JOINED = (0, 32 * KIB)
 RATING = 64 * KIB
@@ -202,11 +200,14 @@ def tile_list_apparent_power_margins_kernel(
         units = 2 * S // P
         all_planes = range(PACK)
         last = PACK - 1
-        squares = squared_powers(0, parts=PACK)
         for u in range(units):
-            ahead = squared_powers(u + 1) if u + 1 < units else None
-            apparent_power(u, squares, parts=PACK if u == 0 else 1)
-            squares = ahead
+            if u == 0:
+                apparent_power(0, squared_powers(0, parts=PACK), parts=PACK)
+                squares = squared_powers(1)
+            else:
+                ahead = squared_powers(u + 1) if u + 1 < units else None
+                apparent_power(u, squares)
+                squares = ahead
             b, j0 = divmod(u * P, S)
             if u < PACK:
                 place(0, all_planes, j0, j0 + P)
@@ -255,18 +256,16 @@ def tile_list_apparent_power_margins_kernel(
 
         def divide(engine, b, c, u, ms=whole):
             if (b, c) not in pairs:
-                early = b == 1 and c < PAIRED
-                pairs[b, c] = (at(f"pairs_early{c}", ROOTS + (8 + 4 * c) * KIB, [P, 2, BANK, 2], BF16) if early
-                               else at("pairs", POWER[0], [P, 2, BANK, 2], BF16, bufs=CHUNKS))
+                pairs[b, c] = at(f"pairs{b}", (POWER[0], rating_at(0, 0))[b], [P, 2, BANK, 2], BF16, bufs=CHUNKS)
             ts = slice(2 * u, 2 * u + 2)
             placed_powers = joined[b][:, ts, chunks[c]][:, :, ms]
             engine.tensor_tensor(woven(pairs[b, c][:, u, ms]), by_fours(placed_powers), by_fours(inverse[b, c][:, ts, ms]), MULT)
 
-        def weave(b, c, ms=whole):
+        def weave(copy, b, c, ms=whole):
             if (b, c) not in grouped:
-                grouped[b, c] = at("grouped", POWER[1], [P, BANK, PACK], BF16, bufs=CHUNKS)
-            words = pairs[b, c][:].rearrange("p u m e -> p u (m e)").bitcast(I32)
-            nc.vector.tensor_copy(out=woven(grouped[b, c][:].bitcast(I32)[:, ms]), in_=by_fours(words[:, :, ms]))
+                grouped[b, c] = at(f"grouped{b}", (JOINED[0] + 16 * KIB, POWER[1])[b], [P, BANK, PACK], BF16, bufs=CHUNKS)
+            words = pairs[b, c][:].rearrange("p u m e -> p u (m e)").bitcast(U32)
+            copy(out=woven(grouped[b, c][:].bitcast(U32)[:, ms]), in_=by_fours(words[:, :, ms]))
 
         def quantise_z(b, c, ms=whole):
             if (b, c) not in z_w:
@@ -278,34 +277,35 @@ def tile_list_apparent_power_margins_kernel(
             invert(0, (c, 0), (c, 1))
             for u in range(2):
                 divide(nc.gpsimd, 0, c, u)
-        invert(1, (0, 0), (1, 0))
-        for c in range(PAIRED):
-            divide(nc.gpsimd, 1, c, 0)
-        invert(1, (0, 1), (1, 1))
-        for c in range(PAIRED, CHUNKS):
-            invert(1, (c, 0), (c, 1))
+        for c in (0, 2):
+            invert(1, (c, 0), (c + 1, 0))
+            for n in range(2):
+                divide(nc.gpsimd, 1, c + n, 0)
+        for c, woven_before in ((0, (0, 1)), (2, (3,))):
+            for early in woven_before:
+                weave(nc.scalar.copy, 0, early)
+            invert(1, (c, 1), (c + 1, 1))
 
-        def both_pairs(c, ms=whole):
-            for u in range(0 if c >= PAIRED else 1, 2):
-                divide(nc.vector, 1, c, u, ms)
-
-        for step in (weave, quantise_z):
-            for c in range(2):
-                step(0, c)
-        for c in range(2):
-            both_pairs(c)
-            weave(0, c + 2)
-            weave(1, c)
-            quantise_z(0, c + 2)
-            quantise_z(1, c)
-        both_pairs(2)
-        both_pairs(3, halves[0])
-        weave(1, 2)
-        weave(1, 3, halves[0])
+        on_vector = nc.vector.tensor_copy
+        quantise_z(0, 0)
+        quantise_z(0, 1)
+        weave(on_vector, 0, 2)
+        divide(nc.vector, 1, 0, 1)
+        quantise_z(0, 2)
+        weave(on_vector, 1, 0)
+        divide(nc.vector, 1, 1, 1)
+        quantise_z(1, 0)
+        weave(on_vector, 1, 1)
+        divide(nc.vector, 1, 2, 1)
+        quantise_z(1, 1)
+        weave(on_vector, 1, 2)
+        divide(nc.vector, 1, 3, 1, halves[0])
         quantise_z(1, 2)
-        both_pairs(3, halves[1])
+        weave(on_vector, 1, 3, halves[0])
+        divide(nc.vector, 1, 3, 1, halves[1])
+        quantise_z(0, 3)
+        weave(on_vector, 1, 3, halves[1])
         quantise_z(1, 3, halves[0])
-        weave(1, 3, halves[1])
         quantise_z(1, 3, halves[1])
 
         rotation = ("act", "rea", "sum", "sum")
@@ -330,7 +330,7 @@ def tile_list_apparent_power_margins_kernel(
             margins(1, n)
             for k, acc in enumerate(accs[n]):
                 width = ms.stop - ms.start
-                res = at("result", rating_at(0, 0), [P, width], F32, bufs=16) if c >= 2 else at("result0", ROOTS, [P, width], F32, bufs=8)
+                res = at("result", rating_at(0, 2), [P, width], F32, bufs=8) if c >= 2 else at("result0", ROOTS, [P, width], F32, bufs=8)
                 copy = nc.vector.tensor_copy if n == len(pieces) - 1 and k % 2 == 0 else nc.scalar.copy
                 copy(out=res[:], in_=acc[:])
                 nc.sync.dma_start(out=out[k * P : (k + 1) * P, chunks[c]][:, ms], in_=res[:])

@@ -23,7 +23,8 @@ PASS = P * PACK
 BANK = 512
 LIST_COL = 16
 CHUNKS = T2 // BANK
-FIRST = 256
+FIRST = 512
+FIRST_WEIGHTS = 256
 SQUARES = 16
 BANKS = {"act": 2, "rea": 2, "sum": 4}
 
@@ -34,7 +35,7 @@ POWER = (128 * KIB, 144 * KIB)
 PAGES = 160 * KIB
 ROOTS = 192 * KIB
 Z_FIRST = 208 * KIB
-V_REST = 222 * KIB
+V_REST = 220 * KIB
 WEIGHTS = 226 * KIB
 
 
@@ -75,7 +76,6 @@ def tile_list_apparent_power_margins_kernel(
         offs2_t = keep.tile([P, S // LIST_COL], U16, name="offs2_t")
         ident = keep.tile([P, P], F32, name="ident")
         wq_s = keep.tile([P, H], U8, name="wq_s", align_bytes=64)
-        v_w = keep.tile([P, S], U32, name="v_w", align_bytes=64)
         wp_w = [at(f"wp_w{b}", WEIGHTS + b * 2 * KIB, [P, PASS], U32) for b in range(2)]
         wp_s = [at(f"wp_s{b}", WEIGHTS + 4 * KIB + b * PASS, [P, PASS], U8) for b in range(2)]
         pages = [at(f"page{t}", PAGES + t * 8 * KIB, [P, T2], F32) for t in range(PACK)]
@@ -87,46 +87,48 @@ def tile_list_apparent_power_margins_kernel(
         def wp_columns(cs):
             return wp[:, cs].rearrange("(p t) c -> p t c", t=PACK)
 
-        def gather_scales(name, offset, j0, j1):
-            picked = at(name, offset, [P, j1 - j0], U8)
-            nc.vector.tensor_copy(out=picked[:], in_=tab_s[:].indirect(offs_t[:, j0 // LIST_COL : j1 // LIST_COL]))
+        def gather(name, offset, table, j0, j1):
+            picked = at(name, offset, [P, j1 - j0], table.dtype)
+            nc.vector.tensor_copy(out=picked[:], in_=table.indirect(offs_t[:, j0 // LIST_COL : j1 // LIST_COL]))
             return picked
 
         half = PASS // 2
         nc.gpsimd.memset(tab_s[:].bitcast(I32), 0)
-        nc.gpsimd.memset(wq_s[:].bitcast(I32), 0)
         nc.vector.memset(squared_const[:, 0:1], 1.0 / 64.0)
+        nc.vector.memset(wq_s[:].bitcast(I32), 0)
         nc.sync.dma_start(offs_t[:], offs)
         nc.sync.dma_start(offs2_t[:], offs2)
+        wq_w = [at(f"wq_w{b}", JOINED[1] + b * KIB, [P, 2 * PASS], U8) for b in range(2)]
+        wq_rows = wq_words[0].rearrange("p (b c) -> p b c", b=2)
+        nc.sync.dma_start(out=wq_w[0][:].bitcast(I32), in_=wq_rows[:, 0, :].bitcast(I32))
         nc.sync.dma_start(out=tab_w[:], in_=tab_words[0].rearrange("p n t -> p (n t)").bitcast(I32))
-        raw0 = [at(f"raw0{n}", rating_at(0, n), [P, PACK, half], F32) for n in range(2)]
-        for n in range(2):
-            nc.sync.dma_start(out=raw0[n][:], in_=wp_columns(slice(n * half, (n + 1) * half)))
+        raw0 = at("raw0", rating_at(0, 0), [P, PACK, PASS], F32)
+        nc.sync.dma_start(out=raw0[:], in_=wp_columns(slice(0, PASS)))
         load_scales([nc.scalar] * 4, tab_s, tab_scales[0])
         nc.scalar.activation(out=under_root[:], in_=squared_const[:, 0:1], func=ACT.Sqrt)
         load_scales([nc.gpsimd, nc.gpsimd, nc.sync, nc.sync], wq_s, wq_scales[0])
         make_identity(nc, ident[:])
-        wq_w = at("wq_w", JOINED[1], [P, 2 * H], U8)
         later = at("later", JOINED[1] + 2 * KIB, [P, PACK * PASS + S], F32)
         raw1 = later[:, 0 : PACK * PASS].rearrange("p (t c) -> p t c", t=PACK)
         wgs_t = later[:, PACK * PASS :]
-        nc.sync.dma_start(out=wq_w[:].bitcast(I32), in_=wq_words[0].bitcast(I32))
-        nc.sync.dma_start(out=wgs_t[:, 0:FIRST], in_=wgs[:, 0:FIRST])
         nc.sync.dma_start(out=raw1, in_=wp_columns(slice(PASS, H)))
-        nc.sync.dma_start(out=wgs_t[:, FIRST:S], in_=wgs[:, FIRST:S])
-        for page in pages[:1]:
+        nc.sync.dma_start(out=wgs_t[:, 0:FIRST_WEIGHTS], in_=wgs[:, 0:FIRST_WEIGHTS])
+        nc.sync.dma_start(out=wq_w[1][:].bitcast(I32), in_=wq_rows[:, 1, :].bitcast(I32))
+        nc.sync.dma_start(out=wgs_t[:, FIRST_WEIGHTS:S], in_=wgs[:, FIRST_WEIGHTS:S])
+        for page in pages[:3]:
             nc.vector.memset(page[:].bitcast(I32), 0)
-        for page in pages[1:]:
-            for ms in chunks:
-                nc.gpsimd.memset(page[:, ms].bitcast(I32), 0)
-        nc.vector.tensor_copy(out=v_w[:], in_=tab_w[:].bitcast(U32).indirect(offs_t[:]))
-        v_s = [gather_scales("v_s_first", ROOTS + KIB, 0, FIRST)]
-        for n in range(2):
-            grouped = at(f"grouped_wp0{n}", V_REST + n * 2 * KIB, [P, half, PACK], BF16)
-            nc.scalar.copy(out=woven(grouped[:]), in_=by_fours(raw0[n][:]))
-            cs = slice(n * half, (n + 1) * half)
+        for ms in chunks:
+            nc.gpsimd.memset(pages[3][:, ms].bitcast(I32), 0)
+        v_w = [gather("v_w_first", V_REST - 4 * KIB, tab_w[:].bitcast(U32), 0, FIRST)]
+        v_s = [gather("v_s_first", V_REST + 4 * KIB, tab_s[:], 0, FIRST)]
+        grouped_wp0 = [at(f"grouped_wp0{n}", V_REST + n * 2 * KIB, [P, half, PACK], BF16) for n in range(2)]
+        columns = [slice(n * half, (n + 1) * half) for n in range(2)]
+        for grouped, cs, copy in zip(grouped_wp0, columns, (nc.vector.tensor_copy, nc.scalar.copy)):
+            copy(out=woven(grouped[:]), in_=by_fours(raw0[:, :, cs]))
+        for grouped, cs in zip(grouped_wp0, columns):
             quantise(wp_w[0][:, cs], wp_s[0][:, cs], grouped[:])
-        v_s.append(gather_scales("v_s_rest", V_REST + 2 * KIB, FIRST, S))
+        v_w.append(gather("v_w_rest", V_REST + KIB, tab_w[:].bitcast(U32), FIRST, S))
+        v_s.append(gather("v_s_rest", V_REST + 3 * KIB, tab_s[:], FIRST, S))
         grouped_wp1 = at("grouped_wp1", rating_at(0, 3), [P, PASS, PACK], BF16)
         nc.vector.tensor_copy(out=woven(grouped_wp1[:]), in_=by_fours(raw1))
         quantise(wp_w[1][:], wp_s[1][:], grouped_wp1[:])
@@ -147,13 +149,13 @@ def tile_list_apparent_power_margins_kernel(
             b, j0 = divmod(u * P, S)
             piece = min(j0 // FIRST, 1)
             js = slice(j0 - piece * FIRST, j0 - piece * FIRST + P)
-            words, scales = v_w[:, j0 : j0 + P].bitcast(FP8X4), v_s[piece][:, js]
+            words, scales = v_w[piece][:, js].bitcast(FP8X4), v_s[piece][:, js]
             act = bank("act", [P, BANK])
             nc.tensor.matmul_mx(out=act[:], lhsT=words, lhsT_scale=scales,
                                 rhs=wp_w[b][:].bitcast(FP8X4), rhs_scale=wp_s[b][:], start=True, stop=True)
             rea = bank("rea", [P, BANK])
             nc.tensor.matmul_mx(out=rea[:], lhsT=words, lhsT_scale=scales,
-                                rhs=wq_w[:, 2 * b * PASS : 2 * (b + 1) * PASS].bitcast(FP4X4),
+                                rhs=wq_w[b][:].bitcast(FP4X4),
                                 rhs_scale=wq_s[:, b * PASS : (b + 1) * PASS], start=True, stop=True)
             squares = []
             for power in (rea, act):

@@ -191,17 +191,19 @@ def tile_list_apparent_power_margins_kernel(
                     for n, sq in enumerate(squares):
                         nc.tensor.matmul(total[:, t, :], sq[:, t0 + t, :], ident[:], start=(n == 0), stop=(n == 1), is_transpose=True)
                 nc.scalar.activation(out=h[b][:, ts, js], in_=total[:], func=ACT.Sqrt, bias=under_root[:])
-                if u < PACK:
+                if b == 0:
                     weigh(b, ts, js)
-
-        def place(b, planes, j0, j1):
-            for t in planes:
-                scatter(b, t, j0, j1)
 
         everything = [slice(0, T2)]
         units = 2 * S // P
-        all_planes = range(PACK)
+        half_units = units // 2
         last = PACK - 1
+        first_pieces, placed_to = [], [0] * PACK
+        while min(placed_to) < half_units:
+            t = len(first_pieces) % PACK
+            ready = min(half_units, 1 + max(sum(placed_to) - 1, 0) // 2)
+            first_pieces.append((t, placed_to[t], ready))
+            placed_to = [ready if n == t else done for n, done in enumerate(placed_to)]
         for u in range(units):
             if u == 0:
                 apparent_power(0, squared_powers(0, parts=PACK), parts=PACK)
@@ -211,26 +213,19 @@ def tile_list_apparent_power_margins_kernel(
                 apparent_power(u, squares)
                 squares = ahead
             b, j0 = divmod(u * P, S)
-            if u < PACK:
-                place(0, all_planes, j0, j0 + P)
-                if u == 1:
-                    load_ratings(0)
-            elif u % 2 == 1:
-                j0, j1 = j0 - P, j0 + P
+            if b == 1 and u % 2 == 1:
                 for t0 in (0, 2):
-                    weigh(b, slice(t0, t0 + 2), slice(j0, j1))
-                if b == 0:
-                    for t in all_planes:
-                        if t < last:
-                            scatter(0, t, j0, j1)
-                        elif j1 == S:
-                            scatter(0, t, S // 2, S)
-                        if j1 == S:
-                            join(0, t, everything if t < last else chunks)
-                elif j1 <= S // 2:
-                    place(1, (0, 1), j0, j1)
-                    if j1 == S // 2:
-                        scatter(1, 2, 0, S // 2)
+                    weigh(b, slice(t0, t0 + 2), slice(j0 - P, j0 + P))
+            if u == 1:
+                load_ratings(0)
+            for t, u0, u1 in first_pieces:
+                if u1 - 1 == u:
+                    scatter(0, t, u0 * P, u1 * P)
+                    if u1 == half_units:
+                        join(0, t, everything if t < last else chunks)
+            if u == half_units + PACK - 1:
+                for t in (0, 1):
+                    scatter(1, t, 0, S // 2)
         load_ratings(1)
         wm_w = at("wm_w", WEIGHTS, [P, 2, N], I32)
         wm_s = at("wm_s", WEIGHTS + 4 * KIB, [P, N], U8)
@@ -239,8 +234,8 @@ def tile_list_apparent_power_margins_kernel(
         for q in range(4):
             nc.sync.dma_start(out=wm_s[32 * q : 32 * q + 8, :].bitcast(I32), in_=wm_scales[:, 4 * q : 4 * q + 4, :].bitcast(I32))
         for t in range(PACK):
-            scatter(1, t, S // 2 if t < PACK - 1 else 0, S)
-            join(1, t, everything if t < PACK - 1 else chunks)
+            scatter(1, t, S // 2 if t < 2 else 0, S)
+            join(1, t, chunks if t % 2 == 1 else everything)
 
         roots = at("roots", ROOTS, [P, 2, T2 // 2], F32)
         halves = (slice(0, BANK // 2), slice(BANK // 2, BANK))
@@ -275,10 +270,11 @@ def tile_list_apparent_power_margins_kernel(
                 z_s[b, c] = at(f"z_s{b}{c}", z_at[b] + 8 * KIB + c * BANK, [P, BANK], U8)
             quantise(z_w[b, c][:, ms], z_s[b, c][:, ms], grouped[b, c][:, ms, :])
 
-        for c in range(CHUNKS):
-            invert(0, (c, 0), (c, 1))
-            for u in range(2):
-                divide(nc.gpsimd, 0, c, u)
+        for u in range(2):
+            for c in (0, 2):
+                invert(0, (c, u), (c + 1, u))
+                for n in range(2):
+                    divide(nc.gpsimd, 0, c + n, u)
         for c in (0, 2):
             invert(1, (c, 0), (c + 1, 0))
             for n in range(2):

@@ -191,7 +191,7 @@ def tile_list_apparent_power_margins_kernel(
                     for n, sq in enumerate(squares):
                         nc.tensor.matmul(total[:, t, :], sq[:, t0 + t, :], ident[:], start=(n == 0), stop=(n == 1), is_transpose=True)
                 nc.scalar.activation(out=h[b][:, ts, js], in_=total[:], func=ACT.Sqrt, bias=under_root[:])
-                if b == 0:
+                if b == 0 or u >= units - 2:
                     weigh(b, ts, js)
 
         everything = [slice(0, T2)]
@@ -213,7 +213,7 @@ def tile_list_apparent_power_margins_kernel(
                 apparent_power(u, squares)
                 squares = ahead
             b, j0 = divmod(u * P, S)
-            if b == 1 and u % 2 == 1:
+            if b == 1 and u % 2 == 1 and u < units - 2:
                 for t0 in (0, 2):
                     weigh(b, slice(t0, t0 + 2), slice(j0 - P, j0 + P))
             if u == 1:
@@ -241,12 +241,18 @@ def tile_list_apparent_power_margins_kernel(
         halves = (slice(0, BANK // 2), slice(BANK // 2, BANK))
         whole = slice(0, BANK)
 
-        def invert(b, *places):
-            parts = [inverse[b, c][:, 2 * u : 2 * u + 2, :].rearrange("p t m -> p (t m)") for c, u in places]
-            for n, part in enumerate(parts):
-                nc.scalar.activation(out=roots[:, n], in_=part, func=ACT.Abs_reciprocal_sqrt)
-            for n, part in enumerate(parts):
-                nc.scalar.activation(out=part, in_=roots[:, n], func=ACT.Square)
+        def invert(*parts):
+            views = [roots[:, n, 0 : part.shape[1] * part.shape[2]].rearrange("p (t m) -> p t m", t=part.shape[1]) for n, part in enumerate(parts)]
+            for part, view in zip(parts, views):
+                nc.scalar.activation(out=view, in_=part, func=ACT.Abs_reciprocal_sqrt)
+            for part, view in zip(parts, views):
+                nc.scalar.activation(out=part, in_=view, func=ACT.Square)
+
+        def invert_pair(b, c, u, ms=whole):
+            invert(*[inverse[b, c][:, t : t + 1, ms] for t in (2 * u, 2 * u + 1)])
+
+        def invert_two_pairs(b, c, u):
+            invert(*[inverse[b, n][:, 2 * u : 2 * u + 2, :] for n in (c, c + 1)])
 
         pairs, grouped, z_w, z_s = {}, {}, {}, {}
         z_at = (Z_FIRST, JOINED[0])
@@ -270,29 +276,33 @@ def tile_list_apparent_power_margins_kernel(
                 z_s[b, c] = at(f"z_s{b}{c}", z_at[b] + 8 * KIB + c * BANK, [P, BANK], U8)
             quantise(z_w[b, c][:, ms], z_s[b, c][:, ms], grouped[b, c][:, ms, :])
 
-        for u in range(2):
-            for c in (0, 2):
-                invert(0, (c, u), (c + 1, u))
-                for n in range(2):
-                    divide(nc.gpsimd, 0, c + n, u)
-        for c in (0, 2):
-            invert(1, (c, 0), (c + 1, 0))
+        for ms in halves:
+            invert_pair(0, 0, 0, ms)
+            divide(nc.gpsimd, 0, 0, 0, ms)
+        for u, c in [(0, 1), (0, 2), (0, 3), (1, 0), (1, 1)]:
+            invert_pair(0, c, u)
+            divide(nc.gpsimd, 0, c, u)
+        for b, u, c in [(0, 1, 2), (1, 0, 0), (1, 0, 2)]:
+            invert_two_pairs(b, c, u)
             for n in range(2):
-                divide(nc.gpsimd, 1, c + n, 0)
-        for c, woven_before in ((0, (0, 1)), (2, (3,))):
+                divide(nc.gpsimd, b, c + n, u)
+        for c, woven_before in ((0, (0, 1)), (2, (2,))):
             for early in woven_before:
                 weave(nc.scalar.copy, 0, early)
-            invert(1, (c, 1), (c + 1, 1))
+            invert_two_pairs(1, c, 1)
 
         on_vector = nc.vector.tensor_copy
         quantise_z(0, 0)
         quantise_z(0, 1)
-        weave(on_vector, 0, 2)
-        divide(nc.vector, 1, 0, 1)
-        quantise_z(0, 2)
-        weave(on_vector, 1, 0)
+        weave(on_vector, 0, 3)
+        for ms in halves:
+            divide(nc.vector, 1, 0, 1, ms)
+        for ms in halves:
+            weave(on_vector, 1, 0, ms)
+        for ms in halves:
+            quantise_z(1, 0, ms)
         divide(nc.vector, 1, 1, 1)
-        quantise_z(1, 0)
+        quantise_z(0, 2)
         weave(on_vector, 1, 1)
         divide(nc.vector, 1, 2, 1)
         quantise_z(1, 1)

@@ -23,9 +23,10 @@ PASS = P * PACK
 BANK = 512
 LIST_COL = 16
 CHUNKS = T2 // BANK
-FIRST = 512
+FIRST = 256
 FIRST_WEIGHTS = 256
 SQUARES = 16
+SINGLE_UNITS = 2
 BANKS = {"act": 2, "rea": 2, "sum": 4}
 
 KIB = 1024
@@ -80,8 +81,8 @@ def tile_list_apparent_power_margins_kernel(
         wp_s = [at(f"wp_s{b}", WEIGHTS + 4 * KIB + b * PASS, [P, PASS], U8) for b in range(2)]
         pages = [at(f"page{t}", PAGES + t * 8 * KIB, [P, T2], F32) for t in range(PACK)]
         tab_w = at("tab_w", ROOTS + KIB, [P, T], I32)
-        tab_s = at("tab_s", rating_at(0, 2), [P, T], U8)
-        squared_const = at("squared_const", JOINED[1] + 2 * KIB - 64, [P, 32], F32)
+        tab_s = at("tab_s", WEIGHTS, [P, T], U8)
+        squared_const = at("squared_const", JOINED[1] + KIB - 64, [P, 288], F32)
         under_root = at("under_root", ROOTS, [P, 1], F32)
 
         def wp_columns(cs):
@@ -94,19 +95,19 @@ def tile_list_apparent_power_margins_kernel(
 
         half = PASS // 2
         nc.gpsimd.memset(tab_s[:].bitcast(I32), 0)
+        nc.gpsimd.memset(wq_s[:].bitcast(I32), 0)
         nc.vector.memset(squared_const[:, 0:1], 1.0 / 64.0)
-        nc.vector.memset(wq_s[:].bitcast(I32), 0)
         nc.sync.dma_start(offs_t[:], offs)
         nc.sync.dma_start(offs2_t[:], offs2)
         wq_w = [at(f"wq_w{b}", JOINED[1] + b * KIB, [P, 2 * PASS], U8) for b in range(2)]
         wq_rows = wq_words[0].rearrange("p (b c) -> p b c", b=2)
-        nc.sync.dma_start(out=wq_w[0][:].bitcast(I32), in_=wq_rows[:, 0, :].bitcast(I32))
-        nc.sync.dma_start(out=tab_w[:], in_=tab_words[0].rearrange("p n t -> p (n t)").bitcast(I32))
         raw0 = at("raw0", rating_at(0, 0), [P, PACK, PASS], F32)
         nc.sync.dma_start(out=raw0[:], in_=wp_columns(slice(0, PASS)))
+        nc.sync.dma_start(out=tab_w[:], in_=tab_words[0].rearrange("p n t -> p (n t)").bitcast(I32))
         load_scales([nc.scalar] * 4, tab_s, tab_scales[0])
+        load_scales([nc.scalar, nc.gpsimd, nc.gpsimd, nc.gpsimd], wq_s, wq_scales[0])
         nc.scalar.activation(out=under_root[:], in_=squared_const[:, 0:1], func=ACT.Sqrt)
-        load_scales([nc.gpsimd, nc.gpsimd, nc.sync, nc.sync], wq_s, wq_scales[0])
+        nc.sync.dma_start(out=wq_w[0][:].bitcast(I32), in_=wq_rows[:, 0, :].bitcast(I32))
         make_identity(nc, ident[:])
         later = at("later", JOINED[1] + 2 * KIB, [P, PACK * PASS + S], F32)
         raw1 = later[:, 0 : PACK * PASS].rearrange("p (t c) -> p t c", t=PACK)
@@ -115,20 +116,21 @@ def tile_list_apparent_power_margins_kernel(
         nc.sync.dma_start(out=wgs_t[:, 0:FIRST_WEIGHTS], in_=wgs[:, 0:FIRST_WEIGHTS])
         nc.sync.dma_start(out=wq_w[1][:].bitcast(I32), in_=wq_rows[:, 1, :].bitcast(I32))
         nc.sync.dma_start(out=wgs_t[:, FIRST_WEIGHTS:S], in_=wgs[:, FIRST_WEIGHTS:S])
-        for page in pages[:3]:
-            nc.vector.memset(page[:].bitcast(I32), 0)
-        for ms in chunks:
-            nc.gpsimd.memset(pages[3][:, ms].bitcast(I32), 0)
-        v_w = [gather("v_w_first", V_REST - 4 * KIB, tab_w[:].bitcast(U32), 0, FIRST)]
-        v_s = [gather("v_s_first", V_REST + 4 * KIB, tab_s[:], 0, FIRST)]
+        for page in pages[:2]:
+            for ms in (slice(0, T2 // 2 - 1), slice(T2 // 2 - 1, T2)):
+                nc.vector.memset(page[:, ms].bitcast(I32), 0)
+        for page in pages[2:]:
+            for m0 in range(0, T2, BANK // 2):
+                nc.gpsimd.memset(page[:, m0 : m0 + BANK // 2].bitcast(I32), 0)
+        v_s = gather("v_s", V_REST + 4 * KIB, tab_s[:], 0, S)
         grouped_wp0 = [at(f"grouped_wp0{n}", V_REST + n * 2 * KIB, [P, half, PACK], BF16) for n in range(2)]
         columns = [slice(n * half, (n + 1) * half) for n in range(2)]
-        for grouped, cs, copy in zip(grouped_wp0, columns, (nc.vector.tensor_copy, nc.scalar.copy)):
-            copy(out=woven(grouped[:]), in_=by_fours(raw0[:, :, cs]))
         for grouped, cs in zip(grouped_wp0, columns):
-            quantise(wp_w[0][:, cs], wp_s[0][:, cs], grouped[:])
+            nc.scalar.copy(out=woven(grouped[:]), in_=by_fours(raw0[:, :, cs]))
+        quantise(wp_w[0][:, columns[0]], wp_s[0][:, columns[0]], grouped_wp0[0][:])
+        v_w = [gather("v_w_first", V_REST - 4 * KIB, tab_w[:].bitcast(U32), 0, FIRST)]
+        quantise(wp_w[0][:, columns[1]], wp_s[0][:, columns[1]], grouped_wp0[1][:])
         v_w.append(gather("v_w_rest", V_REST + KIB, tab_w[:].bitcast(U32), FIRST, S))
-        v_s.append(gather("v_s_rest", V_REST + 3 * KIB, tab_s[:], FIRST, S))
         grouped_wp1 = at("grouped_wp1", rating_at(0, 3), [P, PASS, PACK], BF16)
         nc.vector.tensor_copy(out=woven(grouped_wp1[:]), in_=by_fours(raw1))
         quantise(wp_w[1][:], wp_s[1][:], grouped_wp1[:])
@@ -149,7 +151,7 @@ def tile_list_apparent_power_margins_kernel(
             b, j0 = divmod(u * P, S)
             piece = min(j0 // FIRST, 1)
             js = slice(j0 - piece * FIRST, j0 - piece * FIRST + P)
-            words, scales = v_w[piece][:, js].bitcast(FP8X4), v_s[piece][:, js]
+            words, scales = v_w[piece][:, js].bitcast(FP8X4), v_s[:, j0 : j0 + P]
             act = bank("act", [P, BANK])
             nc.tensor.matmul_mx(out=act[:], lhsT=words, lhsT_scale=scales,
                                 rhs=wp_w[b][:].bitcast(FP8X4), rhs_scale=wp_s[b][:], start=True, stop=True)
@@ -191,19 +193,19 @@ def tile_list_apparent_power_margins_kernel(
                     for n, sq in enumerate(squares):
                         nc.tensor.matmul(total[:, t, :], sq[:, t0 + t, :], ident[:], start=(n == 0), stop=(n == 1), is_transpose=True)
                 nc.scalar.activation(out=h[b][:, ts, js], in_=total[:], func=ACT.Sqrt, bias=under_root[:])
-                if b == 0 or u >= units - 2:
+                if u == 1:
+                    for t in range(PACK):
+                        weigh(b, slice(t, t + 1), js)
+                elif b == 0 or u >= units - 2:
                     weigh(b, ts, js)
 
         everything = [slice(0, T2)]
         units = 2 * S // P
         half_units = units // 2
         last = PACK - 1
-        first_pieces, placed_to = [], [0] * PACK
-        while min(placed_to) < half_units:
-            t = len(first_pieces) % PACK
-            ready = min(half_units, 1 + max(sum(placed_to) - 1, 0) // 2)
-            first_pieces.append((t, placed_to[t], ready))
-            placed_to = [ready if n == t else done for n, done in enumerate(placed_to)]
+        first_pieces = [(t, u, u + 1) for u in range(SINGLE_UNITS) for t in range(PACK)]
+        first_pieces = first_pieces + [(t, SINGLE_UNITS, SINGLE_UNITS + 1 + t) for t in range(PACK)]
+        first_pieces = first_pieces + [(t, SINGLE_UNITS + 1 + t, half_units) for t in range(PACK)]
         for u in range(units):
             if u == 0:
                 apparent_power(0, squared_powers(0, parts=PACK), parts=PACK)
@@ -279,10 +281,10 @@ def tile_list_apparent_power_margins_kernel(
         for ms in halves:
             invert_pair(0, 0, 0, ms)
             divide(nc.gpsimd, 0, 0, 0, ms)
-        for u, c in [(0, 1), (0, 2), (0, 3), (1, 0), (1, 1)]:
+        for u, c in [(0, 1), (0, 2), (0, 3)]:
             invert_pair(0, c, u)
             divide(nc.gpsimd, 0, c, u)
-        for b, u, c in [(0, 1, 2), (1, 0, 0), (1, 0, 2)]:
+        for b, u, c in [(0, 1, 0), (0, 1, 2), (1, 0, 0), (1, 0, 2)]:
             invert_two_pairs(b, c, u)
             for n in range(2):
                 divide(nc.gpsimd, b, c + n, u)
@@ -295,14 +297,11 @@ def tile_list_apparent_power_margins_kernel(
         quantise_z(0, 0)
         quantise_z(0, 1)
         weave(on_vector, 0, 3)
-        for ms in halves:
-            divide(nc.vector, 1, 0, 1, ms)
-        for ms in halves:
-            weave(on_vector, 1, 0, ms)
-        for ms in halves:
-            quantise_z(1, 0, ms)
+        divide(nc.vector, 1, 0, 1)
         divide(nc.vector, 1, 1, 1)
+        weave(on_vector, 1, 0)
         quantise_z(0, 2)
+        quantise_z(1, 0)
         weave(on_vector, 1, 1)
         divide(nc.vector, 1, 2, 1)
         quantise_z(1, 1)

@@ -80,9 +80,9 @@ def tile_list_apparent_power_margins_kernel(
         wp_w = [at(f"wp_w{b}", WEIGHTS + b * 2 * KIB, [P, PASS], U32) for b in range(2)]
         wp_s = [at(f"wp_s{b}", WEIGHTS + 4 * KIB + b * PASS, [P, PASS], U8) for b in range(2)]
         pages = [at(f"page{t}", PAGES + t * 8 * KIB, [P, T2], F32) for t in range(PACK)]
-        tab_w = at("tab_w", ROOTS + KIB, [P, T], I32)
+        tab_w = at("tab_w", JOINED[1] - 8 * KIB, [P, T], I32)
         tab_s = at("tab_s", WEIGHTS, [P, T], U8)
-        squared_const = at("squared_const", JOINED[1] + KIB - 64, [P, 288], F32)
+        squared_const = at("squared_const", JOINED[1] - 64, [P, 544], F32)
         under_root = at("under_root", ROOTS, [P, 1], F32)
 
         def wp_columns(cs):
@@ -103,10 +103,10 @@ def tile_list_apparent_power_margins_kernel(
         wq_rows = wq_words[0].rearrange("p (b c) -> p b c", b=2)
         raw0 = at("raw0", rating_at(0, 0), [P, PACK, PASS], F32)
         nc.sync.dma_start(out=raw0[:], in_=wp_columns(slice(0, PASS)))
-        nc.sync.dma_start(out=tab_w[:], in_=tab_words[0].rearrange("p n t -> p (n t)").bitcast(I32))
-        load_scales([nc.scalar] * 4, tab_s, tab_scales[0])
-        load_scales([nc.scalar, nc.gpsimd, nc.gpsimd, nc.gpsimd], wq_s, wq_scales[0])
+        load_scales([nc.sync] * 4, tab_s, tab_scales[0])
+        load_scales([nc.sync, nc.sync, nc.gpsimd, nc.gpsimd], wq_s, wq_scales[0])
         nc.scalar.activation(out=under_root[:], in_=squared_const[:, 0:1], func=ACT.Sqrt)
+        nc.sync.dma_start(out=tab_w[:], in_=tab_words[0].rearrange("p n t -> p (n t)").bitcast(I32))
         nc.sync.dma_start(out=wq_w[0][:].bitcast(I32), in_=wq_rows[:, 0, :].bitcast(I32))
         make_identity(nc, ident[:])
         later = at("later", JOINED[1] + 2 * KIB, [P, PACK * PASS + S], F32)
@@ -243,18 +243,12 @@ def tile_list_apparent_power_margins_kernel(
         halves = (slice(0, BANK // 2), slice(BANK // 2, BANK))
         whole = slice(0, BANK)
 
-        def invert(*parts):
-            views = [roots[:, n, 0 : part.shape[1] * part.shape[2]].rearrange("p (t m) -> p t m", t=part.shape[1]) for n, part in enumerate(parts)]
-            for part, view in zip(parts, views):
-                nc.scalar.activation(out=view, in_=part, func=ACT.Abs_reciprocal_sqrt)
-            for part, view in zip(parts, views):
-                nc.scalar.activation(out=part, in_=view, func=ACT.Square)
-
-        def invert_pair(b, c, u, ms=whole):
-            invert(*[inverse[b, c][:, t : t + 1, ms] for t in (2 * u, 2 * u + 1)])
-
-        def invert_two_pairs(b, c, u):
-            invert(*[inverse[b, n][:, 2 * u : 2 * u + 2, :] for n in (c, c + 1)])
+        def invert(b, *places):
+            parts = [inverse[b, c][:, 2 * u : 2 * u + 2, :].rearrange("p t m -> p (t m)") for c, u in places]
+            for n, part in enumerate(parts):
+                nc.scalar.activation(out=roots[:, n], in_=part, func=ACT.Abs_reciprocal_sqrt)
+            for n, part in enumerate(parts):
+                nc.scalar.activation(out=part, in_=roots[:, n], func=ACT.Square)
 
         pairs, grouped, z_w, z_s = {}, {}, {}, {}
         z_at = (Z_FIRST, JOINED[0])
@@ -278,29 +272,28 @@ def tile_list_apparent_power_margins_kernel(
                 z_s[b, c] = at(f"z_s{b}{c}", z_at[b] + 8 * KIB + c * BANK, [P, BANK], U8)
             quantise(z_w[b, c][:, ms], z_s[b, c][:, ms], grouped[b, c][:, ms, :])
 
-        for ms in halves:
-            invert_pair(0, 0, 0, ms)
-            divide(nc.gpsimd, 0, 0, 0, ms)
-        for u, c in [(0, 1), (0, 2), (0, 3)]:
-            invert_pair(0, c, u)
-            divide(nc.gpsimd, 0, c, u)
-        for b, u, c in [(0, 1, 0), (0, 1, 2), (1, 0, 0), (1, 0, 2)]:
-            invert_two_pairs(b, c, u)
+        for u in range(2):
+            for c in (0, 2):
+                invert(0, (c, u), (c + 1, u))
+                for n in range(2):
+                    divide(nc.gpsimd, 0, c + n, u)
+        for c in (0, 2):
+            invert(1, (c, 0), (c + 1, 0))
             for n in range(2):
-                divide(nc.gpsimd, b, c + n, u)
-        for c, woven_before in ((0, (0, 1)), (2, (2,))):
+                divide(nc.gpsimd, 1, c + n, 0)
+        for c, woven_before in ((0, (0, 1)), (2, (3,))):
             for early in woven_before:
                 weave(nc.scalar.copy, 0, early)
-            invert_two_pairs(1, c, 1)
+            invert(1, (c, 1), (c + 1, 1))
 
         on_vector = nc.vector.tensor_copy
         quantise_z(0, 0)
         quantise_z(0, 1)
-        weave(on_vector, 0, 3)
+        weave(on_vector, 0, 2)
         divide(nc.vector, 1, 0, 1)
-        divide(nc.vector, 1, 1, 1)
-        weave(on_vector, 1, 0)
         quantise_z(0, 2)
+        weave(on_vector, 1, 0)
+        divide(nc.vector, 1, 1, 1)
         quantise_z(1, 0)
         weave(on_vector, 1, 1)
         divide(nc.vector, 1, 2, 1)

from contextlib import ExitStack

import concourse.mybir as mybir
from concourse.masks import make_identity

K, T, S, H, T2, N = 512, 2048, 1024, 1024, 2048, 512
FLOPS = 2 * (2 * K * H * S + H * N * T2)

F32 = mybir.dt.float32
BF16 = mybir.dt.bfloat16
I32 = mybir.dt.int32
U32 = mybir.dt.uint32
U16 = mybir.dt.uint16
U8 = mybir.dt.uint8
FP8X4 = mybir.dt.float8_e4m3fn_x4
FP4X4 = mybir.dt.float4_e2m1fn_x4
ACT = mybir.ActivationFunctionType
MULT = mybir.AluOpType.mult

P = 128
PACK = 4
PASS = P * PACK
BANK = 512
LIST_COL = 16
CHUNKS = T2 // BANK
FIRST = 256
FIRST_WEIGHTS = 256
SQUARES = 16
SINGLE_UNITS = 2
BANKS = {"act": 2, "rea": 2, "sum": 4}

KIB = 1024
JOINED = (0, 32 * KIB)
RATING = 64 * KIB
POWER = (128 * KIB, 144 * KIB)
PAGES = 160 * KIB
ROOTS = 192 * KIB
Z_FIRST = 208 * KIB
V_REST = 220 * KIB
WEIGHTS = 226 * KIB


def tile_list_apparent_power_margins_kernel(
    tc, tab_words, tab_scales, wp, wq_words, wq_scales, wm_words, wm_scales, offs, offs2, wgs, rating, out
):
    nc = tc.nc
    with ExitStack() as ctx:
        keep = ctx.enter_context(tc.tile_pool(name="keep", bufs=1))
        placed = ctx.enter_context(tc.tile_pool(name="placed", bufs=1))
        psum = ctx.enter_context(tc.psum_pool(name="psum", bufs=1))

        def at(name, offset, shape, dtype, bufs=1):
            return placed.tile(shape, dtype, name=name, tag=name, bufs=bufs, align_bytes=64, offset=offset)

        def bank(tag, shape):
            return psum.tile(shape, F32, name=tag, tag=tag, bufs=BANKS[tag])

        def load_scales(queues, dst, src_rows):
            for q, queue in enumerate(queues):
                queue.dma_start(out=dst[32 * q : 32 * q + 4, :].bitcast(I32), in_=src_rows[4 * q : 4 * q + 4, :].bitcast(I32))

        def woven(grouped, run=4):
            return grouped.rearrange("p (c i) t -> p c t i", i=run)

        def by_fours(planes, run=4):
            return planes.rearrange("p t (c i) -> p c t i", i=run)

        def quantise(words, scales, grouped):
            nc.vector.quantize_mx(out=words.bitcast(FP8X4), scales=scales, in_=grouped.rearrange("p c t -> p (c t)"))

        def rating_at(b, c):
            return RATING + (b * CHUNKS + c) * 8 * KIB

        chunks = [slice(m0, m0 + BANK) for m0 in range(0, T2, BANK)]

        offs_t = keep.tile([P, S // LIST_COL], U16, name="offs_t")
        offs2_t = keep.tile([P, S // LIST_COL], U16, name="offs2_t")
        ident = keep.tile([P, P], F32, name="ident")
        wq_s = keep.tile([P, H], U8, name="wq_s", align_bytes=64)
        wp_w = [at(f"wp_w{b}", WEIGHTS + b * 2 * KIB, [P, PASS], U32) for b in range(2)]
        wp_s = [at(f"wp_s{b}", WEIGHTS + 4 * KIB + b * PASS, [P, PASS], U8) for b in range(2)]
        pages = [at(f"page{t}", PAGES + t * 8 * KIB, [P, T2], F32) for t in range(PACK)]
        tab_w = at("tab_w", JOINED[1] - 8 * KIB, [P, T], I32)
        tab_s = at("tab_s", WEIGHTS, [P, T], U8)
        squared_const = at("squared_const", JOINED[1] - 64, [P, 544], F32)
        under_root = at("under_root", ROOTS, [P, 1], F32)

        def wp_columns(cs):
            return wp[:, cs].rearrange("(p t) c -> p t c", t=PACK)

        def gather(name, offset, table, j0, j1):
            picked = at(name, offset, [P, j1 - j0], table.dtype)
            nc.vector.tensor_copy(out=picked[:], in_=table.indirect(offs_t[:, j0 // LIST_COL : j1 // LIST_COL]))
            return picked

        half = PASS // 2
        nc.gpsimd.memset(tab_s[:].bitcast(I32), 0)
        nc.gpsimd.memset(wq_s[:].bitcast(I32), 0)
        nc.vector.memset(squared_const[:, 0:1], 1.0 / 64.0)
        nc.sync.dma_start(offs_t[:], offs)
        nc.sync.dma_start(offs2_t[:], offs2)
        wq_w = [at(f"wq_w{b}", JOINED[1] + b * KIB, [P, 2 * PASS], U8) for b in range(2)]
        wq_rows = wq_words[0].rearrange("p (b c) -> p b c", b=2)
        raw0 = at("raw0", rating_at(0, 0), [P, PACK, PASS], F32)
        nc.sync.dma_start(out=raw0[:], in_=wp_columns(slice(0, PASS)))
        load_scales([nc.sync] * 4, tab_s, tab_scales[0])
        load_scales([nc.sync, nc.sync, nc.gpsimd, nc.gpsimd], wq_s, wq_scales[0])
        nc.scalar.activation(out=under_root[:], in_=squared_const[:, 0:1], func=ACT.Sqrt)
        nc.sync.dma_start(out=tab_w[:], in_=tab_words[0].rearrange("p n t -> p (n t)").bitcast(I32))
        nc.sync.dma_start(out=wq_w[0][:].bitcast(I32), in_=wq_rows[:, 0, :].bitcast(I32))
        make_identity(nc, ident[:])
        later = at("later", JOINED[1] + 2 * KIB, [P, PACK * PASS + S], F32)
        raw1 = later[:, 0 : PACK * PASS].rearrange("p (t c) -> p t c", t=PACK)
        wgs_t = later[:, PACK * PASS :]
        nc.sync.dma_start(out=raw1, in_=wp_columns(slice(PASS, H)))
        nc.sync.dma_start(out=wgs_t[:, 0:FIRST_WEIGHTS], in_=wgs[:, 0:FIRST_WEIGHTS])
        nc.sync.dma_start(out=wq_w[1][:].bitcast(I32), in_=wq_rows[:, 1, :].bitcast(I32))
        nc.sync.dma_start(out=wgs_t[:, FIRST_WEIGHTS:S], in_=wgs[:, FIRST_WEIGHTS:S])
        for page in pages[:2]:
            for ms in (slice(0, T2 // 2 - 1), slice(T2 // 2 - 1, T2)):
                nc.vector.memset(page[:, ms].bitcast(I32), 0)
        for page in pages[2:]:
            for m0 in range(0, T2, BANK // 2):
                nc.gpsimd.memset(page[:, m0 : m0 + BANK // 2].bitcast(I32), 0)
        v_s = gather("v_s", V_REST + 4 * KIB, tab_s[:], 0, S)
        grouped_wp0 = [at(f"grouped_wp0{n}", V_REST + n * 2 * KIB, [P, half, PACK], BF16) for n in range(2)]
        columns = [slice(n * half, (n + 1) * half) for n in range(2)]
        for grouped, cs in zip(grouped_wp0, columns):
            nc.scalar.copy(out=woven(grouped[:]), in_=by_fours(raw0[:, :, cs]))
        quantise(wp_w[0][:, columns[0]], wp_s[0][:, columns[0]], grouped_wp0[0][:])
        v_w = [gather("v_w_first", V_REST - 4 * KIB, tab_w[:].bitcast(U32), 0, FIRST)]
        quantise(wp_w[0][:, columns[1]], wp_s[0][:, columns[1]], grouped_wp0[1][:])
        v_w.append(gather("v_w_rest", V_REST + KIB, tab_w[:].bitcast(U32), FIRST, S))
        grouped_wp1 = at("grouped_wp1", rating_at(0, 3), [P, PASS, PACK], BF16)
        nc.vector.tensor_copy(out=woven(grouped_wp1[:]), in_=by_fours(raw1))
        quantise(wp_w[1][:], wp_s[1][:], grouped_wp1[:])

        inverse = {}

        def load_ratings(b):
            tile = at(f"rating{b}", rating_at(b, 0), [P, CHUNKS, PACK, BANK], F32)
            for c, ms in enumerate(chunks):
                inverse[b, c] = tile[:, c]
                rows = rating[b * PASS : (b + 1) * PASS, ms]
                nc.sync.dma_start(out=inverse[b, c], in_=rows.rearrange("(p t) m -> p t m", t=PACK))

        h = [at(f"h{b}", POWER[b], [P, PACK, S], F32) for b in range(2)]
        joined = [at(f"joined{b}", JOINED[b], [P, PACK, T2], F32) for b in range(2)]

        def squared_powers(u, parts=1):
            b, j0 = divmod(u * P, S)
            piece = min(j0 // FIRST, 1)
            js = slice(j0 - piece * FIRST, j0 - piece * FIRST + P)
            words, scales = v_w[piece][:, js].bitcast(FP8X4), v_s[:, j0 : j0 + P]
            act = bank("act", [P, BANK])
            nc.tensor.matmul_mx(out=act[:], lhsT=words, lhsT_scale=scales,
                                rhs=wp_w[b][:].bitcast(FP8X4), rhs_scale=wp_s[b][:], start=True, stop=True)
            rea = bank("rea", [P, BANK])
            nc.tensor.matmul_mx(out=rea[:], lhsT=words, lhsT_scale=scales,
                                rhs=wq_w[b][:].bitcast(FP4X4),
                                rhs_scale=wq_s[:, b * PASS : (b + 1) * PASS], start=True, stop=True)
            squares = []
            for power in (rea, act):
                squares.append(at("square", rating_at(1, 0), [P, PACK, P], F32, bufs=SQUARES))
            planes = PACK // parts
            for t0 in range(0, PACK, planes):
                ts = slice(t0, t0 + planes)
                for power, sq in zip((rea, act), squares):
                    nc.scalar.activation(out=sq[:, ts, :], in_=power[:].rearrange("j (p t) -> j t p", t=PACK)[:, ts, :], func=ACT.Square)
            return squares

        def weigh(b, ts, js):
            planes = ts.stop - ts.start
            weights = wgs_t[:, js].unsqueeze(1).to_broadcast([P, planes, js.stop - js.start])
            nc.gpsimd.tensor_tensor(h[b][:, ts, js], h[b][:, ts, js], weights, MULT)

        def scatter(b, t, j0, j1):
            cols = offs2_t[:, j0 // LIST_COL : j1 // LIST_COL]
            nc.vector.tensor_copy(out=pages[t][:].indirect(cols), in_=h[b][:, t, j0:j1])

        def join(b, t, pieces):
            for ms in pieces:
                nc.sync.dma_start(out=joined[b][:, t, ms], in_=pages[t][:, ms])

        def apparent_power(u, squares, parts=1):
            b, j0 = divmod(u * P, S)
            js = slice(j0, j0 + P)
            planes = PACK // parts
            for t0 in range(0, PACK, planes):
                ts = slice(t0, t0 + planes)
                total = bank("sum", [P, planes, P])
                for t in range(planes):
                    for n, sq in enumerate(squares):
                        nc.tensor.matmul(total[:, t, :], sq[:, t0 + t, :], ident[:], start=(n == 0), stop=(n == 1), is_transpose=True)
                nc.scalar.activation(out=h[b][:, ts, js], in_=total[:], func=ACT.Sqrt, bias=under_root[:])
                if u == 1:
                    for t in range(PACK):
                        weigh(b, slice(t, t + 1), js)
                elif b == 0 or u >= units - 2:
                    weigh(b, ts, js)

        everything = [slice(0, T2)]
        units = 2 * S // P
        half_units = units // 2
        last = PACK - 1
        first_pieces = [(t, u, u + 1) for u in range(SINGLE_UNITS) for t in range(PACK)]
        first_pieces = first_pieces + [(t, SINGLE_UNITS, SINGLE_UNITS + 1 + t) for t in range(PACK)]
        first_pieces = first_pieces + [(t, SINGLE_UNITS + 1 + t, half_units) for t in range(PACK)]
        for u in range(units):
            if u == 0:
                apparent_power(0, squared_powers(0, parts=PACK), parts=PACK)
                squares = squared_powers(1)
            else:
                ahead = squared_powers(u + 1) if u + 1 < units else None
                apparent_power(u, squares)
                squares = ahead
            b, j0 = divmod(u * P, S)
            if b == 1 and u % 2 == 1 and u < units - 2:
                for t0 in (0, 2):
                    weigh(b, slice(t0, t0 + 2), slice(j0 - P, j0 + P))
            if u == 1:
                load_ratings(0)
            for t, u0, u1 in first_pieces:
                if u1 - 1 == u:
                    scatter(0, t, u0 * P, u1 * P)
                    if u1 == half_units:
                        join(0, t, everything if t < last else chunks)
            if u == half_units + PACK - 1:
                for t in (0, 1):
                    scatter(1, t, 0, S // 2)
        load_ratings(1)
        wm_w = at("wm_w", WEIGHTS, [P, 2, N], I32)
        wm_s = at("wm_s", WEIGHTS + 4 * KIB, [P, N], U8)
        nc.sync.dma_start(out=wm_w[:], in_=wm_words.rearrange("a p n t -> p a (n t)").bitcast(I32))
        nc.gpsimd.memset(wm_s[:].bitcast(I32), 0)
        for q in range(4):
            nc.sync.dma_start(out=wm_s[32 * q : 32 * q + 8, :].bitcast(I32), in_=wm_scales[:, 4 * q : 4 * q + 4, :].bitcast(I32))
        for t in range(PACK):
            scatter(1, t, S // 2 if t < 2 else 0, S)
            join(1, t, chunks if t % 2 == 1 else everything)

        roots = at("roots", ROOTS, [P, 2, T2 // 2], F32)
        halves = (slice(0, BANK // 2), slice(BANK // 2, BANK))
        whole = slice(0, BANK)

        def invert(b, *places):
            parts = [inverse[b, c][:, 2 * u : 2 * u + 2, :].rearrange("p t m -> p (t m)") for c, u in places]
            for n, part in enumerate(parts):
                nc.scalar.activation(out=roots[:, n], in_=part, func=ACT.Abs_reciprocal_sqrt)
            for n, part in enumerate(parts):
                nc.scalar.activation(out=part, in_=roots[:, n], func=ACT.Square)

        pairs, grouped, z_w, z_s = {}, {}, {}, {}
        z_at = (Z_FIRST, JOINED[0])

        def divide(engine, b, c, u, ms=whole):
            if (b, c) not in pairs:
                pairs[b, c] = at(f"pairs{b}", (POWER[0], rating_at(0, 0))[b], [P, 2, BANK, 2], BF16, bufs=CHUNKS)
            ts = slice(2 * u, 2 * u + 2)
            placed_powers = joined[b][:, ts, chunks[c]][:, :, ms]
            engine.tensor_tensor(woven(pairs[b, c][:, u, ms]), by_fours(placed_powers), by_fours(inverse[b, c][:, ts, ms]), MULT)

        def weave(copy, b, c, ms=whole):
            if (b, c) not in grouped:
                grouped[b, c] = at(f"grouped{b}", (JOINED[0] + 16 * KIB, POWER[1])[b], [P, BANK, PACK], BF16, bufs=CHUNKS)
            words = pairs[b, c][:].rearrange("p u m e -> p u (m e)").bitcast(U32)
            copy(out=woven(grouped[b, c][:].bitcast(U32)[:, ms]), in_=by_fours(words[:, :, ms]))

        def quantise_z(b, c, ms=whole):
            if (b, c) not in z_w:
                z_w[b, c] = at(f"z_w{b}{c}", z_at[b] + c * 2 * KIB, [P, BANK], U32)
                z_s[b, c] = at(f"z_s{b}{c}", z_at[b] + 8 * KIB + c * BANK, [P, BANK], U8)
            quantise(z_w[b, c][:, ms], z_s[b, c][:, ms], grouped[b, c][:, ms, :])

        for u in range(2):
            for c in (0, 2):
                invert(0, (c, u), (c + 1, u))
                for n in range(2):
                    divide(nc.gpsimd, 0, c + n, u)
        for c in (0, 2):
            invert(1, (c, 0), (c + 1, 0))
            for n in range(2):
                divide(nc.gpsimd, 1, c + n, 0)
        for c, woven_before in ((0, (0, 1)), (2, (3,))):
            for early in woven_before:
                weave(nc.scalar.copy, 0, early)
            invert(1, (c, 1), (c + 1, 1))

        on_vector = nc.vector.tensor_copy
        quantise_z(0, 0)
        quantise_z(0, 1)
        weave(on_vector, 0, 2)
        divide(nc.vector, 1, 0, 1)
        quantise_z(0, 2)
        weave(on_vector, 1, 0)
        divide(nc.vector, 1, 1, 1)
        quantise_z(1, 0)
        weave(on_vector, 1, 1)
        divide(nc.vector, 1, 2, 1)
        quantise_z(1, 1)
        weave(on_vector, 1, 2)
        divide(nc.vector, 1, 3, 1, halves[0])
        quantise_z(1, 2)
        weave(on_vector, 1, 3, halves[0])
        divide(nc.vector, 1, 3, 1, halves[1])
        quantise_z(0, 3)
        weave(on_vector, 1, 3, halves[1])
        quantise_z(1, 3, halves[0])
        quantise_z(1, 3, halves[1])

        rotation = ("act", "rea", "sum", "sum")
        pieces = [(c, whole) for c in range(CHUNKS - 1)] + [(CHUNKS - 1, ms) for ms in halves]
        accs = {}

        def margins(b, n):
            c, ms = pieces[n]
            if b == 0:
                accs[n] = [bank(rotation[k], [P, ms.stop - ms.start]) for k in range(N // P)]
            for k, acc in enumerate(accs[n]):
                ns = slice(k * P, (k + 1) * P)
                nc.tensor.matmul_mx(out=acc[:], lhsT=wm_w[:, b, ns].bitcast(FP8X4), lhsT_scale=wm_s[4 * b : P, ns],
                                    rhs=z_w[b, c][:, ms].bitcast(FP8X4), rhs_scale=z_s[b, c][:, ms],
                                    start=(b == 0), stop=(b == 1))

        margins(0, 0)
        margins(0, 1)
        for n, (c, ms) in enumerate(pieces):
            if n >= 2:
                margins(0, n)
            margins(1, n)
            for k, acc in enumerate(accs[n]):
                width = ms.stop - ms.start
                res = at("result", rating_at(0, 2), [P, width], F32, bufs=8) if c >= 2 else at("result0", ROOTS, [P, width], F32, bufs=8)
                copy = nc.vector.tensor_copy if n == len(pieces) - 1 and k % 2 == 0 else nc.scalar.copy
                copy(out=res[:], in_=acc[:])
                nc.sync.dma_start(out=out[k * P : (k + 1) * P, chunks[c]][:, ms], in_=res[:])
